import numpy as np
import ml_dtypes


def mxq(x, axis, fmt="e4m3"):
    dtype, down = {"e4m3": (ml_dtypes.float8_e4m3fn, 7), "e5m2": (ml_dtypes.float8_e5m2, 14)}[fmt]
    v = np.moveaxis(np.asarray(x, np.float32).astype(ml_dtypes.bfloat16).astype(np.float64), axis, -1)
    blocks = v.reshape(v.shape[:-1] + (-1, 32))
    amax = np.abs(blocks).max(-1, keepdims=True)
    byte = np.maximum(np.where(amax > 0, np.frexp(amax)[1] - 1 + 127, 0) - down, 1)
    scale = np.exp2(byte - 127.0)
    codes = (blocks / scale).astype(np.float32).astype(dtype).astype(np.float64)
    return np.moveaxis((codes * scale).reshape(v.shape), -1, axis)


WIDE = False


def mx_kscale(k):
    if not WIDE:
        return np.ones(k)
    levels = np.array([10, -10, 5, -5, 0])
    if k % 512:
        return np.exp2(np.random.permutation(np.resize(levels, k // 32))).repeat(32)
    a = np.empty((k // 512, 16))
    for p in range(k // 512):
        a[p, :8] = np.random.permutation(np.resize(levels, 8))
        for g in range(8):
            far = levels[np.abs(levels - a[p, g]) >= 10]
            a[p, g + 8] = far[np.random.randint(len(far))]
    return np.exp2(a.ravel()).repeat(32)


BF16 = ml_dtypes.bfloat16


def bf(x):
    return np.asarray(x, np.float32).astype(BF16)


def f64(x):
    return np.asarray(x).astype(np.float64)


E2M1 = np.array([0.0, 0.5, 1.0, 1.5, 2.0, 3.0, 4.0, 6.0, -0.0, -0.5, -1.0, -1.5, -2.0, -3.0, -4.0, -6.0])


def pack_weight(w, fmt):
    k, n = w.shape
    w = f64(bf(w)).reshape(k // 32, 32, n)
    amax = np.abs(w).max(1)
    if fmt == "e4m3":
        byte = np.frexp(amax)[1] - 1 + 127 - 7
    else:
        mant, ex = np.frexp(amax / 6.0)
        byte = np.where(mant > 0.5, ex, ex - 1) + 127
    byte = np.clip(np.where(amax > 0, byte, 1), 1, 254)
    scaled = (w * np.exp2(127.0 - byte)[:, None, :]).reshape(k, n).astype(np.float32)
    by_word = np.ascontiguousarray(scaled.reshape(k // 512, 128, 4, n).transpose(0, 1, 3, 2))
    if fmt == "e4m3":
        words = by_word.astype(ml_dtypes.float8_e4m3fn).view(np.uint8)
    else:
        c = by_word.astype(ml_dtypes.float4_e2m1fn).view(np.uint8) & 0xF
        words = c[..., 0::2] | (c[..., 1::2] << 4)
    return np.ascontiguousarray(words), np.ascontiguousarray(byte.astype(np.uint8).reshape(k // 512, 16, n))


def unpack_weight(words, scales, fmt):
    g, p, n, _ = words.shape
    if fmt == "e4m3":
        vals = np.ascontiguousarray(words).view(ml_dtypes.float8_e4m3fn).astype(np.float64)
    else:
        nib = np.empty((g, p, n, 4), np.uint8)
        nib[..., 0::2] = words & 0xF
        nib[..., 1::2] = words >> 4
        vals = E2M1[nib]
    vals = vals * np.repeat(np.exp2(scales.astype(np.float64) - 127.0), 8, axis=1)[..., None]
    return vals.transpose(0, 1, 3, 2).reshape(g * 512, n)
def pack4(w):
    words, scales = pack_weight(w, "e2m1")
    return words.reshape(words.shape[0], 128, -1), scales


def unpack4(words, scales):
    return unpack_weight(words.reshape(words.shape[0], 128, -1, 2), scales, "e2m1")


T, D, J, V = 512, 1536, 1024, 2048


def setup_inputs():
    s = mx_kscale(D)
    v = mx_kscale(V)
    t = mx_kscale(J)
    chosen = np.exp(2.0 * np.random.standard_normal((J, V)))
    rejected = np.exp(2.0 * np.random.standard_normal((J, V)))
    chosen = chosen / chosen.sum(axis=1, keepdims=True)
    rejected = rejected / rejected.sum(axis=1, keepdims=True)
    ut_words, ut_scales = pack4(np.random.standard_normal((V, D)) / v[:, None])
    return {"h": bf(np.random.standard_normal((T, D)) * s),
            "r": bf(2.0 * np.random.standard_normal((D, J)) / np.sqrt(D) / s[:, None]),
            "beta": bf((1.0 + 0.1 * np.random.standard_normal(J)) * t),
            "p_chosen": bf(chosen * v / t[:, None]),
            "p_rejected": bf(rejected * v / t[:, None]),
            "ut_words": ut_words, "ut_scales": ut_scales}


def reference(h, r, beta, p_chosen, p_rejected, ut_words, ut_scales):
    m = mxq(f64(h), 1, "e4m3") @ mxq(f64(r), 0, "e4m3")
    w = f64(beta) / (1.0 + np.exp(-m))
    diff = f64(p_chosen) - f64(p_rejected)
    b = mxq(diff, 1, "e4m3") @ unpack4(ut_words, ut_scales)
    return mxq(w, 1, "e4m3") @ mxq(b, 0, "e4m3")

@@ -1,0 +1,597 @@
+from contextlib import ExitStack
+
+import concourse.mybir as mybir
+from concourse.masks import make_identity
+
+T, D, J, V = 512, 1536, 1024, 2048
+P = 128
+FLOPS = 2 * (T * D * J + J * V * D + T * J * D)
+
+F32 = mybir.dt.float32
+BF16 = mybir.dt.bfloat16
+I32 = mybir.dt.int32
+U32 = mybir.dt.uint32
+U8 = mybir.dt.uint8
+FP8X4 = mybir.dt.float8_e4m3fn_x4
+FP4X4 = mybir.dt.float4_e2m1fn_x4
+ACT = mybir.ActivationFunctionType
+ALU = mybir.AluOpType
+
+NV = V // 512
+ND = D // 512
+NJ = J // 512
+NT = T // P
+TPB = 2
+
+
+def tile_dpo_like_hidden_step_s11_kernel(tc, h, r, beta, p_chosen, p_rejected, ut_words, ut_scales, out):
+    nc = tc.nc
+    with ExitStack() as ctx:
+        keep = ctx.enter_context(tc.tile_pool(name="keep", bufs=1))
+        work = ctx.enter_context(tc.tile_pool(name="work", bufs=2))
+        tp_pool = ctx.enter_context(tc.psum_pool(name="tp_pool", bufs=TPB))
+        acc_pool = ctx.enter_context(tc.psum_pool(name="acc_pool", bufs=8 - TPB))
+        ctx.enter_context(tc.manual_schedule())
+
+        ident = keep.tile([P, P], F32, name="ident")
+        warm = keep.tile([P, 1], F32, name="warm")
+        beta_bf = keep.tile([P, NJ, 4], BF16, name="beta_bf")
+        beta_f = keep.tile([P, NJ, 4], F32, name="beta_f")
+        usc = keep.tile([P, NV, D], U8, name="usc", align_bytes=64)
+        uta = keep.tile([P, 2, 2 * D], U8, name="uta", align_bytes=64)
+        utb = keep.tile([P, 2, 2 * D], U8, name="utb", align_bytes=64)
+        hraw = keep.tile([P, NT, D], BF16, name="hraw", align_bytes=64)
+        hre = keep.tile([P, NT, 2, D // 4, 2], BF16, name="hre", align_bytes=64)
+        hcodes, hscales, rcodes, rscales = [], [], [], []
+        for k in range(ND):
+            t1 = keep.tile([P, T], U32, name="hc%d" % k, align_bytes=64)
+            t2 = keep.tile([P, T], U8, name="hs%d" % k, align_bytes=64)
+            t3 = keep.tile([P, J], U32, name="rc%d" % k, align_bytes=64)
+            t4 = keep.tile([P, J], U8, name="rs%d" % k, align_bytes=64)
+            hcodes.append(t1)
+            hscales.append(t2)
+            rcodes.append(t3)
+            rscales.append(t4)
+        acodes, ascales, bcodes, bscales, sig = [], [], [], [], []
+        braw = keep.tile([P, 4, D], BF16, name="braw", align_bytes=64)
+        braw1 = keep.tile([P, 4, 1024], BF16, name="braw1", align_bytes=64)
+        for g in range(NJ):
+            t1 = keep.tile([P, T], U32, name="ac%d" % g, align_bytes=64)
+            t2 = keep.tile([P, T], U8, name="as%d" % g, align_bytes=64)
+            t3 = keep.tile([P, D], U32, name="bc%d" % g, align_bytes=64)
+            t4 = keep.tile([P, D], U8, name="bs%d" % g, align_bytes=64)
+            t6 = keep.tile([P, 4, T], F32, name="sig%d" % g, align_bytes=64)
+            acodes.append(t1)
+            ascales.append(t2)
+            bcodes.append(t3)
+            bscales.append(t4)
+            sig.append(t6)
+
+        pc, pr, rraw = {}, {}, {}
+
+        def load_p(q, half=None):
+            g, t = q // 4, q % 4
+            if q not in pc:
+                a = work.tile([P, V], BF16, name="pc", tag="pc", bufs=3, align_bytes=64)
+                b = work.tile([P, V], BF16, name="pr", tag="pr", bufs=3, align_bytes=64)
+                pc[q], pr[q] = a, b
+            cols = slice(0, V) if half is None else slice(half * V // 2, (half + 1) * V // 2)
+            rows = slice(g * 512, (g + 1) * 512)
+            src_a = p_chosen[rows, :].rearrange("(m t) v -> m t v", t=4)
+            src_b = p_rejected[rows, :].rearrange("(m t) v -> m t v", t=4)
+            nc.sync.dma_start(out=pc[q][:, cols], in_=src_a[:, t, cols])
+            nc.sync.dma_start(out=pr[q][:, cols], in_=src_b[:, t, cols])
+
+        def ut_cols(v, lo, w):
+            tile = uta if v < 2 else utb
+            return tile[:, v % 2, 2 * lo : 2 * (lo + w)].bitcast(FP4X4)
+
+        def load_r(k):
+            x = work.tile([P, 4, J], BF16, name="rraw", tag="rraw", bufs=2, align_bytes=64)
+            nc.sync.dma_start(out=x[:], in_=r[k * 512 : (k + 1) * 512, :].rearrange("(p j) c -> p j c", j=4))
+            rraw[k] = x
+
+        diff, ct, cc, cs = {}, {}, {}, {}
+
+        def sub(q, half=None):
+            if q not in diff:
+                x = work.tile([P, 2, V // 4, 2], BF16, name="diff", tag="diff", bufs=2, align_bytes=64)
+                diff[q] = x
+            lo, hi = (0, V) if half is None else (half * V // 2, (half + 1) * V // 2)
+            nc.vector.tensor_tensor(
+                out=diff[q][:, :, lo // 4 : hi // 4, :],
+                in0=pc[q][:, lo:hi].rearrange("p (w u e) -> p u w e", u=2, e=2),
+                in1=pr[q][:, lo:hi].rearrange("p (w u e) -> p u w e", u=2, e=2),
+                op=ALU.subtract,
+            )
+
+        bank = {}
+
+        def tr(q, b):
+            words = diff[q][:].rearrange("p u w e -> p (u w e)").bitcast(F32)
+            x = tp_pool.tile([P, 2, 2, P], F32, name="tp", tag="tp")
+            for a in range(2):
+                for u in range(2):
+                    lo = u * 512 + (2 * b + a) * P
+                    nc.tensor.transpose(x[:, a, u, :], words[:, lo : lo + P], ident[:])
+            bank[q, b] = x
+
+        def cp(q, b, eng):
+            if q not in ct:
+                x = work.tile([P, NV, P, 4], BF16, name="ct", tag="ct", bufs=2, align_bytes=64)
+                ct[q] = x
+            dst = ct[q][:, 2 * b : 2 * b + 2, :, :].rearrange("p a r j -> p (a r j)").bitcast(F32)
+            move(eng, dst.rearrange("p (a r u) -> p a r u", a=2, u=2), bank[q, b][:].rearrange("p a u r -> p a r u"))
+
+        def move(eng, dst, src):
+            if eng == "s":
+                nc.scalar.copy(out=dst, in_=src)
+            else:
+                nc.vector.tensor_copy(out=dst, in_=src)
+
+        def quant_c(q, half=None):
+            if q not in cc:
+                x = work.tile([P, NV * P], U32, name="cc", tag="cc", bufs=6, align_bytes=64)
+                y = work.tile([P, NV * P], U8, name="cs", tag="cs", bufs=6, align_bytes=64)
+                cc[q], cs[q] = x, y
+            flat = ct[q][:].rearrange("p a r j -> p (a r j)")
+            lo, hi = (0, 512) if half is None else (256 * half, 256 * half + 256)
+            nc.vector.quantize_mx(
+                out=cc[q][:, lo:hi].bitcast(FP8X4), scales=cs[q][:, lo:hi], in_=flat[:, 4 * lo : 4 * hi]
+            )
+
+        bacc = {}
+
+        def mm_b(q, n, half=None):
+            if (q, n) not in bacc:
+                x = acc_pool.tile([P, 512], F32, name="acc", tag="acc")
+                bacc[q, n] = x
+            for v in range(NV) if half is None else (2 * half, 2 * half + 1):
+                nc.tensor.matmul_mx(
+                    out=bacc[q, n][:],
+                    lhsT=cc[q][:, v * P : (v + 1) * P].bitcast(FP8X4),
+                    lhsT_scale=cs[q][:, v * P : (v + 1) * P],
+                    rhs=ut_cols(v, n * 512, 512),
+                    rhs_scale=usc[:, v, n * 512 : (n + 1) * 512],
+                    start=(v == 0),
+                    stop=(v == NV - 1),
+                )
+
+        def ev_b(q, n, eng):
+            dst = braw if q < 4 else braw1
+            move(eng, dst[:, q % 4, n * 512 : (n + 1) * 512], bacc[q, n][:])
+
+        def grp_tile():
+            x = work.tile([P, 512, 4], BF16, name="grp", tag="grp", bufs=6, align_bytes=64)
+            return x
+
+        gb = {}
+
+        def inter_b(g, n, eng):
+            x = grp_tile()
+            src = braw if g == 0 else braw1
+            move(eng, x[:], src[:, :, n * 512 : (n + 1) * 512].rearrange("p t n -> p n t"))
+            gb[g, n] = x
+
+        def quant_b(g, n):
+            cols = slice(n * 512, (n + 1) * 512)
+            nc.vector.quantize_mx(
+                out=bcodes[g][:, cols].bitcast(FP8X4), scales=bscales[g][:, cols],
+                in_=gb[g, n][:].rearrange("p c j -> p (c j)"),
+            )
+
+        def mm_u(u, ts):
+            if ("u", u) not in bacc:
+                x = acc_pool.tile([P, 4, P], F32, name="acc", tag="acc")
+                bacc["u", u] = x
+            for t in ts:
+                for v in range(NV):
+                    nc.tensor.matmul_mx(
+                        out=bacc["u", u][:, t, :],
+                        lhsT=cc[4 + t][:, v * P : (v + 1) * P].bitcast(FP8X4),
+                        lhsT_scale=cs[4 + t][:, v * P : (v + 1) * P],
+                        rhs=ut_cols(v, u * P, P),
+                        rhs_scale=usc[:, v, u * P : (u + 1) * P],
+                        start=(v == 0),
+                        stop=(v == NV - 1),
+                    )
+
+        def ev_u(u, eng):
+            if (1, u // 4) not in gb:
+                x = grp_tile()
+                gb[1, u // 4] = x
+            c = u % 4
+            move(eng, gb[1, u // 4][:, c * P : (c + 1) * P, :], bacc["u", u][:].rearrange("p t n -> p n t"))
+
+        def quant_u(u):
+            cols = slice(u * P, (u + 1) * P)
+            c = u % 4
+            nc.vector.quantize_mx(
+                out=bcodes[1][:, cols].bitcast(FP8X4), scales=bscales[1][:, cols],
+                in_=gb[1, u // 4][:, c * P : (c + 1) * P, :].rearrange("p c j -> p (c j)"),
+            )
+
+        gr = {}
+
+        def inter_r(k, g, eng):
+            x = grp_tile()
+            move(
+                eng,
+                x[:].rearrange("p (t m) j -> p t m j", t=4),
+                rraw[k][:, :, g * 512 : (g + 1) * 512].rearrange("p j (m t) -> p t m j", t=4),
+            )
+            gr[k, g] = x
+
+        def quant_r(k, g):
+            cols = slice(g * 512, (g + 1) * 512)
+            nc.vector.quantize_mx(
+                out=rcodes[k][:, cols].bitcast(FP8X4), scales=rscales[k][:, cols],
+                in_=gr[k, g][:].rearrange("p c j -> p (c j)"),
+            )
+
+        gh, hbank = {}, {}
+
+        def re_h(i, eng):
+            move(
+                eng,
+                hre[:, i, :, :, :],
+                hraw[:, i, :].rearrange("p (w u e) -> p u w e", u=2, e=2),
+            )
+
+        def tr_h(k, b):
+            x = tp_pool.tile([P, 2, 2, P], F32, name="tp", tag="tp")
+            for a in range(2):
+                words = hre[:, 2 * b + a, :, :, :].rearrange("p u w e -> p (u w e)").bitcast(F32)
+                for u in range(2):
+                    lo = u * (D // 4) + P * k
+                    nc.tensor.transpose(x[:, a, u, :], words[:, lo : lo + P], ident[:])
+            hbank[k, b] = x
+
+        def cp_h(k, b, eng):
+            if k not in gh:
+                x = grp_tile()
+                gh[k] = x
+            dst = gh[k][:, 256 * b : 256 * b + 256, :].rearrange("p c j -> p (c j)").bitcast(F32)
+            move(eng, dst.rearrange("p (a r u) -> p a r u", a=2, u=2), hbank[k, b][:].rearrange("p a u r -> p a r u"))
+
+        def quant_h(k):
+            nc.vector.quantize_mx(
+                out=hcodes[k][:].bitcast(FP8X4), scales=hscales[k][:], in_=gh[k][:].rearrange("p c j -> p (c j)")
+            )
+
+        macc = {}
+
+        def mm_m(g, t):
+            x = acc_pool.tile([P, 512], F32, name="acc", tag="acc")
+            cols = slice(g * 512 + t * P, g * 512 + (t + 1) * P)
+            for k in range(ND):
+                nc.tensor.matmul_mx(
+                    out=x[:],
+                    lhsT=rcodes[k][:, cols].bitcast(FP8X4),
+                    lhsT_scale=rscales[k][:, cols],
+                    rhs=hcodes[k][:].bitcast(FP8X4),
+                    rhs_scale=hscales[k][:],
+                    start=(k == 0),
+                    stop=(k == ND - 1),
+                )
+            macc[g, t] = x
+
+        def sig_m(g, t):
+            nc.scalar.activation(out=sig[g][:, t, :], in_=macc[g, t][:], func=ACT.Sigmoid)
+
+        ga = {}
+
+        def mul_a(g):
+            x = grp_tile()
+            nc.vector.tensor_tensor(
+                out=x[:],
+                in0=sig[g][:].rearrange("p t n -> p n t"),
+                in1=beta_f[:, g : g + 1, :].to_broadcast([P, T, 4]),
+                op=ALU.mult,
+            )
+            ga[g] = x
+
+        def quant_a(g):
+            nc.vector.quantize_mx(
+                out=acodes[g][:].bitcast(FP8X4), scales=ascales[g][:], in_=ga[g][:].rearrange("p c j -> p (c j)")
+            )
+
+        oacc = {}
+
+        def mm_o(i, c0, w, g, pool=None):
+            if g == 0:
+                if pool == "tp":
+                    x = tp_pool.tile([P, 512], F32, name="tp", tag="tp")
+                else:
+                    x = acc_pool.tile([P, 512], F32, name="acc", tag="acc")
+                oacc[i, c0] = x
+            rows, cols = slice(i * P, (i + 1) * P), slice(c0, c0 + w)
+            nc.tensor.matmul_mx(
+                out=oacc[i, c0][:, 0:w],
+                lhsT=acodes[g][:, rows].bitcast(FP8X4),
+                lhsT_scale=ascales[g][:, rows],
+                rhs=bcodes[g][:, cols].bitcast(FP8X4),
+                rhs_scale=bscales[g][:, cols],
+                start=(g == 0),
+                stop=(g == NJ - 1),
+            )
+
+        def ev_o(i, c0, w, eng):
+            if w == 512:
+                x = work.tile([P, 512], F32, name="osb", tag="osb", bufs=5, align_bytes=64)
+            else:
+                x = work.tile([P, 256], F32, name="osh", tag="osh", bufs=8, align_bytes=64)
+            move(eng, x[:, 0:w], oacc[i, c0][:, 0:w])
+            nc.sync.dma_start(out=out[i * P : (i + 1) * P, c0 : c0 + w], in_=x[:, 0:w])
+
+        def load_h():
+            nc.sync.dma_start(out=hraw[:], in_=h.rearrange("(i p) k -> p i k", p=P))
+
+        def load_beta():
+            nc.sync.dma_start(out=beta_bf[:], in_=beta.rearrange("(g p t) -> p g t", g=NJ, t=4))
+
+        def cast_beta():
+            nc.vector.tensor_copy(out=beta_f[:], in_=beta_bf[:])
+
+        def load_usc(lo, hi, eng):
+            for rr in range(4):
+                (nc.scalar if eng == "s" else nc.sync).dma_start(
+                    out=usc[rr:P:32, :, lo:hi].bitcast(I32),
+                    in_=ut_scales[:, rr:16:4, lo:hi].rearrange("g q n -> q g n").bitcast(I32),
+                )
+
+        def load_u(half):
+            dst = uta if half == 0 else utb
+            nc.sync.dma_start(
+                out=dst[:].bitcast(I32),
+                in_=ut_words[2 * half : 2 * half + 2, :, :].rearrange("g p c -> p g c").bitcast(I32),
+            )
+
+        def zero_usc():
+            nc.vector.memset(usc[:].bitcast(I32), 0)
+
+        def start():
+            nc.gpsimd.memset(warm[:], 0.0)
+            nc.scalar.activation(out=warm[:], in_=warm[:], func=ACT.Sigmoid)
+            make_identity(nc, ident[:])
+
+        start()
+        load_p(0, 1)
+        load_p(0, 0)
+        zero_usc()
+        sub(0, 1)
+        load_p(1, 0)
+        load_p(1, 1)
+        sub(1, 0)
+        tr(0, 1)
+        cp(0, 1, "v")
+        load_u(0)
+        tr(1, 0)
+        sub(1, 1)
+        cp(1, 0, "s")
+        load_usc(0, 1536, "y")
+        sub(0, 0)
+        quant_c(1, 0)
+        load_u(1)
+        tr(1, 1)
+        load_p(2)
+        load_p(3)
+        tr(0, 0)
+        load_r(0)
+        cp(1, 1, "v")
+        quant_c(0, 1)
+        cp(0, 0, "v")
+        mm_b(1, 2, 0)
+        mm_b(1, 1, 0)
+        mm_b(1, 0, 0)
+        quant_c(0, 0)
+        quant_c(1, 1)
+        mm_b(1, 1, 1)
+        mm_b(0, 1, 0)
+        mm_b(1, 0, 1)
+        ev_b(1, 1, "v")
+        sub(2)
+        load_p(4)
+        mm_b(0, 0, 0)
+        mm_b(0, 1, 1)
+        tr(2, 1)
+        load_h()
+        ev_b(1, 0, "s")
+        tr(2, 0)
+        cp(2, 1, "s")
+        sub(3)
+        cp(2, 0, "v")
+        quant_c(2)
+        mm_b(1, 2, 1)
+        mm_b(0, 0, 1)
+        tr(3, 1)
+        ev_b(1, 2, "s")
+        tr(3, 0)
+        load_r(1)
+        cp(3, 1, "s")
+        mm_b(0, 2, 0)
+        inter_r(0, 1, "v")
+        inter_r(0, 0, "s")
+        mm_b(2, 2)
+        cp(3, 0, "v")
+        mm_b(0, 2, 1)
+        sub(4)
+        quant_c(3)
+        quant_r(0, 1)
+        quant_r(0, 0)
+        mm_b(2, 1)
+        tr(4, 1)
+        tr(4, 0)
+        ev_b(0, 1, "s")
+        cp(4, 1, "v")
+        mm_b(3, 1)
+        load_r(2)
+        re_h(2, "v")
+        ev_b(0, 0, "s")
+        ev_b(2, 2, "s")
+        cp(4, 0, "v")
+        ev_b(0, 2, "s")
+        mm_b(3, 2)
+        re_h(3, "s")
+        ev_b(2, 1, "s")
+        tr_h(2, 1)
+        re_h(1, "v")
+        tr_h(1, 1)
+        mm_b(3, 0)
+        re_h(0, "v")
+        ev_b(3, 2, "s")
+        cp_h(2, 1, "s")
+        quant_c(4)
+        cp_h(1, 1, "s")
+        tr_h(2, 0)
+        ev_b(3, 1, "s")
+        cp_h(2, 0, "s")
+        tr_h(1, 0)
+        load_p(5)
+        mm_b(4, 1)
+        tr_h(0, 0)
+        inter_r(1, 1, "v")
+        mm_b(2, 0)
+        cp_h(1, 0, "v")
+        tr_h(0, 1)
+        mm_b(4, 0)
+        quant_r(1, 1)
+        inter_r(2, 1, "s")
+        quant_h(2)
+        quant_h(1)
+        load_p(6)
+        load_beta()
+        cp_h(0, 0, "s")
+        sub(5)
+        cp_h(0, 1, "s")
+        quant_r(2, 1)
+        tr(5, 0)
+        ev_b(3, 0, "s")
+        ev_b(4, 1, "s")
+        cp(5, 0, "s")
+        tr(5, 1)
+        ev_b(2, 0, "s")
+        quant_h(0)
+        sub(6)
+        mm_m(1, 3)
+        mm_m(1, 2)
+        mm_m(1, 1)
+        cp(5, 1, "s")
+        inter_r(1, 0, "s")
+        inter_r(2, 0, "v")
+        tr(6, 0)
+        tr(6, 1)
+        mm_m(1, 0)
+        ev_b(4, 0, "v")
+        quant_c(5)
+        quant_r(2, 0)
+        quant_r(1, 0)
+        sig_m(1, 1)
+        cp(6, 0, "s")
+        cp(6, 1, "s")
+        sig_m(1, 3)
+        load_p(7)
+        mm_b(5, 1)
+        mm_b(5, 0)
+        sub(7)
+        tr(7, 1)
+        sig_m(1, 2)
+        quant_c(6)
+        sig_m(1, 0)
+        cp(7, 1, "s")
+        ev_b(5, 0, "s")
+        cast_beta()
+        tr(7, 0)
+        mm_m(0, 1)
+        inter_b(0, 0, "v")
+        mm_m(0, 0)
+        ev_b(5, 1, "s")
+        cp(7, 0, "s")
+        mm_m(0, 2)
+        mm_m(0, 3)
+        sig_m(0, 1)
+        mul_a(1)
+        mm_b(6, 0)
+        sig_m(0, 2)
+        quant_c(7)
+        quant_b(0, 0)
+        mm_b(7, 0)
+        quant_a(1)
+        sig_m(0, 0)
+        sig_m(0, 3)
+        ev_b(6, 0, "s")
+        ev_b(7, 0, "s")
+        mul_a(0)
+        inter_b(1, 0, "v")
+        quant_a(0)
+        quant_b(1, 0)
+        mm_u(11, [0, 1, 2, 3])
+        mm_b(7, 1)
+        mm_u(10, [0, 1, 2, 3])
+        mm_b(6, 1)
+        inter_b(0, 2, "v")
+        inter_b(0, 1, "s")
+        mm_o(0, 0, 512, 0, "tp")
+        mm_o(2, 0, 512, 0)
+        ev_u(11, "s")
+        ev_b(7, 1, "s")
+        ev_u(10, "s")
+        mm_o(0, 0, 512, 1)
+        mm_o(3, 0, 512, 0)
+        mm_o(1, 0, 512, 0, "tp")
+        mm_o(1, 0, 512, 1)
+        ev_b(6, 1, "s")
+        quant_u(11)
+        ev_o(0, 0, 512, "s")
+        quant_b(0, 2)
+        mm_o(3, 0, 512, 1)
+        mm_u(8, [0, 1, 2, 3])
+        ev_o(1, 0, 512, "s")
+        quant_u(10)
+        mm_o(3, 1280, 256, 0)
+        inter_b(1, 1, "v")
+        mm_o(1, 1280, 256, 0, "tp")
+        mm_o(1, 1280, 256, 1)
+        mm_o(0, 1280, 256, 0, "tp")
+        ev_o(3, 0, 512, "s")
+        mm_o(3, 1280, 256, 1)
+        mm_o(2, 0, 512, 1)
+        quant_b(0, 1)
+        quant_b(1, 1)
+        ev_u(8, "s")
+        ev_o(1, 1280, 256, "s")
+        mm_o(2, 1280, 256, 0)
+        ev_o(3, 1280, 256, "s")
+        mm_o(2, 1280, 256, 1)
+        mm_o(0, 1280, 256, 1)
+        ev_o(0, 1280, 256, "v")
+        ev_o(2, 0, 512, "s")
+        mm_u(9, [0, 1, 2, 3])
+        quant_u(8)
+        mm_o(0, 512, 512, 0, "tp")
+        ev_o(2, 1280, 256, "s")
+        mm_o(0, 512, 512, 1)
+        ev_u(9, "v")
+        mm_o(2, 512, 512, 0)
+        ev_o(0, 512, 512, "s")
+        mm_o(2, 512, 512, 1)
+        quant_u(9)
+        mm_o(1, 512, 512, 0, "tp")
+        mm_o(1, 512, 512, 1)
+        ev_o(2, 512, 512, "v")
+        ev_o(1, 512, 512, "s")
+        mm_o(3, 512, 512, 0)
+        mm_o(3, 512, 512, 1)
+        ev_o(3, 512, 512, "v")
+        mm_o(0, 1024, 256, 0, "tp")
+        mm_o(2, 1024, 256, 0)
+        mm_o(3, 1024, 256, 0)
+        mm_o(3, 1024, 256, 1)
+        mm_o(0, 1024, 256, 1)
+        mm_o(2, 1024, 256, 1)
+        ev_o(3, 1024, 256, "v")
+        mm_o(1, 1024, 256, 0, "tp")
+        mm_o(1, 1024, 256, 1)
+        ev_o(1, 1024, 256, "v")
+        ev_o(2, 1024, 256, "s")
+        ev_o(0, 1024, 256, "s")

@@ -21,7 +21,17 @@ NV = V // 512
 ND = D // 512
 NJ = J // 512
 NT = T // P
-TPB = 2
+NS = D // P
+ACC_BANKS = 6
+TP_BANKS = 2
+P_BUFS = 4
+STAGE_BUFS = 6
+BST_BUFS = 5
+SIG_BUFS = 4
+OUT_BUFS = 8
+C_BUFS = 6
+R_BUFS = 2
+WIDE = (3,)
 
 
 def tile_dpo_like_hidden_step_s11_kernel(tc, h, r, beta, p_chosen, p_rejected, ut_words, ut_scales, out):
@@ -29,99 +39,37 @@ def tile_dpo_like_hidden_step_s11_kernel(tc, h, r, beta, p_chosen, p_rejected, u
     with ExitStack() as ctx:
         keep = ctx.enter_context(tc.tile_pool(name="keep", bufs=1))
         work = ctx.enter_context(tc.tile_pool(name="work", bufs=2))
-        tp_pool = ctx.enter_context(tc.psum_pool(name="tp_pool", bufs=TPB))
-        acc_pool = ctx.enter_context(tc.psum_pool(name="acc_pool", bufs=8 - TPB))
+        tp_pool = ctx.enter_context(tc.psum_pool(name="tp_pool", bufs=TP_BANKS))
+        acc_pool = ctx.enter_context(tc.psum_pool(name="acc_pool", bufs=ACC_BANKS))
         ctx.enter_context(tc.manual_schedule())
 
-        ident = keep.tile([P, P], F32, name="ident")
-        warm = keep.tile([P, 1], F32, name="warm")
-        beta_bf = keep.tile([P, NJ, 4], BF16, name="beta_bf")
-        beta_f = keep.tile([P, NJ, 4], F32, name="beta_f")
-        usc = keep.tile([P, NV, D], U8, name="usc", align_bytes=64)
-        uta = keep.tile([P, 2, 2 * D], U8, name="uta", align_bytes=64)
-        utb = keep.tile([P, 2, 2 * D], U8, name="utb", align_bytes=64)
-        hraw = keep.tile([P, NT, D], BF16, name="hraw", align_bytes=64)
-        hre = keep.tile([P, NT, 2, D // 4, 2], BF16, name="hre", align_bytes=64)
-        hcodes, hscales, rcodes, rscales = [], [], [], []
-        for k in range(ND):
-            t1 = keep.tile([P, T], U32, name="hc%d" % k, align_bytes=64)
-            t2 = keep.tile([P, T], U8, name="hs%d" % k, align_bytes=64)
-            t3 = keep.tile([P, J], U32, name="rc%d" % k, align_bytes=64)
-            t4 = keep.tile([P, J], U8, name="rs%d" % k, align_bytes=64)
-            hcodes.append(t1)
-            hscales.append(t2)
-            rcodes.append(t3)
-            rscales.append(t4)
-        acodes, ascales, bcodes, bscales, sig = [], [], [], [], []
-        braw = keep.tile([P, 4, D], BF16, name="braw", align_bytes=64)
-        braw1 = keep.tile([P, 4, 1024], BF16, name="braw1", align_bytes=64)
-        for g in range(NJ):
-            t1 = keep.tile([P, T], U32, name="ac%d" % g, align_bytes=64)
-            t2 = keep.tile([P, T], U8, name="as%d" % g, align_bytes=64)
-            t3 = keep.tile([P, D], U32, name="bc%d" % g, align_bytes=64)
-            t4 = keep.tile([P, D], U8, name="bs%d" % g, align_bytes=64)
-            t6 = keep.tile([P, 4, T], F32, name="sig%d" % g, align_bytes=64)
-            acodes.append(t1)
-            ascales.append(t2)
-            bcodes.append(t3)
-            bscales.append(t4)
-            sig.append(t6)
+        def kept(shape, dtype, name):
+            x = keep.tile(shape, dtype, name=name, align_bytes=64)
+            return x
 
-        pc, pr, rraw = {}, {}, {}
+        ident = kept([P, P], F32, "ident")
+        warm = kept([P, 1], F32, "warm")
+        beta_sb = kept([P, NJ, 4], BF16, "beta_sb")
+        usc = [kept([P, 2, D], U8, "usc%d" % a) for a in range(2)]
+        ut = [kept([P, 2 * D], U8, "ut%d" % v) for v in range(NV)]
+        braw = [kept([P, 4, 512 * WIDE[g]], BF16, "braw%d" % g) for g in range(len(WIDE))]
+        hraw = [kept([P, 2, D], BF16, "hraw%d" % b) for b in range(2)]
+        hre = [kept([P, 2, 2, D // 4, 2], BF16, "hre%d" % b) for b in range(2)]
+        hcodes = [kept([P, T], U32, "hc%d" % k) for k in range(ND)]
+        hscales = [kept([P, T], U8, "hs%d" % k) for k in range(ND)]
+        rcodes = [kept([P, J], U32, "rc%d" % k) for k in range(ND)]
+        rscales = [kept([P, J], U8, "rs%d" % k) for k in range(ND)]
+        acodes = [kept([P, T], U32, "ac%d" % g) for g in range(NJ)]
+        ascales = [kept([P, T], U8, "as%d" % g) for g in range(NJ)]
+        bcodes = [kept([P, D], U32, "bc%d" % g) for g in range(NJ)]
+        bscales = [kept([P, D], U8, "bs%d" % g) for g in range(NJ)]
 
-        def load_p(q, half=None):
-            g, t = q // 4, q % 4
-            if q not in pc:
-                a = work.tile([P, V], BF16, name="pc", tag="pc", bufs=3, align_bytes=64)
-                b = work.tile([P, V], BF16, name="pr", tag="pr", bufs=3, align_bytes=64)
-                pc[q], pr[q] = a, b
-            cols = slice(0, V) if half is None else slice(half * V // 2, (half + 1) * V // 2)
-            rows = slice(g * 512, (g + 1) * 512)
-            src_a = p_chosen[rows, :].rearrange("(m t) v -> m t v", t=4)
-            src_b = p_rejected[rows, :].rearrange("(m t) v -> m t v", t=4)
-            nc.sync.dma_start(out=pc[q][:, cols], in_=src_a[:, t, cols])
-            nc.sync.dma_start(out=pr[q][:, cols], in_=src_b[:, t, cols])
-
-        def ut_cols(v, lo, w):
-            tile = uta if v < 2 else utb
-            return tile[:, v % 2, 2 * lo : 2 * (lo + w)].bitcast(FP4X4)
-
-        def load_r(k):
-            x = work.tile([P, 4, J], BF16, name="rraw", tag="rraw", bufs=2, align_bytes=64)
-            nc.sync.dma_start(out=x[:], in_=r[k * 512 : (k + 1) * 512, :].rearrange("(p j) c -> p j c", j=4))
-            rraw[k] = x
-
-        diff, ct, cc, cs = {}, {}, {}, {}
-
-        def sub(q, half=None):
-            if q not in diff:
-                x = work.tile([P, 2, V // 4, 2], BF16, name="diff", tag="diff", bufs=2, align_bytes=64)
-                diff[q] = x
-            lo, hi = (0, V) if half is None else (half * V // 2, (half + 1) * V // 2)
-            nc.vector.tensor_tensor(
-                out=diff[q][:, :, lo // 4 : hi // 4, :],
-                in0=pc[q][:, lo:hi].rearrange("p (w u e) -> p u w e", u=2, e=2),
-                in1=pr[q][:, lo:hi].rearrange("p (w u e) -> p u w e", u=2, e=2),
-                op=ALU.subtract,
-            )
-
-        bank = {}
-
-        def tr(q, b):
-            words = diff[q][:].rearrange("p u w e -> p (u w e)").bitcast(F32)
-            x = tp_pool.tile([P, 2, 2, P], F32, name="tp", tag="tp")
-            for a in range(2):
-                for u in range(2):
-                    lo = u * 512 + (2 * b + a) * P
-                    nc.tensor.transpose(x[:, a, u, :], words[:, lo : lo + P], ident[:])
-            bank[q, b] = x
-
-        def cp(q, b, eng):
-            if q not in ct:
-                x = work.tile([P, NV, P, 4], BF16, name="ct", tag="ct", bufs=2, align_bytes=64)
-                ct[q] = x
-            dst = ct[q][:, 2 * b : 2 * b + 2, :, :].rearrange("p a r j -> p (a r j)").bitcast(F32)
-            move(eng, dst.rearrange("p (a r u) -> p a r u", a=2, u=2), bank[q, b][:].rearrange("p a u r -> p a r u"))
+        def bank(pool, shape):
+            if pool == "tp":
+                x = tp_pool.tile(shape, F32, name="tp", tag="tp")
+            else:
+                x = acc_pool.tile(shape, F32, name="acc", tag="acc")
+            return x
 
         def move(eng, dst, src):
             if eng == "s":
@@ -129,469 +77,490 @@ def tile_dpo_like_hidden_step_s11_kernel(tc, h, r, beta, p_chosen, p_rejected, u
             else:
                 nc.vector.tensor_copy(out=dst, in_=src)
 
-        def quant_c(q, half=None):
-            if q not in cc:
-                x = work.tile([P, NV * P], U32, name="cc", tag="cc", bufs=6, align_bytes=64)
-                y = work.tile([P, NV * P], U8, name="cs", tag="cs", bufs=6, align_bytes=64)
-                cc[q], cs[q] = x, y
-            flat = ct[q][:].rearrange("p a r j -> p (a r j)")
-            lo, hi = (0, 512) if half is None else (256 * half, 256 * half + 256)
-            nc.vector.quantize_mx(
-                out=cc[q][:, lo:hi].bitcast(FP8X4), scales=cs[q][:, lo:hi], in_=flat[:, 4 * lo : 4 * hi]
-            )
+        def quantize(codes, scales, lo, n, grouped):
+            nc.vector.quantize_mx(out=codes[:, lo : lo + n].bitcast(FP8X4), scales=scales[:, lo : lo + n], in_=grouped)
 
-        bacc = {}
-
-        def mm_b(q, n, half=None):
-            if (q, n) not in bacc:
-                x = acc_pool.tile([P, 512], F32, name="acc", tag="acc")
-                bacc[q, n] = x
-            for v in range(NV) if half is None else (2 * half, 2 * half + 1):
-                nc.tensor.matmul_mx(
-                    out=bacc[q, n][:],
-                    lhsT=cc[q][:, v * P : (v + 1) * P].bitcast(FP8X4),
-                    lhsT_scale=cs[q][:, v * P : (v + 1) * P],
-                    rhs=ut_cols(v, n * 512, 512),
-                    rhs_scale=usc[:, v, n * 512 : (n + 1) * 512],
-                    start=(v == 0),
-                    stop=(v == NV - 1),
-                )
-
-        def ev_b(q, n, eng):
-            dst = braw if q < 4 else braw1
-            move(eng, dst[:, q % 4, n * 512 : (n + 1) * 512], bacc[q, n][:])
-
-        def grp_tile():
-            x = work.tile([P, 512, 4], BF16, name="grp", tag="grp", bufs=6, align_bytes=64)
+        def stage():
+            x = work.tile([P, 512, 4], BF16, name="stage", tag="stage", bufs=STAGE_BUFS, align_bytes=64)
             return x
 
-        gb = {}
+        pc, pr = {}, {}
 
-        def inter_b(g, n, eng):
-            x = grp_tile()
-            src = braw if g == 0 else braw1
-            move(eng, x[:], src[:, :, n * 512 : (n + 1) * 512].rearrange("p t n -> p n t"))
-            gb[g, n] = x
+        def load_p(q, lo=0, hi=V):
+            g, t = divmod(q, 4)
+            if q not in pc:
+                a = work.tile([P, V], BF16, name="pc", tag="pc", bufs=P_BUFS, align_bytes=64)
+                b = work.tile([P, V], BF16, name="pr", tag="pr", bufs=P_BUFS, align_bytes=64)
+                pc[q], pr[q] = a, b
+            rows = slice(g * 512, (g + 1) * 512)
+            nc.sync.dma_start(out=pc[q][:, lo:hi], in_=p_chosen[rows, :].rearrange("(m t) v -> m t v", t=4)[:, t, lo:hi])
+            nc.sync.dma_start(out=pr[q][:, lo:hi], in_=p_rejected[rows, :].rearrange("(m t) v -> m t v", t=4)[:, t, lo:hi])
 
-        def quant_b(g, n):
-            cols = slice(n * 512, (n + 1) * 512)
-            nc.vector.quantize_mx(
-                out=bcodes[g][:, cols].bitcast(FP8X4), scales=bscales[g][:, cols],
-                in_=gb[g, n][:].rearrange("p c j -> p (c j)"),
+        def load_pair(v):
+            key = ("pair", v // 2)
+            if key not in pc:
+                a = work.tile([P, V], BF16, name="pc", tag="pc", bufs=P_BUFS, align_bytes=64)
+                b = work.tile([P, V], BF16, name="pr", tag="pr", bufs=P_BUFS, align_bytes=64)
+                pc[key], pr[key] = a, b
+            cols = slice(1024 * (v % 2), 1024 * (v % 2 + 1))
+            for dst, src in ((pc[key], p_chosen), (pr[key], p_rejected)):
+                nc.sync.dma_start(
+                    out=dst[:, cols].rearrange("p (t c) -> p t c", t=2),
+                    in_=src[0:512, :].rearrange("(m t) v -> m t v", t=4)[:, 0:2, 512 * v : 512 * (v + 1)],
+                )
+
+        def load_ut(v):
+            nc.sync.dma_start(out=ut[v][:].bitcast(I32), in_=ut_words[v].bitcast(I32))
+
+        def zero_usc(a):
+            nc.vector.memset(usc[a][:].bitcast(I32), 0)
+
+        def load_usc(a):
+            for rr in range(4):
+                src = ut_scales[2 * a : 2 * a + 2, rr:16:4, :]
+                nc.sync.dma_start(out=usc[a][rr:P:32, :, :].bitcast(I32), in_=src.rearrange("g q n -> q g n").bitcast(I32))
+
+        rraw = {}
+
+        def load_r(k):
+            x = work.tile([P, 4, J], BF16, name="rraw", tag="rraw", bufs=R_BUFS, align_bytes=64)
+            nc.sync.dma_start(out=x[:], in_=r[k * 512 : (k + 1) * 512, :].rearrange("(p j) c -> p j c", j=4))
+            rraw[k] = x
+
+        def load_h(b):
+            nc.sync.dma_start(out=hraw[b][:], in_=h[256 * b : 256 * (b + 1), :].rearrange("(i p) k -> p i k", p=P))
+
+        def load_beta():
+            nc.sync.dma_start(out=beta_sb[:], in_=beta.rearrange("(g p t) -> p g t", g=NJ, t=4))
+
+        diff, ct, cbank = {}, {}, {}
+
+        def sub(q, lo=0, hi=V):
+            if q not in diff:
+                x = work.tile([P, 2, V // 4, 2], BF16, name="diff", tag="diff", bufs=2, align_bytes=64)
+                diff[q] = x
+            nc.vector.tensor_tensor(
+                out=diff[q][:, :, lo // 4 : hi // 4, :],
+                in0=pc[q][:, lo:hi].rearrange("p (w u e) -> p u w e", u=2, e=2),
+                in1=pr[q][:, lo:hi].rearrange("p (w u e) -> p u w e", u=2, e=2),
+                op=ALU.subtract,
             )
 
-        def mm_u(u, ts):
-            if ("u", u) not in bacc:
-                x = acc_pool.tile([P, 4, P], F32, name="acc", tag="acc")
-                bacc["u", u] = x
-            for t in ts:
+        def tr_c(q, b, pool="tp"):
+            words = diff[q][:].rearrange("p u w e -> p (u w e)").bitcast(F32)
+            x = bank(pool, [P, 2, 2, P])
+            for a in range(2):
+                for u in range(2):
+                    lo = u * 512 + (2 * b + a) * P
+                    nc.tensor.transpose(x[:, a, u, :], words[:, lo : lo + P], ident[:])
+            cbank[q, b] = x
+
+        def out_words(eng, dst, src):
+            words = dst.rearrange("p c j -> p (c j)").bitcast(F32)
+            move(eng, words.rearrange("p (a r u) -> p a r u", a=2, u=2), src[:].rearrange("p a u r -> p a r u"))
+
+        def cp_c(q, b, eng):
+            if q not in ct:
+                ct[q] = stage()
+            out_words(eng, ct[q][:, 256 * b : 256 * (b + 1), :], cbank[q, b])
+
+        ccodes, cscales = {}, {}
+
+        def quant_c(q, lo=0, hi=512):
+            if q not in ccodes:
+                x = work.tile([P, NV * P], U32, name="cc", tag="cc", bufs=C_BUFS, align_bytes=64)
+                y = work.tile([P, NV * P], U8, name="cs", tag="cs", bufs=C_BUFS, align_bytes=64)
+                ccodes[q], cscales[q] = x, y
+            quantize(ccodes[q], cscales[q], lo, hi - lo, ct[q][:, lo:hi, :].rearrange("p c j -> p (c j)"))
+
+        bacc, bst = {}, {}
+
+        def pass_any(dst, q, v, lo, n):
+            key, at = (("pair", v // 2), 2 * (v % 2) + q) if q < 2 else (q, v)
+            nc.tensor.matmul_mx(
+                out=dst,
+                lhsT=ccodes[key][:, at * P : (at + 1) * P].bitcast(FP8X4),
+                lhsT_scale=cscales[key][:, at * P : (at + 1) * P],
+                rhs=ut[v][:, 2 * lo : 2 * (lo + n)].bitcast(FP4X4),
+                rhs_scale=usc[v // 2][:, v % 2, lo : lo + n],
+                start=(v == 0),
+                stop=(v == NV - 1),
+            )
+
+        def pass_b(g, s, t, v, pool="acc"):
+            if (g, s) not in bacc:
+                bacc[g, s] = bank(pool, [P, 4, P])
+            pass_any(bacc[g, s][:, t, :], 4 * g + t, v, s * P, P)
+
+        wacc, wst = {}, {}
+
+        def mm_w(q, c, vs=(0, 1, 2, 3), pool="acc"):
+            if (q, c) not in wacc:
+                wacc[q, c] = bank(pool, [P, 512])
+            for v in vs:
+                pass_any(wacc[q, c][:], q, v, 512 * c, 512)
+
+        def ev_w(q, c, eng):
+            move(eng, braw[q // 4][:, q % 4, 512 * c : 512 * (c + 1)], wacc[q, c][:])
+
+        def inter_b(g, c, eng, lo=0, hi=512):
+            if (g, c) not in wst:
+                wst[g, c] = stage()
+            move(eng, wst[g, c][:, lo:hi, :], braw[g][:, :, 512 * c + lo : 512 * c + hi].rearrange("p t n -> p n t"))
+
+        def inter_p(g, j, eng):
+            x = work.tile([P, 2 * P, 4], BF16, name="bst", tag="bst", bufs=BST_BUFS, align_bytes=64)
+            bst[g, j] = x
+            move(eng, x[:], braw[g][:, :, 256 * j : 256 * (j + 1)].rearrange("p t n -> p n t"))
+
+        def quant_w(g, c):
+            quantize(bcodes[g], bscales[g], 512 * c, 512, wst[g, c][:].rearrange("p c j -> p (c j)"))
+
+        def mm_tile(q, strips, vs=(0, 1, 2, 3)):
+            g, t = divmod(q, 4)
+            for s in strips:
+                for v in vs:
+                    pass_b(g, s, t, v)
+
+        def mm_strip(g, s, pool="acc"):
+            for t in range(4):
                 for v in range(NV):
-                    nc.tensor.matmul_mx(
-                        out=bacc["u", u][:, t, :],
-                        lhsT=cc[4 + t][:, v * P : (v + 1) * P].bitcast(FP8X4),
-                        lhsT_scale=cs[4 + t][:, v * P : (v + 1) * P],
-                        rhs=ut_cols(v, u * P, P),
-                        rhs_scale=usc[:, v, u * P : (u + 1) * P],
-                        start=(v == 0),
-                        stop=(v == NV - 1),
-                    )
+                    pass_b(g, s, t, v, pool)
 
-        def ev_u(u, eng):
-            if (1, u // 4) not in gb:
-                x = grp_tile()
-                gb[1, u // 4] = x
-            c = u % 4
-            move(eng, gb[1, u // 4][:, c * P : (c + 1) * P, :], bacc["u", u][:].rearrange("p t n -> p n t"))
+        def ev_b(g, s, eng):
+            if (g, s // 2) not in bst:
+                x = work.tile([P, 2 * P, 4], BF16, name="bst", tag="bst", bufs=BST_BUFS, align_bytes=64)
+                bst[g, s // 2] = x
+            c = s % 2
+            move(eng, bst[g, s // 2][:, c * P : (c + 1) * P, :], bacc[g, s][:].rearrange("p t n -> p n t"))
 
-        def quant_u(u):
-            cols = slice(u * P, (u + 1) * P)
-            c = u % 4
-            nc.vector.quantize_mx(
-                out=bcodes[1][:, cols].bitcast(FP8X4), scales=bscales[1][:, cols],
-                in_=gb[1, u // 4][:, c * P : (c + 1) * P, :].rearrange("p c j -> p (c j)"),
-            )
+        def quant_b(g, s, n):
+            c = s % 2
+            src = bst[g, s // 2][:, c * P : (c + n) * P, :].rearrange("p c j -> p (c j)")
+            quantize(bcodes[g], bscales[g], s * P, n * P, src)
 
-        gr = {}
+        rst, hst, hbank = {}, {}, {}
 
         def inter_r(k, g, eng):
-            x = grp_tile()
+            rst[k, g] = stage()
             move(
                 eng,
-                x[:].rearrange("p (t m) j -> p t m j", t=4),
+                rst[k, g][:].rearrange("p (t m) j -> p t m j", t=4),
                 rraw[k][:, :, g * 512 : (g + 1) * 512].rearrange("p j (m t) -> p t m j", t=4),
             )
-            gr[k, g] = x
 
         def quant_r(k, g):
-            cols = slice(g * 512, (g + 1) * 512)
-            nc.vector.quantize_mx(
-                out=rcodes[k][:, cols].bitcast(FP8X4), scales=rscales[k][:, cols],
-                in_=gr[k, g][:].rearrange("p c j -> p (c j)"),
-            )
+            quantize(rcodes[k], rscales[k], g * 512, 512, rst[k, g][:].rearrange("p c j -> p (c j)"))
 
-        gh, hbank = {}, {}
-
-        def re_h(i, eng):
+        def re_h(b, eng):
             move(
                 eng,
-                hre[:, i, :, :, :],
-                hraw[:, i, :].rearrange("p (w u e) -> p u w e", u=2, e=2),
+                hre[b][:],
+                hraw[b][:].rearrange("p i (w u e) -> p i u w e", u=2, e=2),
             )
 
-        def tr_h(k, b):
-            x = tp_pool.tile([P, 2, 2, P], F32, name="tp", tag="tp")
+        def tr_h(k, b, pool="acc"):
+            x = bank(pool, [P, 2, 2, P])
             for a in range(2):
-                words = hre[:, 2 * b + a, :, :, :].rearrange("p u w e -> p (u w e)").bitcast(F32)
+                words = hre[b][:, a, :, :, :].rearrange("p u w e -> p (u w e)").bitcast(F32)
                 for u in range(2):
                     lo = u * (D // 4) + P * k
                     nc.tensor.transpose(x[:, a, u, :], words[:, lo : lo + P], ident[:])
             hbank[k, b] = x
 
         def cp_h(k, b, eng):
-            if k not in gh:
-                x = grp_tile()
-                gh[k] = x
-            dst = gh[k][:, 256 * b : 256 * b + 256, :].rearrange("p c j -> p (c j)").bitcast(F32)
-            move(eng, dst.rearrange("p (a r u) -> p a r u", a=2, u=2), hbank[k, b][:].rearrange("p a u r -> p a r u"))
+            if k not in hst:
+                hst[k] = stage()
+            out_words(eng, hst[k][:, 256 * b : 256 * (b + 1), :], hbank[k, b])
 
-        def quant_h(k):
-            nc.vector.quantize_mx(
-                out=hcodes[k][:].bitcast(FP8X4), scales=hscales[k][:], in_=gh[k][:].rearrange("p c j -> p (c j)")
-            )
+        def quant_h(k, lo=0, hi=512):
+            quantize(hcodes[k], hscales[k], lo, hi - lo, hst[k][:, lo:hi, :].rearrange("p c j -> p (c j)"))
 
-        macc = {}
+        macc, sig, ast = {}, {}, {}
 
-        def mm_m(g, t):
-            x = acc_pool.tile([P, 512], F32, name="acc", tag="acc")
-            cols = slice(g * 512 + t * P, g * 512 + (t + 1) * P)
-            for k in range(ND):
-                nc.tensor.matmul_mx(
-                    out=x[:],
-                    lhsT=rcodes[k][:, cols].bitcast(FP8X4),
-                    lhsT_scale=rscales[k][:, cols],
-                    rhs=hcodes[k][:].bitcast(FP8X4),
-                    rhs_scale=hscales[k][:],
-                    start=(k == 0),
-                    stop=(k == ND - 1),
-                )
-            macc[g, t] = x
+        def mm_m(g, b, w, pool="acc"):
+            x = bank(pool, [P, 2, 256])
+            toks = slice(256 * b, 256 * (b + 1))
+            for e in range(2):
+                lo = g * 512 + (2 * w + e) * P
+                for k in range(ND):
+                    nc.tensor.matmul_mx(
+                        out=x[:, e, :],
+                        lhsT=rcodes[k][:, lo : lo + P].bitcast(FP8X4),
+                        lhsT_scale=rscales[k][:, lo : lo + P],
+                        rhs=hcodes[k][:, toks].bitcast(FP8X4),
+                        rhs_scale=hscales[k][:, toks],
+                        start=(k == 0),
+                        stop=(k == ND - 1),
+                    )
+            macc[g, b, w] = x
 
-        def sig_m(g, t):
-            nc.scalar.activation(out=sig[g][:, t, :], in_=macc[g, t][:], func=ACT.Sigmoid)
+        def sig_m(g, b, w):
+            if (g, b) not in sig:
+                x = work.tile([P, 2, 256, 2], F32, name="sig", tag="sig", bufs=SIG_BUFS, align_bytes=64)
+                sig[g, b] = x
+            nc.scalar.activation(out=sig[g, b][:, w, :, :], in_=macc[g, b, w][:].rearrange("p e n -> p n e"), func=ACT.Sigmoid)
 
-        ga = {}
-
-        def mul_a(g):
-            x = grp_tile()
+        def mul_a(g, b):
+            if g not in ast:
+                ast[g] = stage()
             nc.vector.tensor_tensor(
-                out=x[:],
-                in0=sig[g][:].rearrange("p t n -> p n t"),
-                in1=beta_f[:, g : g + 1, :].to_broadcast([P, T, 4]),
+                out=ast[g][:, 256 * b : 256 * (b + 1), :].rearrange("p n (w e) -> p n w e", w=2),
+                in0=sig[g, b][:].rearrange("p w n e -> p n w e"),
+                in1=beta_sb[:, g : g + 1, :].to_broadcast([P, 256, 4]).rearrange("p n (w e) -> p n w e", w=2),
                 op=ALU.mult,
             )
-            ga[g] = x
 
-        def quant_a(g):
-            nc.vector.quantize_mx(
-                out=acodes[g][:].bitcast(FP8X4), scales=ascales[g][:], in_=ga[g][:].rearrange("p c j -> p (c j)")
-            )
+        def quant_a(g, b):
+            src = ast[g][:, 256 * b : 256 * (b + 1), :].rearrange("p c j -> p (c j)")
+            quantize(acodes[g], ascales[g], 256 * b, 256, src)
 
         oacc = {}
 
-        def mm_o(i, c0, w, g, pool=None):
-            if g == 0:
-                if pool == "tp":
-                    x = tp_pool.tile([P, 512], F32, name="tp", tag="tp")
-                else:
-                    x = acc_pool.tile([P, 512], F32, name="acc", tag="acc")
-                oacc[i, c0] = x
+        def mm_o(i, c0, w, pool="acc"):
+            x = bank(pool, [P, 512])
             rows, cols = slice(i * P, (i + 1) * P), slice(c0, c0 + w)
-            nc.tensor.matmul_mx(
-                out=oacc[i, c0][:, 0:w],
-                lhsT=acodes[g][:, rows].bitcast(FP8X4),
-                lhsT_scale=ascales[g][:, rows],
-                rhs=bcodes[g][:, cols].bitcast(FP8X4),
-                rhs_scale=bscales[g][:, cols],
-                start=(g == 0),
-                stop=(g == NJ - 1),
-            )
+            for g in range(NJ):
+                nc.tensor.matmul_mx(
+                    out=x[:, 0:w],
+                    lhsT=acodes[g][:, rows].bitcast(FP8X4),
+                    lhsT_scale=ascales[g][:, rows],
+                    rhs=bcodes[g][:, cols].bitcast(FP8X4),
+                    rhs_scale=bscales[g][:, cols],
+                    start=(g == 0),
+                    stop=(g == NJ - 1),
+                )
+            oacc[i, c0] = x
 
         def ev_o(i, c0, w, eng):
-            if w == 512:
-                x = work.tile([P, 512], F32, name="osb", tag="osb", bufs=5, align_bytes=64)
-            else:
-                x = work.tile([P, 256], F32, name="osh", tag="osh", bufs=8, align_bytes=64)
+            x = work.tile([P, 512], F32, name="osb", tag="osb", bufs=OUT_BUFS, align_bytes=64)
             move(eng, x[:, 0:w], oacc[i, c0][:, 0:w])
             nc.sync.dma_start(out=out[i * P : (i + 1) * P, c0 : c0 + w], in_=x[:, 0:w])
 
-        def load_h():
-            nc.sync.dma_start(out=hraw[:], in_=h.rearrange("(i p) k -> p i k", p=P))
+        def mm_o2(i0, c0, pool="acc"):
+            x = bank(pool, [P, 2, 256])
+            cols = slice(c0, c0 + 256)
+            for a in range(2):
+                rows = slice((i0 + a) * P, (i0 + a + 1) * P)
+                for g in range(NJ):
+                    nc.tensor.matmul_mx(
+                        out=x[:, a, :],
+                        lhsT=acodes[g][:, rows].bitcast(FP8X4),
+                        lhsT_scale=ascales[g][:, rows],
+                        rhs=bcodes[g][:, cols].bitcast(FP8X4),
+                        rhs_scale=bscales[g][:, cols],
+                        start=(g == 0),
+                        stop=(g == NJ - 1),
+                    )
+            oacc[i0, c0] = x
 
-        def load_beta():
-            nc.sync.dma_start(out=beta_bf[:], in_=beta.rearrange("(g p t) -> p g t", g=NJ, t=4))
-
-        def cast_beta():
-            nc.vector.tensor_copy(out=beta_f[:], in_=beta_bf[:])
-
-        def load_usc(lo, hi, eng):
-            for rr in range(4):
-                (nc.scalar if eng == "s" else nc.sync).dma_start(
-                    out=usc[rr:P:32, :, lo:hi].bitcast(I32),
-                    in_=ut_scales[:, rr:16:4, lo:hi].rearrange("g q n -> q g n").bitcast(I32),
-                )
-
-        def load_u(half):
-            dst = uta if half == 0 else utb
-            nc.sync.dma_start(
-                out=dst[:].bitcast(I32),
-                in_=ut_words[2 * half : 2 * half + 2, :, :].rearrange("g p c -> p g c").bitcast(I32),
-            )
-
-        def zero_usc():
-            nc.vector.memset(usc[:].bitcast(I32), 0)
+        def ev_o2(i0, c0, eng):
+            x = work.tile([P, 2, 256], F32, name="osb", tag="osb", bufs=OUT_BUFS, align_bytes=64)
+            move(eng, x[:], oacc[i0, c0][:])
+            dst = out[i0 * P : (i0 + 2) * P, c0 : c0 + 256].rearrange("(a p) c -> p a c", a=2)
+            nc.sync.dma_start(out=dst, in_=x[:])
 
         def start():
             nc.gpsimd.memset(warm[:], 0.0)
             nc.scalar.activation(out=warm[:], in_=warm[:], func=ACT.Sigmoid)
             make_identity(nc, ident[:])
 
+
         start()
-        load_p(0, 1)
-        load_p(0, 0)
-        zero_usc()
-        sub(0, 1)
-        load_p(1, 0)
-        load_p(1, 1)
-        sub(1, 0)
-        tr(0, 1)
-        cp(0, 1, "v")
-        load_u(0)
-        tr(1, 0)
-        sub(1, 1)
-        cp(1, 0, "s")
-        load_usc(0, 1536, "y")
-        sub(0, 0)
-        quant_c(1, 0)
-        load_u(1)
-        tr(1, 1)
-        load_p(2)
+        zero_usc(0)
+        load_pair(0)
+        load_ut(0)
+        load_usc(0)
+        load_pair(1)
+        load_ut(1)
+        zero_usc(1)
+        load_pair(2)
+        load_usc(1)
+        load_ut(2)
+        load_pair(3)
+        load_ut(3)
+        load_p(2, 0, V // 2)
+        load_p(2, V // 2, V)
         load_p(3)
-        tr(0, 0)
-        load_r(0)
-        cp(1, 1, "v")
-        quant_c(0, 1)
-        cp(0, 0, "v")
-        mm_b(1, 2, 0)
-        mm_b(1, 1, 0)
-        mm_b(1, 0, 0)
-        quant_c(0, 0)
-        quant_c(1, 1)
-        mm_b(1, 1, 1)
-        mm_b(0, 1, 0)
-        mm_b(1, 0, 1)
-        ev_b(1, 1, "v")
-        sub(2)
+
+
+        def strip(g, s, eng="s"):
+            mm_strip(g, s)
+            ev_b(g, s, eng)
+
+
+        def turn(q, engs="ss"):
+            for b in range(2):
+                tr_c(q, b)
+            for b in range(2):
+                cp_c(q, b, engs[b])
+
+
+        def half(key, b):
+            sub(key, b * V // 2, (b + 1) * V // 2)
+            tr_c(key, b)
+            cp_c(key, b, "s")
+
+
+        def quant_half(key, b):
+            quant_c(key, 256 * b, 256 * (b + 1))
+
+
+        def mm_pair(v):
+            for q in range(2):
+                for c in range(ND):
+                    mm_w(q, c, (v,))
+
+
+        early = range(ACC_BANKS)
+        half(("pair", 0), 0)
+        for v in range(1, NV):
+            half(("pair", v // 2), v % 2)
+            quant_half(("pair", (v - 1) // 2), (v - 1) % 2)
+            mm_pair(v - 1)
         load_p(4)
-        mm_b(0, 0, 0)
-        mm_b(0, 1, 1)
-        tr(2, 1)
-        load_h()
-        ev_b(1, 0, "s")
-        tr(2, 0)
-        cp(2, 1, "s")
+        load_r(0)
+        load_p(5)
+        half(2, 0)
+        quant_half(("pair", 1), 1)
+        sub(2, V // 2, V)
+        mm_pair(3)
+        for c in range(ND):
+            ev_w(0, c, "svs"[c])
+        tr_c(2, 1)
+        quant_half(2, 0)
         sub(3)
-        cp(2, 0, "v")
-        quant_c(2)
-        mm_b(1, 2, 1)
-        mm_b(0, 0, 1)
-        tr(3, 1)
-        ev_b(1, 2, "s")
-        tr(3, 0)
+        cp_c(2, 1, "s")
+        for c in range(ND):
+            ev_w(1, c, "s")
+        load_p(6)
+        for c in range(ND):
+            mm_w(2, c, (0, 1))
+        quant_half(2, 1)
+        load_p(7)
+        load_h(0)
+        load_h(1)
         load_r(1)
-        cp(3, 1, "s")
-        mm_b(0, 2, 0)
-        inter_r(0, 1, "v")
-        inter_r(0, 0, "s")
-        mm_b(2, 2)
-        cp(3, 0, "v")
-        mm_b(0, 2, 1)
+        load_beta()
+        turn(3)
+        for c in range(ND):
+            mm_w(2, c, (2, 3))
+            ev_w(2, c, "s")
         sub(4)
         quant_c(3)
-        quant_r(0, 1)
-        quant_r(0, 0)
-        mm_b(2, 1)
-        tr(4, 1)
-        tr(4, 0)
-        ev_b(0, 1, "s")
-        cp(4, 1, "v")
-        mm_b(3, 1)
-        load_r(2)
-        re_h(2, "v")
-        ev_b(0, 0, "s")
-        ev_b(2, 2, "s")
-        cp(4, 0, "v")
-        ev_b(0, 2, "s")
-        mm_b(3, 2)
-        re_h(3, "s")
-        ev_b(2, 1, "s")
-        tr_h(2, 1)
-        re_h(1, "v")
-        tr_h(1, 1)
-        mm_b(3, 0)
-        re_h(0, "v")
-        ev_b(3, 2, "s")
-        cp_h(2, 1, "s")
+        turn(4)
+        for c in range(ND):
+            mm_w(3, c)
+            ev_w(3, c, "s")
+        inter_r(0, 0, "v")
         quant_c(4)
-        cp_h(1, 1, "s")
-        tr_h(2, 0)
-        ev_b(3, 1, "s")
-        cp_h(2, 0, "s")
-        tr_h(1, 0)
-        load_p(5)
-        mm_b(4, 1)
-        tr_h(0, 0)
-        inter_r(1, 1, "v")
-        mm_b(2, 0)
-        cp_h(1, 0, "v")
-        tr_h(0, 1)
-        mm_b(4, 0)
-        quant_r(1, 1)
-        inter_r(2, 1, "s")
-        quant_h(2)
-        quant_h(1)
-        load_p(6)
-        load_beta()
-        cp_h(0, 0, "s")
         sub(5)
-        cp_h(0, 1, "s")
-        quant_r(2, 1)
-        tr(5, 0)
-        ev_b(3, 0, "s")
-        ev_b(4, 1, "s")
-        cp(5, 0, "s")
-        tr(5, 1)
-        ev_b(2, 0, "s")
-        quant_h(0)
+        quant_r(0, 0)
+        turn(5)
+        mm_tile(4, early)
         sub(6)
-        mm_m(1, 3)
-        mm_m(1, 2)
-        mm_m(1, 1)
-        cp(5, 1, "s")
-        inter_r(1, 0, "s")
-        inter_r(2, 0, "v")
-        tr(6, 0)
-        tr(6, 1)
-        mm_m(1, 0)
-        ev_b(4, 0, "v")
         quant_c(5)
-        quant_r(2, 0)
-        quant_r(1, 0)
-        sig_m(1, 1)
-        cp(6, 0, "s")
-        cp(6, 1, "s")
-        sig_m(1, 3)
-        load_p(7)
-        mm_b(5, 1)
-        mm_b(5, 0)
+        inter_r(0, 1, "v")
+        load_r(2)
+        inter_p(0, 0, "s")
+        turn(6)
+        mm_tile(5, early)
         sub(7)
-        tr(7, 1)
-        sig_m(1, 2)
         quant_c(6)
-        sig_m(1, 0)
-        cp(7, 1, "s")
-        ev_b(5, 0, "s")
-        cast_beta()
-        tr(7, 0)
-        mm_m(0, 1)
-        inter_b(0, 0, "v")
-        mm_m(0, 0)
-        ev_b(5, 1, "s")
-        cp(7, 0, "s")
-        mm_m(0, 2)
-        mm_m(0, 3)
-        sig_m(0, 1)
-        mul_a(1)
-        mm_b(6, 0)
-        sig_m(0, 2)
+        quant_r(0, 1)
+        re_h(0, "v")
+        inter_p(0, 1, "s")
+        quant_b(0, 0, 2)
+        turn(7)
+        mm_tile(6, early)
+        re_h(1, "v")
         quant_c(7)
-        quant_b(0, 0)
-        mm_b(7, 0)
-        quant_a(1)
-        sig_m(0, 0)
-        sig_m(0, 3)
-        ev_b(6, 0, "s")
-        ev_b(7, 0, "s")
-        mul_a(0)
-        inter_b(1, 0, "v")
-        quant_a(0)
-        quant_b(1, 0)
-        mm_u(11, [0, 1, 2, 3])
-        mm_b(7, 1)
-        mm_u(10, [0, 1, 2, 3])
-        mm_b(6, 1)
-        inter_b(0, 2, "v")
-        inter_b(0, 1, "s")
-        mm_o(0, 0, 512, 0, "tp")
-        mm_o(2, 0, 512, 0)
-        ev_u(11, "s")
-        ev_b(7, 1, "s")
-        ev_u(10, "s")
-        mm_o(0, 0, 512, 1)
-        mm_o(3, 0, 512, 0)
-        mm_o(1, 0, 512, 0, "tp")
-        mm_o(1, 0, 512, 1)
-        ev_b(6, 1, "s")
-        quant_u(11)
-        ev_o(0, 0, 512, "s")
-        quant_b(0, 2)
-        mm_o(3, 0, 512, 1)
-        mm_u(8, [0, 1, 2, 3])
-        ev_o(1, 0, 512, "s")
-        quant_u(10)
-        mm_o(3, 1280, 256, 0)
-        inter_b(1, 1, "v")
-        mm_o(1, 1280, 256, 0, "tp")
-        mm_o(1, 1280, 256, 1)
-        mm_o(0, 1280, 256, 0, "tp")
-        ev_o(3, 0, 512, "s")
-        mm_o(3, 1280, 256, 1)
-        mm_o(2, 0, 512, 1)
-        quant_b(0, 1)
-        quant_b(1, 1)
-        ev_u(8, "s")
-        ev_o(1, 1280, 256, "s")
-        mm_o(2, 1280, 256, 0)
-        ev_o(3, 1280, 256, "s")
-        mm_o(2, 1280, 256, 1)
-        mm_o(0, 1280, 256, 1)
-        ev_o(0, 1280, 256, "v")
-        ev_o(2, 0, 512, "s")
-        mm_u(9, [0, 1, 2, 3])
-        quant_u(8)
-        mm_o(0, 512, 512, 0, "tp")
-        ev_o(2, 1280, 256, "s")
-        mm_o(0, 512, 512, 1)
-        ev_u(9, "v")
-        mm_o(2, 512, 512, 0)
-        ev_o(0, 512, 512, "s")
-        mm_o(2, 512, 512, 1)
-        quant_u(9)
-        mm_o(1, 512, 512, 0, "tp")
-        mm_o(1, 512, 512, 1)
-        ev_o(2, 512, 512, "v")
-        ev_o(1, 512, 512, "s")
-        mm_o(3, 512, 512, 0)
-        mm_o(3, 512, 512, 1)
-        ev_o(3, 512, 512, "v")
-        mm_o(0, 1024, 256, 0, "tp")
-        mm_o(2, 1024, 256, 0)
-        mm_o(3, 1024, 256, 0)
-        mm_o(3, 1024, 256, 1)
-        mm_o(0, 1024, 256, 1)
-        mm_o(2, 1024, 256, 1)
-        ev_o(3, 1024, 256, "v")
-        mm_o(1, 1024, 256, 0, "tp")
-        mm_o(1, 1024, 256, 1)
-        ev_o(1, 1024, 256, "v")
-        ev_o(2, 1024, 256, "s")
-        ev_o(0, 1024, 256, "s")
+        quant_b(0, 2, 2)
+        inter_p(0, 2, "s")
+        for k in range(2):
+            tr_h(k, 0, "tp")
+        for k in range(2):
+            cp_h(k, 0, "s")
+        inter_r(1, 0, "v")
+        quant_b(0, 4, 2)
+        mm_tile(7, early)
+        ev_b(1, 0, "s")
+        ev_b(1, 1, "s")
+        tr_h(2, 0, "tp")
+        tr_h(0, 1, "tp")
+        tr_h(1, 1, "acc")
+        tr_h(2, 1, "acc")
+        ev_b(1, 2, "s")
+        ev_b(1, 3, "s")
+        inter_r(2, 0, "v")
+        quant_r(1, 0)
+        quant_r(2, 0)
+        cp_h(2, 0, "s")
+        cp_h(0, 1, "s")
+        cp_h(1, 1, "s")
+        ev_b(1, 4, "s")
+        cp_h(2, 1, "s")
+        ev_b(1, 5, "s")
+        strip(1, 6)
+        for k in range(ND):
+            quant_h(k)
+        inter_r(1, 1, "v")
+        strip(1, 7)
+        quant_b(1, 0, 2)
+        quant_r(1, 1)
+        inter_r(2, 1, "v")
+        strip(1, 8)
+        inter_p(0, 3, "s")
+        quant_b(1, 2, 2)
+        quant_r(2, 1)
+
+
+        def margins(g):
+            for b in range(2):
+                for w in range(2):
+                    mm_m(g, b, w)
+                    sig_m(g, b, w)
+
+
+        margins(0)
+        mul_a(0, 0)
+        quant_b(0, 6, 2)
+        quant_b(1, 4, 2)
+        quant_a(0, 0)
+        mul_a(0, 1)
+        inter_p(0, 4, "s")
+        strip(1, 9)
+        quant_b(1, 6, 2)
+        quant_a(0, 1)
+        margins(1)
+        mul_a(1, 0)
+        quant_b(0, 8, 2)
+        quant_a(1, 0)
+        strip(1, 10)
+        mul_a(1, 1)
+        quant_b(1, 8, 2)
+        quant_a(1, 1)
+        inter_p(0, 5, "v")
+        quant_b(1, 10, 1)
+        quant_b(0, 10, 2)
+
+
+        def result(i, c0, w, eng):
+            mm_o(i, c0, w)
+            ev_o(i, c0, w, eng)
+
+
+        for c in range(2):
+            for i in range(2):
+                result(i, 512 * c, 512, "s")
+        for i0 in (0, 2):
+            mm_o2(i0, 1024)
+            ev_o2(i0, 1024, "vs"[i0 // 2])
+        result(2, 0, 512, "v")
+        strip(1, 11)
+        quant_b(1, 11, 1)
+        result(3, 0, 512, "s")
+        result(2, 512, 512, "v")
+        result(3, 512, 512, "s")
+        for i in range(NT):
+            result(i, 1280, 256, "vs"[i % 2])

@@ -211,7 +211,8 @@ def tile_dpo_like_hidden_step_s11_kernel(tc, h, r, beta, p_chosen, p_rejected, u
         def inter_p(g, j, eng):
             x = work.tile([P, 2 * P, 4], BF16, name="bst", tag="bst", bufs=BST_BUFS, align_bytes=64)
             bst[g, j] = x
-            move(eng, x[:], braw[g][:, :, 256 * j : 256 * (j + 1)].rearrange("p t n -> p n t"))
+            src = braw[g][:, :, 256 * j : 256 * (j + 1)]
+            move(eng, x[:].rearrange("p (c i) t -> p c t i", i=4), src.rearrange("p t (c i) -> p c t i", i=4))
 
         def quant_w(g, c):
             quantize(bcodes[g], bscales[g], 512 * c, 512, wst[g, c][:].rearrange("p c j -> p (c j)"))
@@ -245,8 +246,8 @@ def tile_dpo_like_hidden_step_s11_kernel(tc, h, r, beta, p_chosen, p_rejected, u
             rst[k, g] = stage()
             move(
                 eng,
-                rst[k, g][:].rearrange("p (t m) j -> p t m j", t=4),
-                rraw[k][:, :, g * 512 : (g + 1) * 512].rearrange("p j (m t) -> p t m j", t=4),
+                rst[k, g][:].rearrange("p (t a b) j -> p a t b j", t=4, b=2),
+                rraw[k][:, :, g * 512 : (g + 1) * 512].rearrange("p j (a b t) -> p a t b j", t=4, b=2),
             )
 
         def quant_r(k, g):
@@ -418,8 +419,8 @@ def tile_dpo_like_hidden_step_s11_kernel(tc, h, r, beta, p_chosen, p_rejected, u
             half(("pair", v // 2), v % 2)
             quant_half(("pair", (v - 1) // 2), (v - 1) % 2)
             mm_pair(v - 1)
-        load_p(4)
         load_r(0)
+        load_p(4)
         load_p(5)
         half(2, 0)
         quant_half(("pair", 1), 1)
@@ -438,51 +439,57 @@ def tile_dpo_like_hidden_step_s11_kernel(tc, h, r, beta, p_chosen, p_rejected, u
             mm_w(2, c, (0, 1))
         quant_half(2, 1)
         load_p(7)
+        load_r(1)
         load_h(0)
         load_h(1)
-        load_r(1)
         load_beta()
         turn(3)
         for c in range(ND):
             mm_w(2, c, (2, 3))
             ev_w(2, c, "s")
-        sub(4)
-        quant_c(3)
-        turn(4)
-        for c in range(ND):
-            mm_w(3, c)
-            ev_w(3, c, "s")
         inter_r(0, 0, "v")
-        quant_c(4)
+        quant_half(3, 0)
+        quant_half(3, 1)
+        sub(4)
+        for c in range(2):
+            mm_w(3, c)
+        ev_w(3, 0, "s")
+        turn(4)
+        ev_w(3, 1, "s")
+        inter_r(0, 1, "v")
+        load_r(2)
+        mm_w(3, 2)
+        ev_w(3, 2, "s")
         sub(5)
         quant_r(0, 0)
+        quant_c(4)
         turn(5)
         mm_tile(4, early)
         sub(6)
+        quant_r(0, 1)
         quant_c(5)
-        inter_r(0, 1, "v")
-        load_r(2)
         inter_p(0, 0, "s")
         turn(6)
         mm_tile(5, early)
         sub(7)
+        inter_p(0, 3, "v")
         quant_c(6)
-        quant_r(0, 1)
-        re_h(0, "v")
-        inter_p(0, 1, "s")
+        inter_r(1, 0, "v")
         quant_b(0, 0, 2)
+        inter_p(0, 1, "s")
         turn(7)
         mm_tile(6, early)
-        re_h(1, "v")
+        re_h(0, "v")
         quant_c(7)
-        quant_b(0, 2, 2)
+        quant_r(1, 0)
+        quant_b(0, 6, 2)
         inter_p(0, 2, "s")
         for k in range(2):
             tr_h(k, 0, "tp")
         for k in range(2):
             cp_h(k, 0, "s")
-        inter_r(1, 0, "v")
-        quant_b(0, 4, 2)
+        re_h(1, "v")
+        inter_r(1, 1, "v")
         mm_tile(7, early)
         ev_b(1, 0, "s")
         ev_b(1, 1, "s")
@@ -490,11 +497,12 @@ def tile_dpo_like_hidden_step_s11_kernel(tc, h, r, beta, p_chosen, p_rejected, u
         tr_h(0, 1, "tp")
         tr_h(1, 1, "acc")
         tr_h(2, 1, "acc")
+        quant_b(0, 2, 2)
+        inter_r(2, 0, "v")
+        quant_r(1, 1)
+        quant_r(2, 0)
         ev_b(1, 2, "s")
         ev_b(1, 3, "s")
-        inter_r(2, 0, "v")
-        quant_r(1, 0)
-        quant_r(2, 0)
         cp_h(2, 0, "s")
         cp_h(0, 1, "s")
         cp_h(1, 1, "s")
@@ -503,46 +511,22 @@ def tile_dpo_like_hidden_step_s11_kernel(tc, h, r, beta, p_chosen, p_rejected, u
         ev_b(1, 5, "s")
         strip(1, 6)
         for k in range(ND):
-            quant_h(k)
-        inter_r(1, 1, "v")
-        strip(1, 7)
-        quant_b(1, 0, 2)
-        quant_r(1, 1)
+            quant_h(k, 0, 256)
         inter_r(2, 1, "v")
-        strip(1, 8)
-        inter_p(0, 3, "s")
-        quant_b(1, 2, 2)
+        quant_b(0, 4, 2)
         quant_r(2, 1)
+        strip(1, 7)
+        for k in range(ND):
+            quant_h(k, 256, 512)
+        quant_b(1, 0, 2)
+        strip(1, 8)
+        quant_b(1, 2, 2)
 
 
-        def margins(g):
-            for b in range(2):
-                for w in range(2):
-                    mm_m(g, b, w)
-                    sig_m(g, b, w)
-
-
-        margins(0)
-        mul_a(0, 0)
-        quant_b(0, 6, 2)
-        quant_b(1, 4, 2)
-        quant_a(0, 0)
-        mul_a(0, 1)
-        inter_p(0, 4, "s")
-        strip(1, 9)
-        quant_b(1, 6, 2)
-        quant_a(0, 1)
-        margins(1)
-        mul_a(1, 0)
-        quant_b(0, 8, 2)
-        quant_a(1, 0)
-        strip(1, 10)
-        mul_a(1, 1)
-        quant_b(1, 8, 2)
-        quant_a(1, 1)
-        inter_p(0, 5, "v")
-        quant_b(1, 10, 1)
-        quant_b(0, 10, 2)
+        def margins(g, b):
+            for w in range(2):
+                mm_m(g, b, w)
+                sig_m(g, b, w)
 
 
         def result(i, c0, w, eng):
@@ -550,13 +534,35 @@ def tile_dpo_like_hidden_step_s11_kernel(tc, h, r, beta, p_chosen, p_rejected, u
             ev_o(i, c0, w, eng)
 
 
+        margins(0, 0)
+        mul_a(0, 0)
+        quant_b(1, 4, 2)
+        quant_a(0, 0)
+        margins(1, 0)
+        mul_a(1, 0)
+        quant_b(1, 6, 2)
+        quant_a(1, 0)
+        margins(0, 1)
+        mul_a(0, 1)
+        inter_p(0, 4, "v")
+        quant_a(0, 1)
+        margins(1, 1)
+        mul_a(1, 1)
+        quant_b(0, 8, 2)
+        quant_a(1, 1)
         for c in range(2):
             for i in range(2):
                 result(i, 512 * c, 512, "s")
+        strip(1, 9)
+        quant_b(1, 8, 2)
+        result(2, 0, 512, "v")
+        inter_p(0, 5, "s")
+        strip(1, 10)
+        quant_b(0, 10, 2)
+        quant_b(1, 10, 1)
         for i0 in (0, 2):
             mm_o2(i0, 1024)
             ev_o2(i0, 1024, "vs"[i0 // 2])
-        result(2, 0, 512, "v")
         strip(1, 11)
         quant_b(1, 11, 1)
         result(3, 0, 512, "s")

@@ -26,10 +26,10 @@ ACC_BANKS = 6
 TP_BANKS = 2
 P_BUFS = 4
 STAGE_BUFS = 6
-BST_BUFS = 5
+BST_BUFS = 6
 SIG_BUFS = 4
 OUT_BUFS = 8
-C_BUFS = 6
+C_BUFS = 5
 R_BUFS = 2
 WIDE = (3,)
 
@@ -442,7 +442,6 @@ def tile_dpo_like_hidden_step_s11_kernel(tc, h, r, beta, p_chosen, p_rejected, u
         load_r(1)
         load_h(0)
         load_h(1)
-        load_beta()
         turn(3)
         for c in range(ND):
             mm_w(2, c, (2, 3))
@@ -451,18 +450,20 @@ def tile_dpo_like_hidden_step_s11_kernel(tc, h, r, beta, p_chosen, p_rejected, u
         quant_half(3, 0)
         quant_half(3, 1)
         sub(4)
-        for c in range(2):
-            mm_w(3, c)
+        mm_w(3, 0)
+        mm_w(3, 1, (0, 1))
         ev_w(3, 0, "s")
         turn(4)
-        ev_w(3, 1, "s")
         inter_r(0, 1, "v")
         load_r(2)
+        load_beta()
+        mm_w(3, 1, (2, 3))
         mm_w(3, 2)
+        ev_w(3, 1, "s")
         ev_w(3, 2, "s")
         sub(5)
-        quant_r(0, 0)
         quant_c(4)
+        quant_r(0, 0)
         turn(5)
         mm_tile(4, early)
         sub(6)
@@ -472,17 +473,15 @@ def tile_dpo_like_hidden_step_s11_kernel(tc, h, r, beta, p_chosen, p_rejected, u
         turn(6)
         mm_tile(5, early)
         sub(7)
-        inter_p(0, 3, "v")
+        quant_b(0, 0, 2)
         quant_c(6)
         inter_r(1, 0, "v")
-        quant_b(0, 0, 2)
         inter_p(0, 1, "s")
         turn(7)
         mm_tile(6, early)
         re_h(0, "v")
         quant_c(7)
         quant_r(1, 0)
-        quant_b(0, 6, 2)
         inter_p(0, 2, "s")
         for k in range(2):
             tr_h(k, 0, "tp")
@@ -504,11 +503,10 @@ def tile_dpo_like_hidden_step_s11_kernel(tc, h, r, beta, p_chosen, p_rejected, u
         ev_b(1, 2, "s")
         ev_b(1, 3, "s")
         cp_h(2, 0, "s")
-        cp_h(0, 1, "s")
-        cp_h(1, 1, "s")
         ev_b(1, 4, "s")
-        cp_h(2, 1, "s")
         ev_b(1, 5, "s")
+        for k in range(ND):
+            cp_h(k, 1, "s")
         strip(1, 6)
         for k in range(ND):
             quant_h(k, 0, 256)
@@ -518,9 +516,7 @@ def tile_dpo_like_hidden_step_s11_kernel(tc, h, r, beta, p_chosen, p_rejected, u
         strip(1, 7)
         for k in range(ND):
             quant_h(k, 256, 512)
-        quant_b(1, 0, 2)
         strip(1, 8)
-        quant_b(1, 2, 2)
 
 
         def margins(g, b):
@@ -536,36 +532,41 @@ def tile_dpo_like_hidden_step_s11_kernel(tc, h, r, beta, p_chosen, p_rejected, u
 
         margins(0, 0)
         mul_a(0, 0)
-        quant_b(1, 4, 2)
+        quant_b(1, 0, 2)
         quant_a(0, 0)
         margins(1, 0)
         mul_a(1, 0)
-        quant_b(1, 6, 2)
+        quant_b(1, 2, 2)
         quant_a(1, 0)
         margins(0, 1)
         mul_a(0, 1)
-        inter_p(0, 4, "v")
+        quant_b(1, 4, 2)
         quant_a(0, 1)
         margins(1, 1)
         mul_a(1, 1)
-        quant_b(0, 8, 2)
+        quant_b(1, 6, 2)
         quant_a(1, 1)
-        for c in range(2):
-            for i in range(2):
-                result(i, 512 * c, 512, "s")
+        inter_p(0, 3, "s")
         strip(1, 9)
+        inter_p(0, 4, "v")
+        quant_b(0, 6, 2)
         quant_b(1, 8, 2)
-        result(2, 0, 512, "v")
-        inter_p(0, 5, "s")
+        quant_b(0, 8, 2)
+        for i in range(2):
+            result(i, 0, 512, "s")
         strip(1, 10)
-        quant_b(0, 10, 2)
+        inter_p(0, 5, "v")
         quant_b(1, 10, 1)
+        quant_b(0, 10, 2)
+        for i in range(2, 4):
+            result(i, 0, 512, "s")
+        result(0, 512, 512, "v")
         for i0 in (0, 2):
             mm_o2(i0, 1024)
-            ev_o2(i0, 1024, "vs"[i0 // 2])
+            ev_o2(i0, 1024, "sv"[i0 // 2])
         strip(1, 11)
         quant_b(1, 11, 1)
-        result(3, 0, 512, "s")
+        result(1, 512, 512, "s")
         result(2, 512, 512, "v")
         result(3, 512, 512, "s")
         for i in range(NT):

@@ -233,7 +233,8 @@ def tile_dpo_like_hidden_step_s11_kernel(tc, h, r, beta, p_chosen, p_rejected, u
                 x = work.tile([P, 2 * P, 4], BF16, name="bst", tag="bst", bufs=BST_BUFS, align_bytes=64)
                 bst[g, s // 2] = x
             c = s % 2
-            move(eng, bst[g, s // 2][:, c * P : (c + 1) * P, :], bacc[g, s][:].rearrange("p t n -> p n t"))
+            dst = bst[g, s // 2][:, c * P : (c + 1) * P, :].rearrange("p (c i) t -> p c t i", i=2)
+            move(eng, dst, bacc[g, s][:].rearrange("p t (c i) -> p c t i", i=2))
 
         def quant_b(g, s, n):
             c = s % 2
@@ -318,10 +319,12 @@ def tile_dpo_like_hidden_step_s11_kernel(tc, h, r, beta, p_chosen, p_rejected, u
 
         oacc = {}
 
-        def mm_o(i, c0, w, pool="acc"):
-            x = bank(pool, [P, 512])
+        def mm_o(i, c0, w, pool="acc", groups=(0, 1)):
+            if (i, c0) not in oacc:
+                oacc[i, c0] = bank(pool, [P, 512])
+            x = oacc[i, c0]
             rows, cols = slice(i * P, (i + 1) * P), slice(c0, c0 + w)
-            for g in range(NJ):
+            for g in groups:
                 nc.tensor.matmul_mx(
                     out=x[:, 0:w],
                     lhsT=acodes[g][:, rows].bitcast(FP8X4),
@@ -331,7 +334,6 @@ def tile_dpo_like_hidden_step_s11_kernel(tc, h, r, beta, p_chosen, p_rejected, u
                     start=(g == 0),
                     stop=(g == NJ - 1),
                 )
-            oacc[i, c0] = x
 
         def ev_o(i, c0, w, eng):
             x = work.tile([P, 512], F32, name="osb", tag="osb", bufs=OUT_BUFS, align_bytes=64)
@@ -467,13 +469,12 @@ def tile_dpo_like_hidden_step_s11_kernel(tc, h, r, beta, p_chosen, p_rejected, u
         turn(5)
         mm_tile(4, early)
         sub(6)
-        quant_r(0, 1)
         quant_c(5)
         inter_p(0, 0, "s")
         turn(6)
         mm_tile(5, early)
         sub(7)
-        quant_b(0, 0, 2)
+        quant_r(0, 1)
         quant_c(6)
         inter_r(1, 0, "v")
         inter_p(0, 1, "s")
@@ -482,6 +483,7 @@ def tile_dpo_like_hidden_step_s11_kernel(tc, h, r, beta, p_chosen, p_rejected, u
         re_h(0, "v")
         quant_c(7)
         quant_r(1, 0)
+        quant_b(0, 0, 2)
         inter_p(0, 2, "s")
         for k in range(2):
             tr_h(k, 0, "tp")
@@ -561,13 +563,17 @@ def tile_dpo_like_hidden_step_s11_kernel(tc, h, r, beta, p_chosen, p_rejected, u
         for i in range(2, 4):
             result(i, 0, 512, "s")
         result(0, 512, 512, "v")
+        result(1, 512, 512, "s")
         for i0 in (0, 2):
             mm_o2(i0, 1024)
-            ev_o2(i0, 1024, "sv"[i0 // 2])
+            ev_o2(i0, 1024, "vs"[i0 // 2])
         strip(1, 11)
         quant_b(1, 11, 1)
-        result(1, 512, 512, "s")
-        result(2, 512, 512, "v")
-        result(3, 512, 512, "s")
+        result(2, 512, 512, "s")
+        mm_o(3, 512, 512)
         for i in range(NT):
-            result(i, 1280, 256, "vs"[i % 2])
+            mm_o(i, 1280, 256, "tp" if i < 2 else "acc", (0,))
+        ev_o(3, 512, 512, "v")
+        for i in range(NT):
+            mm_o(i, 1280, 256, "acc", (1,))
+            ev_o(i, 1280, 256, "sv"[i % 2])

@@ -48,7 +48,6 @@ def tile_dpo_like_hidden_step_s11_kernel(tc, h, r, beta, p_chosen, p_rejected, u
             return x
 
         ident = kept([P, P], F32, "ident")
-        warm = kept([P, 1], F32, "warm")
         beta_sb = kept([P, NJ, 4], BF16, "beta_sb")
         usc = [kept([P, 2, D], U8, "usc%d" % a) for a in range(2)]
         ut = [kept([P, 2 * D], U8, "ut%d" % v) for v in range(NV)]
@@ -364,8 +363,6 @@ def tile_dpo_like_hidden_step_s11_kernel(tc, h, r, beta, p_chosen, p_rejected, u
             nc.sync.dma_start(out=dst, in_=x[:])
 
         def start():
-            nc.gpsimd.memset(warm[:], 0.0)
-            nc.scalar.activation(out=warm[:], in_=warm[:], func=ACT.Sigmoid)
             make_identity(nc, ident[:])
 
 

@@ -22,16 +22,13 @@ ND = D // 512
 NJ = J // 512
 NT = T // P
 NS = D // P
-ACC_BANKS = 6
-TP_BANKS = 2
 P_BUFS = 4
-STAGE_BUFS = 6
-BST_BUFS = 6
-SIG_BUFS = 4
-OUT_BUFS = 8
-C_BUFS = 5
+STAGE_BUFS = 5
+BST_BUFS = 4
+OUT_BUFS = 9
+C_BUFS = 4
 R_BUFS = 2
-WIDE = (3,)
+DIFF_BUFS = 3
 
 
 def tile_dpo_like_hidden_step_s11_kernel(tc, h, r, beta, p_chosen, p_rejected, ut_words, ut_scales, out):
@@ -39,8 +36,7 @@ def tile_dpo_like_hidden_step_s11_kernel(tc, h, r, beta, p_chosen, p_rejected, u
     with ExitStack() as ctx:
         keep = ctx.enter_context(tc.tile_pool(name="keep", bufs=1))
         work = ctx.enter_context(tc.tile_pool(name="work", bufs=2))
-        tp_pool = ctx.enter_context(tc.psum_pool(name="tp_pool", bufs=TP_BANKS))
-        acc_pool = ctx.enter_context(tc.psum_pool(name="acc_pool", bufs=ACC_BANKS))
+        psum = ctx.enter_context(tc.psum_pool(name="psum", bufs=1))
         ctx.enter_context(tc.manual_schedule())
 
         def kept(shape, dtype, name):
@@ -49,9 +45,12 @@ def tile_dpo_like_hidden_step_s11_kernel(tc, h, r, beta, p_chosen, p_rejected, u
 
         ident = kept([P, P], F32, "ident")
         beta_sb = kept([P, NJ, 4], BF16, "beta_sb")
-        usc = [kept([P, 2, D], U8, "usc%d" % a) for a in range(2)]
-        ut = [kept([P, 2 * D], U8, "ut%d" % v) for v in range(NV)]
-        braw = [kept([P, 4, 512 * WIDE[g]], BF16, "braw%d" % g) for g in range(len(WIDE))]
+        usc = [kept([P, 2, 1024], U8, "usc%d" % a) for a in range(2)] + [kept([P, NV, 512], U8, "usc2")]
+        ut = [kept([P, 2048], U8, "ut%d" % v) for v in range(NV)]
+        utc = kept([P, NV, 1024], U8, "utc")
+        braw = {0: kept([P, 4, D], BF16, "braw")}
+        bstage = kept([P, D, 4], BF16, "bstage")
+        wstage = kept([P, D, 4], BF16, "wstage")
         hraw = [kept([P, 2, D], BF16, "hraw%d" % b) for b in range(2)]
         hre = [kept([P, 2, 2, D // 4, 2], BF16, "hre%d" % b) for b in range(2)]
         hcodes = [kept([P, T], U32, "hc%d" % k) for k in range(ND)]
@@ -63,11 +62,13 @@ def tile_dpo_like_hidden_step_s11_kernel(tc, h, r, beta, p_chosen, p_rejected, u
         bcodes = [kept([P, D], U32, "bc%d" % g) for g in range(NJ)]
         bscales = [kept([P, D], U8, "bs%d" % g) for g in range(NJ)]
 
+        rings = {"tp": [0, 1], "acc": [2, 3, 4, 5, 6, 7]}
+
         def bank(pool, shape):
-            if pool == "tp":
-                x = tp_pool.tile(shape, F32, name="tp", tag="tp")
-            else:
-                x = acc_pool.tile(shape, F32, name="acc", tag="acc")
+            ring = rings[pool]
+            b = ring[0]
+            rings[pool] = ring[1:] + ring[:1]
+            x = psum.tile(shape, F32, name="bank%d" % b, tag="bank%d" % b)
             return x
 
         def move(eng, dst, src):
@@ -83,6 +84,36 @@ def tile_dpo_like_hidden_step_s11_kernel(tc, h, r, beta, p_chosen, p_rejected, u
             x = work.tile([P, 512, 4], BF16, name="stage", tag="stage", bufs=STAGE_BUFS, align_bytes=64)
             return x
 
+        def half_stage():
+            x = work.tile([P, 256, 4], BF16, name="bst", tag="bst", bufs=BST_BUFS, align_bytes=64)
+            return x
+
+        warm = {}
+
+        def warm_table():
+            x = half_stage()
+            nc.scalar.activation(out=x[:, 0:1, 0:1], in_=ident[:, 0:1].unsqueeze(2), func=ACT.Sigmoid)
+
+        def warm_zero():
+            warm["in"] = stage()
+            nc.vector.memset(warm["in"][:].rearrange("p c j -> p (c j)").bitcast(I32), 0)
+
+        def warm_quant():
+            quantize(acodes[1], ascales[1], 0, 512, warm["in"][:].rearrange("p c j -> p (c j)"))
+
+        def warm_pe(n):
+            x = psum.tile([P, 512], F32, name="bank7", tag="bank7")
+            for i in range(n):
+                nc.tensor.matmul_mx(
+                    out=x[:],
+                    lhsT=acodes[1][:, 0:P].bitcast(FP8X4),
+                    lhsT_scale=ascales[1][:, 0:P],
+                    rhs=acodes[1][:].bitcast(FP8X4),
+                    rhs_scale=ascales[1][:],
+                    start=True,
+                    stop=True,
+                )
+
         pc, pr = {}, {}
 
         def load_p(q, lo=0, hi=V):
@@ -95,36 +126,41 @@ def tile_dpo_like_hidden_step_s11_kernel(tc, h, r, beta, p_chosen, p_rejected, u
             nc.sync.dma_start(out=pc[q][:, lo:hi], in_=p_chosen[rows, :].rearrange("(m t) v -> m t v", t=4)[:, t, lo:hi])
             nc.sync.dma_start(out=pr[q][:, lo:hi], in_=p_rejected[rows, :].rearrange("(m t) v -> m t v", t=4)[:, t, lo:hi])
 
-        def load_pair(v):
-            key = ("pair", v // 2)
-            if key not in pc:
-                a = work.tile([P, V], BF16, name="pc", tag="pc", bufs=P_BUFS, align_bytes=64)
-                b = work.tile([P, V], BF16, name="pr", tag="pr", bufs=P_BUFS, align_bytes=64)
-                pc[key], pr[key] = a, b
-            cols = slice(1024 * (v % 2), 1024 * (v % 2 + 1))
-            for dst, src in ((pc[key], p_chosen), (pr[key], p_rejected)):
-                nc.sync.dma_start(
-                    out=dst[:, cols].rearrange("p (t c) -> p t c", t=2),
-                    in_=src[0:512, :].rearrange("(m t) v -> m t v", t=4)[:, 0:2, 512 * v : 512 * (v + 1)],
-                )
+        def load_pc(q):
+            g, t = divmod(q, 4)
+            a = work.tile([P, V], BF16, name="pc", tag="pc", bufs=P_BUFS, align_bytes=64)
+            b = work.tile([P, V], BF16, name="pr", tag="pr", bufs=P_BUFS, align_bytes=64)
+            pc[q], pr[q] = a, b
+            nc.sync.dma_start(out=a[:], in_=p_chosen[g * 512 : (g + 1) * 512, :].rearrange("(m t) v -> m t v", t=4)[:, t, :])
 
-        def load_ut(v):
-            nc.sync.dma_start(out=ut[v][:].bitcast(I32), in_=ut_words[v].bitcast(I32))
+        def load_pr(q, lo, hi):
+            g, t = divmod(q, 4)
+            src = p_rejected[g * 512 : (g + 1) * 512, :].rearrange("(m t) v -> m t v", t=4)
+            nc.sync.dma_start(out=pr[q][:, lo:hi], in_=src[:, t, lo:hi])
+
+        def load_utv(v):
+            nc.sync.dma_start(out=ut[v][:].bitcast(I32), in_=ut_words[v, :, 0:2048].bitcast(I32))
+
+        def load_utc():
+            nc.sync.dma_start(out=utc[:].bitcast(I32), in_=ut_words[:, :, 2048:3072].rearrange("g p n -> p g n").bitcast(I32))
 
         def zero_usc(a):
             nc.vector.memset(usc[a][:].bitcast(I32), 0)
 
         def load_usc(a):
             for rr in range(4):
-                src = ut_scales[2 * a : 2 * a + 2, rr:16:4, :]
+                src = ut_scales[2 * a : 2 * a + 2, rr:16:4, 0:1024] if a < 2 else ut_scales[:, rr:16:4, 1024:D]
                 nc.sync.dma_start(out=usc[a][rr:P:32, :, :].bitcast(I32), in_=src.rearrange("g q n -> q g n").bitcast(I32))
 
         rraw = {}
 
-        def load_r(k):
-            x = work.tile([P, 4, J], BF16, name="rraw", tag="rraw", bufs=R_BUFS, align_bytes=64)
-            nc.sync.dma_start(out=x[:], in_=r[k * 512 : (k + 1) * 512, :].rearrange("(p j) c -> p j c", j=4))
-            rraw[k] = x
+        def load_r(k, gs=(0, 1)):
+            if k not in rraw:
+                x = work.tile([P, 4, J], BF16, name="rraw", tag="rraw", bufs=R_BUFS, align_bytes=64)
+                rraw[k] = x
+            cols = slice(512 * gs[0], 512 * (gs[-1] + 1))
+            src = r[k * 512 : (k + 1) * 512, :].rearrange("(p j) c -> p j c", j=4)
+            nc.sync.dma_start(out=rraw[k][:, :, cols], in_=src[:, :, cols])
 
         def load_h(b):
             nc.sync.dma_start(out=hraw[b][:], in_=h[256 * b : 256 * (b + 1), :].rearrange("(i p) k -> p i k", p=P))
@@ -136,7 +172,7 @@ def tile_dpo_like_hidden_step_s11_kernel(tc, h, r, beta, p_chosen, p_rejected, u
 
         def sub(q, lo=0, hi=V):
             if q not in diff:
-                x = work.tile([P, 2, V // 4, 2], BF16, name="diff", tag="diff", bufs=2, align_bytes=64)
+                x = work.tile([P, 2, V // 4, 2], BF16, name="diff", tag="diff", bufs=DIFF_BUFS, align_bytes=64)
                 diff[q] = x
             nc.vector.tensor_tensor(
                 out=diff[q][:, :, lo // 4 : hi // 4, :],
@@ -175,13 +211,16 @@ def tile_dpo_like_hidden_step_s11_kernel(tc, h, r, beta, p_chosen, p_rejected, u
         bacc, bst = {}, {}
 
         def pass_any(dst, q, v, lo, n):
-            key, at = (("pair", v // 2), 2 * (v % 2) + q) if q < 2 else (q, v)
+            if lo < 1024:
+                codes, scales = ut[v][:, 2 * lo : 2 * (lo + n)], usc[v // 2][:, v % 2, lo : lo + n]
+            else:
+                codes, scales = utc[:, v, 2 * (lo - 1024) : 2 * (lo - 1024 + n)], usc[2][:, v, lo - 1024 : lo - 1024 + n]
             nc.tensor.matmul_mx(
                 out=dst,
-                lhsT=ccodes[key][:, at * P : (at + 1) * P].bitcast(FP8X4),
-                lhsT_scale=cscales[key][:, at * P : (at + 1) * P],
-                rhs=ut[v][:, 2 * lo : 2 * (lo + n)].bitcast(FP4X4),
-                rhs_scale=usc[v // 2][:, v % 2, lo : lo + n],
+                lhsT=ccodes[q][:, v * P : (v + 1) * P].bitcast(FP8X4),
+                lhsT_scale=cscales[q][:, v * P : (v + 1) * P],
+                rhs=codes.bitcast(FP4X4),
+                rhs_scale=scales,
                 start=(v == 0),
                 stop=(v == NV - 1),
             )
@@ -191,7 +230,7 @@ def tile_dpo_like_hidden_step_s11_kernel(tc, h, r, beta, p_chosen, p_rejected, u
                 bacc[g, s] = bank(pool, [P, 4, P])
             pass_any(bacc[g, s][:, t, :], 4 * g + t, v, s * P, P)
 
-        wacc, wst = {}, {}
+        wacc = {}
 
         def mm_w(q, c, vs=(0, 1, 2, 3), pool="acc"):
             if (q, c) not in wacc:
@@ -203,24 +242,16 @@ def tile_dpo_like_hidden_step_s11_kernel(tc, h, r, beta, p_chosen, p_rejected, u
             move(eng, braw[q // 4][:, q % 4, 512 * c : 512 * (c + 1)], wacc[q, c][:])
 
         def inter_b(g, c, eng, lo=0, hi=512):
-            if (g, c) not in wst:
-                wst[g, c] = stage()
-            move(eng, wst[g, c][:, lo:hi, :], braw[g][:, :, 512 * c + lo : 512 * c + hi].rearrange("p t n -> p n t"))
+            src = braw[g][:, :, 512 * c + lo : 512 * c + hi]
+            move(eng, wstage[:, 512 * c + lo : 512 * c + hi, :].rearrange("p (c i) t -> p c t i", i=4), src.rearrange("p t (c i) -> p c t i", i=4))
 
-        def inter_p(g, j, eng):
-            x = work.tile([P, 2 * P, 4], BF16, name="bst", tag="bst", bufs=BST_BUFS, align_bytes=64)
-            bst[g, j] = x
-            src = braw[g][:, :, 256 * j : 256 * (j + 1)]
-            move(eng, x[:].rearrange("p (c i) t -> p c t i", i=4), src.rearrange("p t (c i) -> p c t i", i=4))
+        def quant_w(g, c, lo=0, hi=512):
+            quantize(bcodes[g], bscales[g], 512 * c + lo, hi - lo, wstage[:, 512 * c + lo : 512 * c + hi, :].rearrange("p c j -> p (c j)"))
 
-        def quant_w(g, c):
-            quantize(bcodes[g], bscales[g], 512 * c, 512, wst[g, c][:].rearrange("p c j -> p (c j)"))
-
-        def mm_tile(q, strips, vs=(0, 1, 2, 3)):
+        def mm_ts(q, s, vs=(0, 1, 2, 3), pool="acc"):
             g, t = divmod(q, 4)
-            for s in strips:
-                for v in vs:
-                    pass_b(g, s, t, v)
+            for v in vs:
+                pass_b(g, s, t, v, pool)
 
         def mm_strip(g, s, pool="acc"):
             for t in range(4):
@@ -228,26 +259,22 @@ def tile_dpo_like_hidden_step_s11_kernel(tc, h, r, beta, p_chosen, p_rejected, u
                     pass_b(g, s, t, v, pool)
 
         def ev_b(g, s, eng):
-            if (g, s // 2) not in bst:
-                x = work.tile([P, 2 * P, 4], BF16, name="bst", tag="bst", bufs=BST_BUFS, align_bytes=64)
-                bst[g, s // 2] = x
-            c = s % 2
-            dst = bst[g, s // 2][:, c * P : (c + 1) * P, :].rearrange("p (c i) t -> p c t i", i=2)
+            dst = bstage[:, s * P : (s + 1) * P, :].rearrange("p (c i) t -> p c t i", i=2)
             move(eng, dst, bacc[g, s][:].rearrange("p t (c i) -> p c t i", i=2))
 
         def quant_b(g, s, n):
-            c = s % 2
-            src = bst[g, s // 2][:, c * P : (c + n) * P, :].rearrange("p c j -> p (c j)")
+            src = bstage[:, s * P : (s + n) * P, :].rearrange("p c j -> p (c j)")
             quantize(bcodes[g], bscales[g], s * P, n * P, src)
 
         rst, hst, hbank = {}, {}, {}
 
-        def inter_r(k, g, eng):
-            rst[k, g] = stage()
+        def inter_r(k, g, eng, lo=0, hi=512):
+            if (k, g) not in rst:
+                rst[k, g] = stage()
             move(
                 eng,
-                rst[k, g][:].rearrange("p (t a b) j -> p a t b j", t=4, b=2),
-                rraw[k][:, :, g * 512 : (g + 1) * 512].rearrange("p j (a b t) -> p a t b j", t=4, b=2),
+                rst[k, g][:].rearrange("p (t a b) j -> p a t b j", t=4, b=2)[:, lo // 8 : hi // 8, :, :, :],
+                rraw[k][:, :, g * 512 + lo : g * 512 + hi].rearrange("p j (a b t) -> p a t b j", t=4, b=2),
             )
 
         def quant_r(k, g):
@@ -260,7 +287,7 @@ def tile_dpo_like_hidden_step_s11_kernel(tc, h, r, beta, p_chosen, p_rejected, u
                 hraw[b][:].rearrange("p i (w u e) -> p i u w e", u=2, e=2),
             )
 
-        def tr_h(k, b, pool="acc"):
+        def tr_h(k, b, pool="tp"):
             x = bank(pool, [P, 2, 2, P])
             for a in range(2):
                 words = hre[b][:, a, :, :, :].rearrange("p u w e -> p (u w e)").bitcast(F32)
@@ -270,12 +297,11 @@ def tile_dpo_like_hidden_step_s11_kernel(tc, h, r, beta, p_chosen, p_rejected, u
             hbank[k, b] = x
 
         def cp_h(k, b, eng):
-            if k not in hst:
-                hst[k] = stage()
-            out_words(eng, hst[k][:, 256 * b : 256 * (b + 1), :], hbank[k, b])
+            hst[k, b] = half_stage()
+            out_words(eng, hst[k, b][:], hbank[k, b])
 
-        def quant_h(k, lo=0, hi=512):
-            quantize(hcodes[k], hscales[k], lo, hi - lo, hst[k][:, lo:hi, :].rearrange("p c j -> p (c j)"))
+        def quant_h(k, b):
+            quantize(hcodes[k], hscales[k], 256 * b, 256, hst[k, b][:].rearrange("p c j -> p (c j)"))
 
         macc, sig, ast = {}, {}, {}
 
@@ -298,22 +324,21 @@ def tile_dpo_like_hidden_step_s11_kernel(tc, h, r, beta, p_chosen, p_rejected, u
 
         def sig_m(g, b, w):
             if (g, b) not in sig:
-                x = work.tile([P, 2, 256, 2], F32, name="sig", tag="sig", bufs=SIG_BUFS, align_bytes=64)
+                x = work.tile([P, 2, 256, 2], F32, name="sig", tag="pc", bufs=P_BUFS, align_bytes=64)
                 sig[g, b] = x
             nc.scalar.activation(out=sig[g, b][:, w, :, :], in_=macc[g, b, w][:].rearrange("p e n -> p n e"), func=ACT.Sigmoid)
 
         def mul_a(g, b):
-            if g not in ast:
-                ast[g] = stage()
+            ast[g, b] = half_stage()
             nc.vector.tensor_tensor(
-                out=ast[g][:, 256 * b : 256 * (b + 1), :].rearrange("p n (w e) -> p n w e", w=2),
+                out=ast[g, b][:].rearrange("p n (w e) -> p n w e", w=2),
                 in0=sig[g, b][:].rearrange("p w n e -> p n w e"),
                 in1=beta_sb[:, g : g + 1, :].to_broadcast([P, 256, 4]).rearrange("p n (w e) -> p n w e", w=2),
                 op=ALU.mult,
             )
 
         def quant_a(g, b):
-            src = ast[g][:, 256 * b : 256 * (b + 1), :].rearrange("p c j -> p (c j)")
+            src = ast[g, b][:].rearrange("p c j -> p (c j)")
             quantize(acodes[g], ascales[g], 256 * b, 256, src)
 
         oacc = {}
@@ -362,215 +387,279 @@ def tile_dpo_like_hidden_step_s11_kernel(tc, h, r, beta, p_chosen, p_rejected, u
             dst = out[i0 * P : (i0 + 2) * P, c0 : c0 + 256].rearrange("(a p) c -> p a c", a=2)
             nc.sync.dma_start(out=dst, in_=x[:])
 
-        def start():
-            make_identity(nc, ident[:])
-
-
-        start()
+        make_identity(nc, ident[:])
+        load_p(0,0,1024)
+        warm_zero()
+        load_p(1,0,1024)
+        warm_table()
         zero_usc(0)
-        load_pair(0)
-        load_ut(0)
+        warm_quant()
         load_usc(0)
-        load_pair(1)
-        load_ut(1)
         zero_usc(1)
-        load_pair(2)
+        warm_pe(3)
+        zero_usc(2)
+        load_utv(0)
+        load_p(2,0,1024)
+        sub(0,0,1024)
+        tr_c(0,0)
+        warm_pe(2)
+        load_utv(1)
+        sub(1,0,1024)
+        load_p(0,1024,2048)
+        cp_c(0,0,"s")
+        load_p(1,1024,2048)
+        tr_c(1,0)
+        quant_c(0,0,256)
+        load_p(2,1024,2048)
+        mm_w(0,0,(0,))
+        cp_c(1,0,"s")
+        mm_w(0,1,(0,))
+        quant_c(1,0,256)
         load_usc(1)
-        load_ut(2)
-        load_pair(3)
-        load_ut(3)
-        load_p(2, 0, V // 2)
-        load_p(2, V // 2, V)
-        load_p(3)
-
-
-        def strip(g, s, eng="s"):
-            mm_strip(g, s)
-            ev_b(g, s, eng)
-
-
-        def turn(q, engs="ss"):
-            for b in range(2):
-                tr_c(q, b)
-            for b in range(2):
-                cp_c(q, b, engs[b])
-
-
-        def half(key, b):
-            sub(key, b * V // 2, (b + 1) * V // 2)
-            tr_c(key, b)
-            cp_c(key, b, "s")
-
-
-        def quant_half(key, b):
-            quant_c(key, 256 * b, 256 * (b + 1))
-
-
-        def mm_pair(v):
-            for q in range(2):
-                for c in range(ND):
-                    mm_w(q, c, (v,))
-
-
-        early = range(ACC_BANKS)
-        half(("pair", 0), 0)
-        for v in range(1, NV):
-            half(("pair", v // 2), v % 2)
-            quant_half(("pair", (v - 1) // 2), (v - 1) % 2)
-            mm_pair(v - 1)
-        load_r(0)
+        sub(2,0,1024)
+        mm_w(1,0,(0,))
+        mm_w(1,1,(0,))
+        tr_c(2,0)
+        mm_w(0,0,(1,))
+        cp_c(2,0,"s")
+        mm_w(0,1,(1,))
+        mm_w(1,0,(1,))
+        sub(0,1024,2048)
+        mm_w(1,1,(1,))
+        quant_c(2,0,256)
+        load_utv(2)
+        tr_c(0,1)
+        mm_w(2,0,(0,1))
+        load_utv(3)
+        sub(1,1024,2048)
+        cp_c(0,1,"s")
+        mm_w(2,1,(0,1))
+        load_usc(2)
+        tr_c(1,1)
+        sub(2,1024,2048)
+        load_utc()
+        quant_c(0,256,512)
+        cp_c(1,1,"s")
+        load_p(3,0,1024)
+        tr_c(2,1)
+        mm_w(0,0,(2,))
+        quant_c(1,256,512)
+        cp_c(2,1,"s")
+        mm_w(0,1,(2,))
+        mm_w(1,0,(2,))
+        load_p(3,1024,2048)
+        mm_w(1,1,(2,))
+        quant_c(2,256,512)
         load_p(4)
+        mm_w(0,0,(3,))
         load_p(5)
-        half(2, 0)
-        quant_half(("pair", 1), 1)
-        sub(2, V // 2, V)
-        mm_pair(3)
-        for c in range(ND):
-            ev_w(0, c, "svs"[c])
-        tr_c(2, 1)
-        quant_half(2, 0)
-        sub(3)
-        cp_c(2, 1, "s")
-        for c in range(ND):
-            ev_w(1, c, "s")
+        mm_w(0,1,(3,))
+        mm_w(1,0,(3,))
+        ev_w(0,0,"s")
+        mm_w(1,1,(3,))
+        ev_w(0,1,"v")
+        mm_w(2,0,(2,3))
+        ev_w(1,0,"s")
+        mm_w(2,1,(2,3))
+        ev_w(2,0,"s")
         load_p(6)
-        for c in range(ND):
-            mm_w(2, c, (0, 1))
-        quant_half(2, 1)
-        load_p(7)
-        load_r(1)
-        load_h(0)
-        load_h(1)
-        turn(3)
-        for c in range(ND):
-            mm_w(2, c, (2, 3))
-            ev_w(2, c, "s")
-        inter_r(0, 0, "v")
-        quant_half(3, 0)
-        quant_half(3, 1)
+        mm_w(0,2)
+        sub(3,0,1024)
+        ev_w(1,1,"v")
+        load_r(0)
+        tr_c(3,0)
+        mm_w(1,2)
+        sub(3,1024,2048)
+        cp_c(3,0,"s")
+        load_pc(7)
+        ev_w(2,1,"s")
+        quant_c(3,0,256)
+        tr_c(3,1)
+        load_pr(7,0,1024)
+        mm_w(2,2)
+        cp_c(3,1,"s")
+        load_pr(7,1024,2048)
+        ev_w(0,2,"s")
+        quant_c(3,256,512)
+        mm_w(3,0,(0,1))
         sub(4)
-        mm_w(3, 0)
-        mm_w(3, 1, (0, 1))
-        ev_w(3, 0, "s")
-        turn(4)
-        inter_r(0, 1, "v")
-        load_r(2)
-        load_beta()
-        mm_w(3, 1, (2, 3))
-        mm_w(3, 2)
-        ev_w(3, 1, "s")
-        ev_w(3, 2, "s")
+        ev_w(1,2,"s")
+        mm_w(3,1,(0,1))
+        load_r(1)
+        mm_w(3,2,(0,1))
+        ev_w(2,2,"v")
+        tr_c(4,0)
+        load_h(0)
         sub(5)
+        tr_c(4,1)
+        mm_w(3,0,(2,3))
+        cp_c(4,0,"s")
+        cp_c(4,1,"s")
+        mm_w(3,1,(2,3))
+        ev_w(3,0,"v")
+        mm_w(3,2,(2,3))
+        ev_w(3,1,"s")
         quant_c(4)
-        quant_r(0, 0)
-        turn(5)
-        mm_tile(4, early)
+        tr_c(5,0)
+        ev_w(3,2,"s")
+        tr_c(5,1)
         sub(6)
+        mm_ts(4,0,(0,1,2,3))
+        cp_c(5,0,"s")
+        mm_ts(4,1,(0,1,2,3))
+        mm_ts(4,2,(0,1,2,3))
+        cp_c(5,1,"s")
+        inter_b(0,0,"v",0,256)
+        mm_ts(4,3,(0,1,2,3))
+        mm_ts(4,4,(0,1,2,3))
         quant_c(5)
-        inter_p(0, 0, "s")
-        turn(6)
-        mm_tile(5, early)
-        sub(7)
-        quant_r(0, 1)
+        inter_r(0,1,"s",0,256)
+        mm_ts(4,5,(0,1,2,3))
+        tr_c(6,0)
+        inter_r(0,0,"v")
+        tr_c(6,1)
+        mm_ts(5,0,(0,1,2,3))
+        cp_c(6,0,"s")
+        mm_ts(5,1,(0,1,2,3))
+        mm_ts(5,2,(0,1,2,3))
+        cp_c(6,1,"s")
+        sub(7,0,1024)
+        mm_ts(5,3,(0,1,2,3))
+        inter_r(0,1,"s",256,512)
+        mm_ts(5,4,(0,1,2,3))
+        sub(7,1024,2048)
+        mm_ts(5,5,(0,1,2,3))
         quant_c(6)
-        inter_r(1, 0, "v")
-        inter_p(0, 1, "s")
-        turn(7)
-        mm_tile(6, early)
-        re_h(0, "v")
+        tr_c(7,0)
+        tr_c(7,1)
+        quant_r(0,0)
+        mm_ts(6,0,(0,1,2,3))
+        load_r(2)
+        cp_c(7,0,"s")
+        load_h(1)
+        load_beta()
+        mm_ts(6,1,(0,1,2,3))
+        inter_b(0,0,"v",256,512)
+        cp_c(7,1,"s")
+        mm_ts(6,2,(0,1,2,3))
+        mm_ts(6,3,(0,1,2,3))
+        inter_r(1,1,"s",0,256)
+        mm_ts(6,4,(0,1,2,3))
         quant_c(7)
-        quant_r(1, 0)
-        quant_b(0, 0, 2)
-        inter_p(0, 2, "s")
-        for k in range(2):
-            tr_h(k, 0, "tp")
-        for k in range(2):
-            cp_h(k, 0, "s")
-        re_h(1, "v")
-        inter_r(1, 1, "v")
-        mm_tile(7, early)
-        ev_b(1, 0, "s")
-        ev_b(1, 1, "s")
-        tr_h(2, 0, "tp")
-        tr_h(0, 1, "tp")
-        tr_h(1, 1, "acc")
-        tr_h(2, 1, "acc")
-        quant_b(0, 2, 2)
-        inter_r(2, 0, "v")
-        quant_r(1, 1)
-        quant_r(2, 0)
-        ev_b(1, 2, "s")
-        ev_b(1, 3, "s")
-        cp_h(2, 0, "s")
-        ev_b(1, 4, "s")
-        ev_b(1, 5, "s")
-        for k in range(ND):
-            cp_h(k, 1, "s")
-        strip(1, 6)
-        for k in range(ND):
-            quant_h(k, 0, 256)
-        inter_r(2, 1, "v")
-        quant_b(0, 4, 2)
-        quant_r(2, 1)
-        strip(1, 7)
-        for k in range(ND):
-            quant_h(k, 256, 512)
-        strip(1, 8)
-
-
-        def margins(g, b):
-            for w in range(2):
-                mm_m(g, b, w)
-                sig_m(g, b, w)
-
-
-        def result(i, c0, w, eng):
-            mm_o(i, c0, w)
-            ev_o(i, c0, w, eng)
-
-
-        margins(0, 0)
-        mul_a(0, 0)
-        quant_b(1, 0, 2)
-        quant_a(0, 0)
-        margins(1, 0)
-        mul_a(1, 0)
-        quant_b(1, 2, 2)
-        quant_a(1, 0)
-        margins(0, 1)
-        mul_a(0, 1)
-        quant_b(1, 4, 2)
-        quant_a(0, 1)
-        margins(1, 1)
-        mul_a(1, 1)
-        quant_b(1, 6, 2)
-        quant_a(1, 1)
-        inter_p(0, 3, "s")
-        strip(1, 9)
-        inter_p(0, 4, "v")
-        quant_b(0, 6, 2)
-        quant_b(1, 8, 2)
-        quant_b(0, 8, 2)
-        for i in range(2):
-            result(i, 0, 512, "s")
-        strip(1, 10)
-        inter_p(0, 5, "v")
-        quant_b(1, 10, 1)
-        quant_b(0, 10, 2)
-        for i in range(2, 4):
-            result(i, 0, 512, "s")
-        result(0, 512, 512, "v")
-        result(1, 512, 512, "s")
-        for i0 in (0, 2):
-            mm_o2(i0, 1024)
-            ev_o2(i0, 1024, "vs"[i0 // 2])
-        strip(1, 11)
-        quant_b(1, 11, 1)
-        result(2, 512, 512, "s")
-        mm_o(3, 512, 512)
-        for i in range(NT):
-            mm_o(i, 1280, 256, "tp" if i < 2 else "acc", (0,))
-        ev_o(3, 512, 512, "v")
-        for i in range(NT):
-            mm_o(i, 1280, 256, "acc", (1,))
-            ev_o(i, 1280, 256, "sv"[i % 2])
+        mm_ts(6,5,(0,1,2,3))
+        quant_r(0,1)
+        mm_ts(7,0,(0,1,2,3))
+        mm_ts(7,1,(0,1,2,3))
+        re_h(0,"v")
+        mm_ts(7,2,(0,1,2,3))
+        ev_b(1,0,"s")
+        mm_ts(7,3,(0,1,2,3))
+        mm_ts(7,4,(0,1,2,3))
+        inter_r(1,1,"s",256,512)
+        inter_r(1,0,"v")
+        mm_ts(7,5,(0,1,2,3))
+        rings["tp"], rings["acc"] = [0, 1, 2], [3, 4, 5, 6, 7]
+        tr_h(0,0)
+        tr_h(1,0)
+        ev_b(1,1,"s")
+        tr_h(2,0)
+        inter_r(2,0,"v")
+        ev_b(1,2,"s")
+        mm_strip(1,6)
+        cp_h(0,0,"s")
+        quant_r(1,0)
+        ev_b(1,3,"s")
+        mm_strip(1,7)
+        quant_r(1,1)
+        cp_h(1,0,"s")
+        re_h(1,"v")
+        cp_h(2,0,"s")
+        mm_strip(1,8)
+        ev_b(1,4,"s")
+        quant_r(2,0)
+        ev_b(1,5,"s")
+        quant_h(0,0)
+        tr_h(0,1)
+        quant_h(1,0)
+        ev_b(1,6,"s")
+        tr_h(1,1)
+        quant_h(2,0)
+        tr_h(2,1)
+        rings["tp"], rings["acc"] = [], [6, 7, 3, 4, 5, 0, 1, 2]
+        inter_r(2,1,"v")
+        ev_b(1,7,"s")
+        mm_m(0,0,0)
+        cp_h(0,1,"s")
+        cp_h(1,1,"s")
+        mm_m(0,0,1)
+        quant_w(0,0)
+        cp_h(2,1,"s")
+        quant_r(2,1)
+        mm_strip(1,9)
+        sig_m(0,0,0)
+        quant_h(0,1)
+        sig_m(0,0,1)
+        quant_h(1,1)
+        quant_h(2,1)
+        mm_m(1,0,0)
+        ev_b(1,8,"s")
+        mul_a(0,0)
+        ev_b(1,9,"s")
+        mm_m(1,0,1)
+        sig_m(1,0,0)
+        quant_b(1,0,4)
+        mm_m(0,1,0)
+        quant_a(0,0)
+        sig_m(1,0,1)
+        inter_b(0,1,"v",0,256)
+        mm_m(0,1,1)
+        inter_b(0,2,"s",0,256)
+        mul_a(1,0)
+        mm_m(1,1,0)
+        sig_m(0,1,0)
+        inter_b(0,1,"v",256,512)
+        mm_m(1,1,1)
+        sig_m(0,1,1)
+        quant_a(1,0)
+        mm_o(0,0,512)
+        sig_m(1,1,0)
+        mul_a(0,1)
+        mm_o(1,0,512)
+        sig_m(1,1,1)
+        mm_strip(1,10)
+        ev_o(0,0,512,"s")
+        quant_w(0,1)
+        ev_o(1,0,512,"s")
+        quant_b(1,4,4)
+        mm_o(0,512,512)
+        inter_b(0,2,"s",256,512)
+        mul_a(1,1)
+        mm_o(1,512,512)
+        mm_strip(1,11)
+        quant_a(0,1)
+        ev_b(1,10,"s")
+        quant_b(1,8,2)
+        ev_o(0,512,512,"s")
+        quant_a(1,1)
+        ev_o(1,512,512,"v")
+        mm_o(2,0,512)
+        ev_b(1,11,"s")
+        quant_w(0,2)
+        mm_o(3,0,512)
+        ev_o(2,0,512,"s")
+        mm_o(2,512,512)
+        quant_b(1,10,2)
+        ev_o(3,0,512,"v")
+        mm_o(3,512,512)
+        ev_o(2,512,512,"s")
+        mm_o(0,1024,512)
+        ev_o(3,512,512,"v")
+        mm_o(1,1024,512)
+        ev_o(0,1024,512,"s")
+        mm_o(2,1024,512)
+        ev_o(1,1024,512,"v")
+        mm_o(3,1024,256)
+        mm_o(3,1280,256)
+        ev_o(2,1024,512,"s")
+        ev_o(3,1024,256,"v")
+        ev_o(3,1280,256,"s")

@@ -25,9 +25,9 @@ NS = D // P
 P_BUFS = 4
 STAGE_BUFS = 5
 BST_BUFS = 4
-OUT_BUFS = 9
+OUT_BUFS = 5
 C_BUFS = 4
-R_BUFS = 2
+R_BUFS = 3
 DIFF_BUFS = 3
 
 
@@ -45,7 +45,7 @@ def tile_dpo_like_hidden_step_s11_kernel(tc, h, r, beta, p_chosen, p_rejected, u
 
         ident = kept([P, P], F32, "ident")
         beta_sb = kept([P, NJ, 4], BF16, "beta_sb")
-        usc = [kept([P, 2, 1024], U8, "usc%d" % a) for a in range(2)] + [kept([P, NV, 512], U8, "usc2")]
+        usc = [kept([P, NV, 1024], U8, "usc0"), kept([P, NV, 512], U8, "usc1")]
         ut = [kept([P, 2048], U8, "ut%d" % v) for v in range(NV)]
         utc = kept([P, NV, 1024], U8, "utc")
         braw = {0: kept([P, 4, D], BF16, "braw")}
@@ -149,7 +149,7 @@ def tile_dpo_like_hidden_step_s11_kernel(tc, h, r, beta, p_chosen, p_rejected, u
 
         def load_usc(a):
             for rr in range(4):
-                src = ut_scales[2 * a : 2 * a + 2, rr:16:4, 0:1024] if a < 2 else ut_scales[:, rr:16:4, 1024:D]
+                src = ut_scales[:, rr:16:4, 0:1024] if a == 0 else ut_scales[:, rr:16:4, 1024:D]
                 nc.sync.dma_start(out=usc[a][rr:P:32, :, :].bitcast(I32), in_=src.rearrange("g q n -> q g n").bitcast(I32))
 
         rraw = {}
@@ -212,9 +212,9 @@ def tile_dpo_like_hidden_step_s11_kernel(tc, h, r, beta, p_chosen, p_rejected, u
 
         def pass_any(dst, q, v, lo, n):
             if lo < 1024:
-                codes, scales = ut[v][:, 2 * lo : 2 * (lo + n)], usc[v // 2][:, v % 2, lo : lo + n]
+                codes, scales = ut[v][:, 2 * lo : 2 * (lo + n)], usc[0][:, v, lo : lo + n]
             else:
-                codes, scales = utc[:, v, 2 * (lo - 1024) : 2 * (lo - 1024 + n)], usc[2][:, v, lo - 1024 : lo - 1024 + n]
+                codes, scales = utc[:, v, 2 * (lo - 1024) : 2 * (lo - 1024 + n)], usc[1][:, v, lo - 1024 : lo - 1024 + n]
             nc.tensor.matmul_mx(
                 out=dst,
                 lhsT=ccodes[q][:, v * P : (v + 1) * P].bitcast(FP8X4),
@@ -341,7 +341,7 @@ def tile_dpo_like_hidden_step_s11_kernel(tc, h, r, beta, p_chosen, p_rejected, u
             src = ast[g, b][:].rearrange("p c j -> p (c j)")
             quantize(acodes[g], ascales[g], 256 * b, 256, src)
 
-        oacc = {}
+        oacc, stores = {}, []
 
         def mm_o(i, c0, w, pool="acc", groups=(0, 1)):
             if (i, c0) not in oacc:
@@ -359,8 +359,16 @@ def tile_dpo_like_hidden_step_s11_kernel(tc, h, r, beta, p_chosen, p_rejected, u
                     stop=(g == NJ - 1),
                 )
 
+        def out_tile(shape):
+            stores.append(shape)
+            if len(stores) % 2:
+                x = work.tile(shape, F32, name="osb", tag="osb", bufs=OUT_BUFS, align_bytes=64)
+            else:
+                x = work.tile(shape, F32, name="osb", tag="pr", bufs=P_BUFS, align_bytes=64)
+            return x
+
         def ev_o(i, c0, w, eng):
-            x = work.tile([P, 512], F32, name="osb", tag="osb", bufs=OUT_BUFS, align_bytes=64)
+            x = out_tile([P, 512])
             move(eng, x[:, 0:w], oacc[i, c0][:, 0:w])
             nc.sync.dma_start(out=out[i * P : (i + 1) * P, c0 : c0 + w], in_=x[:, 0:w])
 
@@ -382,164 +390,175 @@ def tile_dpo_like_hidden_step_s11_kernel(tc, h, r, beta, p_chosen, p_rejected, u
             oacc[i0, c0] = x
 
         def ev_o2(i0, c0, eng):
-            x = work.tile([P, 2, 256], F32, name="osb", tag="osb", bufs=OUT_BUFS, align_bytes=64)
+            x = out_tile([P, 2, 256])
             move(eng, x[:], oacc[i0, c0][:])
             dst = out[i0 * P : (i0 + 2) * P, c0 : c0 + 256].rearrange("(a p) c -> p a c", a=2)
             nc.sync.dma_start(out=dst, in_=x[:])
 
         make_identity(nc, ident[:])
         load_p(0,0,1024)
-        warm_zero()
+        zero_usc(0)
         load_p(1,0,1024)
         warm_table()
-        zero_usc(0)
-        warm_quant()
+        warm_zero()
         load_usc(0)
         zero_usc(1)
-        warm_pe(3)
-        zero_usc(2)
         load_utv(0)
         load_p(2,0,1024)
         sub(0,0,1024)
+        warm_quant()
         tr_c(0,0)
-        warm_pe(2)
         load_utv(1)
         sub(1,0,1024)
+        warm_pe(2)
         load_p(0,1024,2048)
         cp_c(0,0,"s")
         load_p(1,1024,2048)
-        tr_c(1,0)
         quant_c(0,0,256)
-        load_p(2,1024,2048)
-        mm_w(0,0,(0,))
+        tr_c(1,0)
+        warm_pe(1)
+        load_utv(2)
         cp_c(1,0,"s")
+        mm_w(0,0,(0,))
         mm_w(0,1,(0,))
+        load_p(2,1024,2048)
         quant_c(1,0,256)
-        load_usc(1)
         sub(2,0,1024)
         mm_w(1,0,(0,))
         mm_w(1,1,(0,))
+        load_utv(3)
         tr_c(2,0)
         mm_w(0,0,(1,))
+        load_utc()
         cp_c(2,0,"s")
         mm_w(0,1,(1,))
         mm_w(1,0,(1,))
+        load_usc(1)
         sub(0,1024,2048)
         mm_w(1,1,(1,))
         quant_c(2,0,256)
-        load_utv(2)
         tr_c(0,1)
-        mm_w(2,0,(0,1))
-        load_utv(3)
+        mm_w(2,0,(0,))
         sub(1,1024,2048)
         cp_c(0,1,"s")
-        mm_w(2,1,(0,1))
-        load_usc(2)
+        mm_w(2,1,(0,))
         tr_c(1,1)
-        sub(2,1024,2048)
-        load_utc()
         quant_c(0,256,512)
+        mm_w(2,0,(1,))
+        load_pc(3)
         cp_c(1,1,"s")
-        load_p(3,0,1024)
-        tr_c(2,1)
+        mm_w(2,1,(1,))
         mm_w(0,0,(2,))
-        quant_c(1,256,512)
-        cp_c(2,1,"s")
+        load_pr(3,0,1024)
+        sub(2,1024,2048)
         mm_w(0,1,(2,))
+        quant_c(1,256,512)
+        load_pr(3,1024,2048)
+        tr_c(2,1)
         mm_w(1,0,(2,))
-        load_p(3,1024,2048)
+        cp_c(2,1,"s")
         mm_w(1,1,(2,))
-        quant_c(2,256,512)
-        load_p(4)
         mm_w(0,0,(3,))
-        load_p(5)
         mm_w(0,1,(3,))
+        load_p(4)
+        quant_c(2,256,512)
         mm_w(1,0,(3,))
+        load_r(0)
         ev_w(0,0,"s")
+        load_pc(5)
         mm_w(1,1,(3,))
         ev_w(0,1,"v")
+        load_pr(5,0,1024)
         mm_w(2,0,(2,3))
         ev_w(1,0,"s")
+        ev_w(1,1,"v")
         mm_w(2,1,(2,3))
         ev_w(2,0,"s")
-        load_p(6)
+        load_pr(5,1024,2048)
         mm_w(0,2)
-        sub(3,0,1024)
-        ev_w(1,1,"v")
-        load_r(0)
-        tr_c(3,0)
-        mm_w(1,2)
-        sub(3,1024,2048)
-        cp_c(3,0,"s")
-        load_pc(7)
         ev_w(2,1,"s")
-        quant_c(3,0,256)
-        tr_c(3,1)
-        load_pr(7,0,1024)
-        mm_w(2,2)
-        cp_c(3,1,"s")
-        load_pr(7,1024,2048)
+        load_pc(6)
+        sub(3,0,1024)
+        mm_w(1,2)
+        load_pr(6,0,1024)
+        sub(3,1024,2048)
         ev_w(0,2,"s")
-        quant_c(3,256,512)
-        mm_w(3,0,(0,1))
-        sub(4)
+        tr_c(3,0)
+        load_pr(6,1024,2048)
+        tr_c(3,1)
+        mm_w(2,2)
+        cp_c(3,0,"s")
+        cp_c(3,1,"s")
+        load_pc(7)
+        quant_c(3,0,256)
+        sub(4,0,1024)
         ev_w(1,2,"s")
+        mm_w(3,0,(0,1))
+        quant_c(3,256,512)
+        ev_w(2,2,"s")
         mm_w(3,1,(0,1))
-        load_r(1)
+        sub(4,1024,2048)
         mm_w(3,2,(0,1))
-        ev_w(2,2,"v")
+        load_pr(7,0,1024)
+        inter_r(0,0,"v")
         tr_c(4,0)
-        load_h(0)
-        sub(5)
         tr_c(4,1)
         mm_w(3,0,(2,3))
         cp_c(4,0,"s")
+        load_pr(7,1024,2048)
         cp_c(4,1,"s")
         mm_w(3,1,(2,3))
-        ev_w(3,0,"v")
+        load_r(1)
+        sub(5,0,1024)
+        ev_w(3,0,"s")
         mm_w(3,2,(2,3))
-        ev_w(3,1,"s")
-        quant_c(4)
+        quant_c(4,0,256)
+        load_h(0)
         tr_c(5,0)
+        ev_w(3,1,"s")
+        sub(5,1024,2048)
         ev_w(3,2,"s")
+        quant_c(4,256,512)
         tr_c(5,1)
-        sub(6)
+        load_r(2)
+        inter_r(0,1,"v",0,256)
         mm_ts(4,0,(0,1,2,3))
         cp_c(5,0,"s")
         mm_ts(4,1,(0,1,2,3))
-        mm_ts(4,2,(0,1,2,3))
+        load_h(1)
+        sub(6,0,1024)
         cp_c(5,1,"s")
-        inter_b(0,0,"v",0,256)
+        mm_ts(4,2,(0,1,2,3))
         mm_ts(4,3,(0,1,2,3))
+        load_beta()
+        sub(6,1024,2048)
+        inter_b(0,0,"s",0,256)
         mm_ts(4,4,(0,1,2,3))
-        quant_c(5)
-        inter_r(0,1,"s",0,256)
         mm_ts(4,5,(0,1,2,3))
+        quant_c(5)
         tr_c(6,0)
-        inter_r(0,0,"v")
+        quant_r(0,0)
         tr_c(6,1)
         mm_ts(5,0,(0,1,2,3))
         cp_c(6,0,"s")
-        mm_ts(5,1,(0,1,2,3))
-        mm_ts(5,2,(0,1,2,3))
-        cp_c(6,1,"s")
         sub(7,0,1024)
-        mm_ts(5,3,(0,1,2,3))
-        inter_r(0,1,"s",256,512)
-        mm_ts(5,4,(0,1,2,3))
+        mm_ts(5,1,(0,1,2,3))
+        cp_c(6,1,"s")
+        mm_ts(5,2,(0,1,2,3))
         sub(7,1024,2048)
-        mm_ts(5,5,(0,1,2,3))
+        mm_ts(5,3,(0,1,2,3))
+        inter_b(0,0,"s",256,512)
+        mm_ts(5,4,(0,1,2,3))
         quant_c(6)
+        mm_ts(5,5,(0,1,2,3))
         tr_c(7,0)
+        inter_r(0,1,"v",256,512)
         tr_c(7,1)
-        quant_r(0,0)
         mm_ts(6,0,(0,1,2,3))
-        load_r(2)
+        quant_w(0,0)
         cp_c(7,0,"s")
-        load_h(1)
-        load_beta()
         mm_ts(6,1,(0,1,2,3))
-        inter_b(0,0,"v",256,512)
+        quant_r(0,1)
         cp_c(7,1,"s")
         mm_ts(6,2,(0,1,2,3))
         mm_ts(6,3,(0,1,2,3))
@@ -547,111 +566,110 @@ def tile_dpo_like_hidden_step_s11_kernel(tc, h, r, beta, p_chosen, p_rejected, u
         mm_ts(6,4,(0,1,2,3))
         quant_c(7)
         mm_ts(6,5,(0,1,2,3))
-        quant_r(0,1)
+        inter_r(1,0,"v",0,256)
         mm_ts(7,0,(0,1,2,3))
         mm_ts(7,1,(0,1,2,3))
+        inter_r(1,1,"s",256,512)
         re_h(0,"v")
         mm_ts(7,2,(0,1,2,3))
-        ev_b(1,0,"s")
         mm_ts(7,3,(0,1,2,3))
         mm_ts(7,4,(0,1,2,3))
-        inter_r(1,1,"s",256,512)
-        inter_r(1,0,"v")
+        inter_r(1,0,"v",256,512)
         mm_ts(7,5,(0,1,2,3))
         rings["tp"], rings["acc"] = [0, 1, 2], [3, 4, 5, 6, 7]
+        ev_b(1,0,"s")
         tr_h(0,0)
-        tr_h(1,0)
-        ev_b(1,1,"s")
-        tr_h(2,0)
         inter_r(2,0,"v")
+        ev_b(1,1,"s")
+        tr_h(1,0)
+        tr_h(2,0)
         ev_b(1,2,"s")
         mm_strip(1,6)
         cp_h(0,0,"s")
         quant_r(1,0)
-        ev_b(1,3,"s")
-        mm_strip(1,7)
-        quant_r(1,1)
         cp_h(1,0,"s")
+        quant_r(1,1)
+        mm_strip(1,7)
+        ev_b(1,3,"s")
         re_h(1,"v")
         cp_h(2,0,"s")
         mm_strip(1,8)
-        ev_b(1,4,"s")
         quant_r(2,0)
-        ev_b(1,5,"s")
+        ev_b(1,4,"s")
         quant_h(0,0)
-        tr_h(0,1)
+        ev_b(1,5,"s")
         quant_h(1,0)
+        tr_h(0,1)
+        quant_h(2,0)
         ev_b(1,6,"s")
         tr_h(1,1)
-        quant_h(2,0)
-        tr_h(2,1)
-        rings["tp"], rings["acc"] = [], [6, 7, 3, 4, 5, 0, 1, 2]
         inter_r(2,1,"v")
         ev_b(1,7,"s")
+        tr_h(2,1)
+        rings["tp"], rings["acc"] = [], [6, 7, 3, 4, 5, 0, 1, 2]
         mm_m(0,0,0)
         cp_h(0,1,"s")
+        quant_b(1,0,4)
         cp_h(1,1,"s")
         mm_m(0,0,1)
-        quant_w(0,0)
-        cp_h(2,1,"s")
         quant_r(2,1)
+        cp_h(2,1,"s")
         mm_strip(1,9)
-        sig_m(0,0,0)
         quant_h(0,1)
-        sig_m(0,0,1)
+        sig_m(0,0,0)
         quant_h(1,1)
+        sig_m(0,0,1)
         quant_h(2,1)
+        inter_b(0,1,"v",0,256)
         mm_m(1,0,0)
         ev_b(1,8,"s")
         mul_a(0,0)
         ev_b(1,9,"s")
         mm_m(1,0,1)
         sig_m(1,0,0)
-        quant_b(1,0,4)
         mm_m(0,1,0)
-        quant_a(0,0)
+        inter_b(0,1,"v",256,512)
         sig_m(1,0,1)
-        inter_b(0,1,"v",0,256)
+        quant_a(0,0)
         mm_m(0,1,1)
         inter_b(0,2,"s",0,256)
         mul_a(1,0)
         mm_m(1,1,0)
         sig_m(0,1,0)
-        inter_b(0,1,"v",256,512)
+        quant_w(0,1)
         mm_m(1,1,1)
         sig_m(0,1,1)
         quant_a(1,0)
+        quant_b(1,4,4)
         mm_o(0,0,512)
         sig_m(1,1,0)
         mul_a(0,1)
         mm_o(1,0,512)
         sig_m(1,1,1)
-        mm_strip(1,10)
-        ev_o(0,0,512,"s")
-        quant_w(0,1)
-        ev_o(1,0,512,"s")
-        quant_b(1,4,4)
         mm_o(0,512,512)
-        inter_b(0,2,"s",256,512)
-        mul_a(1,1)
-        mm_o(1,512,512)
-        mm_strip(1,11)
-        quant_a(0,1)
-        ev_b(1,10,"s")
+        ev_o(0,0,512,"s")
         quant_b(1,8,2)
+        mm_o(1,512,512)
+        ev_o(1,0,512,"s")
+        mul_a(1,1)
+        mm_strip(1,10)
         ev_o(0,512,512,"s")
+        inter_b(0,2,"s",256,512)
+        quant_a(0,1)
         quant_a(1,1)
-        ev_o(1,512,512,"v")
         mm_o(2,0,512)
-        ev_b(1,11,"s")
-        quant_w(0,2)
+        ev_o(1,512,512,"v")
         mm_o(3,0,512)
+        ev_b(1,10,"s")
+        quant_w(0,2)
+        mm_strip(1,11)
         ev_o(2,0,512,"s")
-        mm_o(2,512,512)
-        quant_b(1,10,2)
         ev_o(3,0,512,"v")
+        mm_o(2,512,512)
+        ev_b(1,11,"s")
         mm_o(3,512,512)
         ev_o(2,512,512,"s")
+        quant_b(1,10,2)
         mm_o(0,1024,512)
         ev_o(3,512,512,"v")
         mm_o(1,1024,512)

@@ -253,6 +253,18 @@ def tile_dpo_like_hidden_step_s11_kernel(tc, h, r, beta, p_chosen, p_rejected, u
             for v in vs:
                 pass_b(g, s, t, v, pool)
 
+        def mm_tile(q, vs=(0, 1, 2, 3)):
+            g, t = divmod(q, 4)
+            for v in vs:
+                for s in range(6):
+                    pass_b(g, s, t, v)
+
+        def mm_strips(g, s0, n):
+            for t in range(4):
+                for v in range(NV):
+                    for s in range(s0, s0 + n):
+                        pass_b(g, s, t, v)
+
         def mm_strip(g, s, pool="acc"):
             for t in range(4):
                 for v in range(NV):
@@ -414,12 +426,12 @@ def tile_dpo_like_hidden_step_s11_kernel(tc, h, r, beta, p_chosen, p_rejected, u
         load_p(0,1024,2048)
         cp_c(0,0,"s")
         load_p(1,1024,2048)
-        quant_c(0,0,256)
         tr_c(1,0)
+        quant_c(0,0,256)
         warm_pe(1)
         load_utv(2)
-        cp_c(1,0,"s")
         mm_w(0,0,(0,))
+        cp_c(1,0,"s")
         mm_w(0,1,(0,))
         load_p(2,1024,2048)
         quant_c(1,0,256)
@@ -430,24 +442,24 @@ def tile_dpo_like_hidden_step_s11_kernel(tc, h, r, beta, p_chosen, p_rejected, u
         tr_c(2,0)
         mm_w(0,0,(1,))
         load_utc()
-        cp_c(2,0,"s")
         mm_w(0,1,(1,))
-        mm_w(1,0,(1,))
+        cp_c(2,0,"s")
         load_usc(1)
         sub(0,1024,2048)
+        mm_w(1,0,(1,))
         mm_w(1,1,(1,))
         quant_c(2,0,256)
         tr_c(0,1)
         mm_w(2,0,(0,))
         sub(1,1024,2048)
-        cp_c(0,1,"s")
         mm_w(2,1,(0,))
+        cp_c(0,1,"s")
         tr_c(1,1)
         quant_c(0,256,512)
         mm_w(2,0,(1,))
         load_pc(3)
-        cp_c(1,1,"s")
         mm_w(2,1,(1,))
+        cp_c(1,1,"s")
         mm_w(0,0,(2,))
         load_pr(3,0,1024)
         sub(2,1024,2048)
@@ -456,25 +468,25 @@ def tile_dpo_like_hidden_step_s11_kernel(tc, h, r, beta, p_chosen, p_rejected, u
         load_pr(3,1024,2048)
         tr_c(2,1)
         mm_w(1,0,(2,))
-        cp_c(2,1,"s")
         mm_w(1,1,(2,))
+        cp_c(2,1,"s")
         mm_w(0,0,(3,))
         mm_w(0,1,(3,))
         load_p(4)
-        quant_c(2,256,512)
         mm_w(1,0,(3,))
+        quant_c(2,256,512)
         load_r(0)
         ev_w(0,0,"s")
         load_pc(5)
         mm_w(1,1,(3,))
-        ev_w(0,1,"v")
         load_pr(5,0,1024)
+        ev_w(0,1,"v")
         mm_w(2,0,(2,3))
         ev_w(1,0,"s")
         ev_w(1,1,"v")
         mm_w(2,1,(2,3))
-        ev_w(2,0,"s")
         load_pr(5,1024,2048)
+        ev_w(2,0,"s")
         mm_w(0,2)
         ev_w(2,1,"s")
         load_pc(6)
@@ -488,8 +500,8 @@ def tile_dpo_like_hidden_step_s11_kernel(tc, h, r, beta, p_chosen, p_rejected, u
         tr_c(3,1)
         mm_w(2,2)
         cp_c(3,0,"s")
-        cp_c(3,1,"s")
         load_pc(7)
+        cp_c(3,1,"s")
         quant_c(3,0,256)
         sub(4,0,1024)
         ev_w(1,2,"s")
@@ -504,173 +516,161 @@ def tile_dpo_like_hidden_step_s11_kernel(tc, h, r, beta, p_chosen, p_rejected, u
         tr_c(4,0)
         tr_c(4,1)
         mm_w(3,0,(2,3))
-        cp_c(4,0,"s")
         load_pr(7,1024,2048)
-        cp_c(4,1,"s")
+        cp_c(4,0,"s")
         mm_w(3,1,(2,3))
+        cp_c(4,1,"s")
         load_r(1)
         sub(5,0,1024)
-        ev_w(3,0,"s")
         mm_w(3,2,(2,3))
+        ev_w(3,0,"s")
         quant_c(4,0,256)
         load_h(0)
+        sub(5,1024,2048)
         tr_c(5,0)
         ev_w(3,1,"s")
-        sub(5,1024,2048)
-        ev_w(3,2,"s")
         quant_c(4,256,512)
         tr_c(5,1)
+        ev_w(3,2,"s")
         load_r(2)
         inter_r(0,1,"v",0,256)
-        mm_ts(4,0,(0,1,2,3))
+        mm_tile(4)
         cp_c(5,0,"s")
-        mm_ts(4,1,(0,1,2,3))
         load_h(1)
         sub(6,0,1024)
         cp_c(5,1,"s")
-        mm_ts(4,2,(0,1,2,3))
-        mm_ts(4,3,(0,1,2,3))
         load_beta()
         sub(6,1024,2048)
         inter_b(0,0,"s",0,256)
-        mm_ts(4,4,(0,1,2,3))
-        mm_ts(4,5,(0,1,2,3))
         quant_c(5)
         tr_c(6,0)
         quant_r(0,0)
         tr_c(6,1)
-        mm_ts(5,0,(0,1,2,3))
-        cp_c(6,0,"s")
+        mm_tile(5)
         sub(7,0,1024)
-        mm_ts(5,1,(0,1,2,3))
-        cp_c(6,1,"s")
-        mm_ts(5,2,(0,1,2,3))
+        cp_c(6,0,"s")
         sub(7,1024,2048)
-        mm_ts(5,3,(0,1,2,3))
+        cp_c(6,1,"s")
         inter_b(0,0,"s",256,512)
-        mm_ts(5,4,(0,1,2,3))
         quant_c(6)
-        mm_ts(5,5,(0,1,2,3))
         tr_c(7,0)
         inter_r(0,1,"v",256,512)
         tr_c(7,1)
-        mm_ts(6,0,(0,1,2,3))
-        quant_w(0,0)
+        mm_tile(6)
         cp_c(7,0,"s")
-        mm_ts(6,1,(0,1,2,3))
         quant_r(0,1)
         cp_c(7,1,"s")
-        mm_ts(6,2,(0,1,2,3))
-        mm_ts(6,3,(0,1,2,3))
+        quant_w(0,0,0,256)
+        quant_c(7,0,256)
         inter_r(1,1,"s",0,256)
-        mm_ts(6,4,(0,1,2,3))
-        quant_c(7)
-        mm_ts(6,5,(0,1,2,3))
-        inter_r(1,0,"v",0,256)
+        quant_c(7,256,512)
         mm_ts(7,0,(0,1,2,3))
-        mm_ts(7,1,(0,1,2,3))
-        inter_r(1,1,"s",256,512)
         re_h(0,"v")
+        mm_ts(7,1,(0,1,2,3))
         mm_ts(7,2,(0,1,2,3))
+        ev_b(1,0,"s")
+        inter_r(1,0,"v")
         mm_ts(7,3,(0,1,2,3))
         mm_ts(7,4,(0,1,2,3))
-        inter_r(1,0,"v",256,512)
+        ev_b(1,1,"s")
         mm_ts(7,5,(0,1,2,3))
         rings["tp"], rings["acc"] = [0, 1, 2], [3, 4, 5, 6, 7]
-        ev_b(1,0,"s")
         tr_h(0,0)
+        ev_b(1,2,"s")
         inter_r(2,0,"v")
-        ev_b(1,1,"s")
         tr_h(1,0)
         tr_h(2,0)
-        ev_b(1,2,"s")
-        mm_strip(1,6)
         cp_h(0,0,"s")
-        quant_r(1,0)
+        mm_strip(1,6)
         cp_h(1,0,"s")
-        quant_r(1,1)
-        mm_strip(1,7)
+        quant_r(1,0)
         ev_b(1,3,"s")
         re_h(1,"v")
+        mm_strip(1,7)
         cp_h(2,0,"s")
-        mm_strip(1,8)
         quant_r(2,0)
         ev_b(1,4,"s")
-        quant_h(0,0)
+        mm_strip(1,8)
+        inter_r(1,1,"v",256,512)
         ev_b(1,5,"s")
+        ev_b(1,6,"s")
+        quant_h(0,0)
         quant_h(1,0)
         tr_h(0,1)
-        quant_h(2,0)
-        ev_b(1,6,"s")
-        tr_h(1,1)
-        inter_r(2,1,"v")
         ev_b(1,7,"s")
+        quant_h(2,0)
+        tr_h(1,1)
+        quant_r(1,1)
         tr_h(2,1)
         rings["tp"], rings["acc"] = [], [6, 7, 3, 4, 5, 0, 1, 2]
-        mm_m(0,0,0)
         cp_h(0,1,"s")
-        quant_b(1,0,4)
+        mm_m(0,0,0)
+        inter_r(2,1,"v")
         cp_h(1,1,"s")
         mm_m(0,0,1)
-        quant_r(2,1)
         cp_h(2,1,"s")
-        mm_strip(1,9)
-        quant_h(0,1)
+        quant_w(0,0,256,512)
         sig_m(0,0,0)
-        quant_h(1,1)
+        mm_strip(1,9)
+        quant_b(1,0,4)
         sig_m(0,0,1)
-        quant_h(2,1)
-        inter_b(0,1,"v",0,256)
-        mm_m(1,0,0)
+        quant_r(2,1)
         ev_b(1,8,"s")
-        mul_a(0,0)
+        mm_m(1,0,0)
+        quant_h(0,1)
+        quant_h(1,1)
         ev_b(1,9,"s")
+        quant_h(2,1)
         mm_m(1,0,1)
+        mul_a(0,0)
         sig_m(1,0,0)
         mm_m(0,1,0)
-        inter_b(0,1,"v",256,512)
         sig_m(1,0,1)
-        quant_a(0,0)
+        inter_b(0,1,"v",0,256)
         mm_m(0,1,1)
         inter_b(0,2,"s",0,256)
+        quant_a(0,0)
         mul_a(1,0)
         mm_m(1,1,0)
-        sig_m(0,1,0)
-        quant_w(0,1)
         mm_m(1,1,1)
-        sig_m(0,1,1)
+        sig_m(0,1,0)
+        quant_w(0,1,0,256)
         quant_a(1,0)
-        quant_b(1,4,4)
+        sig_m(0,1,1)
         mm_o(0,0,512)
+        inter_b(0,1,"v",256,512)
         sig_m(1,1,0)
-        mul_a(0,1)
         mm_o(1,0,512)
+        quant_b(1,4,4)
         sig_m(1,1,1)
-        mm_o(0,512,512)
-        ev_o(0,0,512,"s")
-        quant_b(1,8,2)
-        mm_o(1,512,512)
-        ev_o(1,0,512,"s")
-        mul_a(1,1)
         mm_strip(1,10)
+        quant_w(0,1,256,512)
+        ev_o(0,0,512,"s")
+        mul_a(0,1)
+        ev_o(1,0,512,"s")
+        mm_o(0,512,512)
+        ev_b(1,10,"s")
+        mul_a(1,1)
+        mm_o(1,512,512)
         ev_o(0,512,512,"s")
-        inter_b(0,2,"s",256,512)
+        mm_strip(1,11)
         quant_a(0,1)
+        ev_o(1,512,512,"s")
+        quant_b(1,8,2)
         quant_a(1,1)
         mm_o(2,0,512)
-        ev_o(1,512,512,"v")
-        mm_o(3,0,512)
-        ev_b(1,10,"s")
-        quant_w(0,2)
-        mm_strip(1,11)
-        ev_o(2,0,512,"s")
-        ev_o(3,0,512,"v")
-        mm_o(2,512,512)
+        inter_b(0,2,"v",256,512)
         ev_b(1,11,"s")
-        mm_o(3,512,512)
-        ev_o(2,512,512,"s")
+        mm_o(3,0,512)
+        quant_w(0,2,0,256)
+        ev_o(2,0,512,"s")
+        mm_o(2,512,512)
         quant_b(1,10,2)
+        quant_w(0,2,256,512)
+        ev_o(3,0,512,"s")
+        mm_o(3,512,512)
         mm_o(0,1024,512)
+        ev_o(2,512,512,"s")
         ev_o(3,512,512,"v")
         mm_o(1,1024,512)
         ev_o(0,1024,512,"s")

@@ -24,8 +24,8 @@ NT = T // P
 NS = D // P
 P_BUFS = 4
 STAGE_BUFS = 5
-BST_BUFS = 4
-OUT_BUFS = 5
+BST_BUFS = 3
+OUT_BUFS = 4
 C_BUFS = 4
 R_BUFS = 3
 DIFF_BUFS = 3
@@ -48,7 +48,7 @@ def tile_dpo_like_hidden_step_s11_kernel(tc, h, r, beta, p_chosen, p_rejected, u
         usc = [kept([P, NV, 1024], U8, "usc0"), kept([P, NV, 512], U8, "usc1")]
         ut = [kept([P, 2048], U8, "ut%d" % v) for v in range(NV)]
         utc = kept([P, NV, 1024], U8, "utc")
-        braw = {0: kept([P, 4, D], BF16, "braw")}
+        braw = [kept([P, 4, D], BF16, "braw0"), kept([P, 4, 512], BF16, "braw1")]
         bstage = kept([P, D, 4], BF16, "bstage")
         wstage = kept([P, D, 4], BF16, "wstage")
         hraw = [kept([P, 2, D], BF16, "hraw%d" % b) for b in range(2)]
@@ -65,9 +65,12 @@ def tile_dpo_like_hidden_step_s11_kernel(tc, h, r, beta, p_chosen, p_rejected, u
         rings = {"tp": [0, 1], "acc": [2, 3, 4, 5, 6, 7]}
 
         def bank(pool, shape):
-            ring = rings[pool]
-            b = ring[0]
-            rings[pool] = ring[1:] + ring[:1]
+            if isinstance(pool, int):
+                b = pool
+            else:
+                ring = rings[pool]
+                b = ring[0]
+                rings[pool] = ring[1:] + ring[:1]
             x = psum.tile(shape, F32, name="bank%d" % b, tag="bank%d" % b)
             return x
 
@@ -239,14 +242,14 @@ def tile_dpo_like_hidden_step_s11_kernel(tc, h, r, beta, p_chosen, p_rejected, u
                 pass_any(wacc[q, c][:], q, v, 512 * c, 512)
 
         def ev_w(q, c, eng):
-            move(eng, braw[q // 4][:, q % 4, 512 * c : 512 * (c + 1)], wacc[q, c][:])
+            move(eng, braw[q // 4][:, q % 4, 512 * c : 512 * (c + 1)] if q < 4 else braw[1][:, q % 4, :], wacc[q, c][:])
 
         def inter_b(g, c, eng, lo=0, hi=512):
-            src = braw[g][:, :, 512 * c + lo : 512 * c + hi]
-            move(eng, wstage[:, 512 * c + lo : 512 * c + hi, :].rearrange("p (c i) t -> p c t i", i=4), src.rearrange("p t (c i) -> p c t i", i=4))
+            src = braw[g][:, :, 512 * c + lo : 512 * c + hi] if g == 0 else braw[1][:, :, lo:hi]
+            move(eng, (wstage, bstage)[g][:, 512 * c + lo : 512 * c + hi, :].rearrange("p (c i) t -> p c t i", i=4), src.rearrange("p t (c i) -> p c t i", i=4))
 
         def quant_w(g, c, lo=0, hi=512):
-            quantize(bcodes[g], bscales[g], 512 * c + lo, hi - lo, wstage[:, 512 * c + lo : 512 * c + hi, :].rearrange("p c j -> p (c j)"))
+            quantize(bcodes[g], bscales[g], 512 * c + lo, hi - lo, (wstage, bstage)[g][:, 512 * c + lo : 512 * c + hi, :].rearrange("p c j -> p (c j)"))
 
         def mm_ts(q, s, vs=(0, 1, 2, 3), pool="acc"):
             g, t = divmod(q, 4)
@@ -256,8 +259,8 @@ def tile_dpo_like_hidden_step_s11_kernel(tc, h, r, beta, p_chosen, p_rejected, u
         def mm_tile(q, vs=(0, 1, 2, 3)):
             g, t = divmod(q, 4)
             for v in vs:
-                for s in range(6):
-                    pass_b(g, s, t, v)
+                for s in range(4):
+                    pass_b(g, s, t, v, 2 + s)
 
         def mm_strips(g, s0, n):
             for t in range(4):
@@ -373,8 +376,10 @@ def tile_dpo_like_hidden_step_s11_kernel(tc, h, r, beta, p_chosen, p_rejected, u
 
         def out_tile(shape):
             stores.append(shape)
-            if len(stores) % 2:
+            if len(stores) % 3 == 1:
                 x = work.tile(shape, F32, name="osb", tag="osb", bufs=OUT_BUFS, align_bytes=64)
+            elif len(stores) % 3 == 2:
+                x = work.tile(shape, F32, name="osb", tag="diff", bufs=DIFF_BUFS, align_bytes=64)
             else:
                 x = work.tile(shape, F32, name="osb", tag="pr", bufs=P_BUFS, align_bytes=64)
             return x
@@ -425,18 +430,18 @@ def tile_dpo_like_hidden_step_s11_kernel(tc, h, r, beta, p_chosen, p_rejected, u
         warm_pe(2)
         load_p(0,1024,2048)
         cp_c(0,0,"s")
-        load_p(1,1024,2048)
-        tr_c(1,0)
         quant_c(0,0,256)
+        tr_c(1,0)
+        load_p(1,1024,2048)
         warm_pe(1)
-        load_utv(2)
-        mm_w(0,0,(0,))
         cp_c(1,0,"s")
+        mm_w(0,0,(0,))
+        load_utv(2)
         mm_w(0,1,(0,))
-        load_p(2,1024,2048)
         quant_c(1,0,256)
-        sub(2,0,1024)
+        load_p(2,1024,2048)
         mm_w(1,0,(0,))
+        sub(2,0,1024)
         mm_w(1,1,(0,))
         load_utv(3)
         tr_c(2,0)
@@ -444,9 +449,9 @@ def tile_dpo_like_hidden_step_s11_kernel(tc, h, r, beta, p_chosen, p_rejected, u
         load_utc()
         mm_w(0,1,(1,))
         cp_c(2,0,"s")
+        mm_w(1,0,(1,))
         load_usc(1)
         sub(0,1024,2048)
-        mm_w(1,0,(1,))
         mm_w(1,1,(1,))
         quant_c(2,0,256)
         tr_c(0,1)
@@ -472,212 +477,215 @@ def tile_dpo_like_hidden_step_s11_kernel(tc, h, r, beta, p_chosen, p_rejected, u
         cp_c(2,1,"s")
         mm_w(0,0,(3,))
         mm_w(0,1,(3,))
-        load_p(4)
-        mm_w(1,0,(3,))
-        quant_c(2,256,512)
         load_r(0)
+        quant_c(2,256,512)
+        load_pc(4)
+        mm_w(1,0,(3,))
         ev_w(0,0,"s")
-        load_pc(5)
+        load_pr(4,0,1024)
         mm_w(1,1,(3,))
-        load_pr(5,0,1024)
+        load_pr(4,1024,2048)
         ev_w(0,1,"v")
         mm_w(2,0,(2,3))
+        load_pc(5)
         ev_w(1,0,"s")
         ev_w(1,1,"v")
         mm_w(2,1,(2,3))
-        load_pr(5,1024,2048)
         ev_w(2,0,"s")
-        mm_w(0,2)
+        mm_w(0,2,(0,1,2,3),2)
+        load_pr(5,0,1024)
         ev_w(2,1,"s")
-        load_pc(6)
+        load_pr(5,1024,2048)
         sub(3,0,1024)
-        mm_w(1,2)
-        load_pr(6,0,1024)
+        mm_w(1,2,(0,1,2,3),3)
+        load_pc(6)
         sub(3,1024,2048)
         ev_w(0,2,"s")
         tr_c(3,0)
-        load_pr(6,1024,2048)
         tr_c(3,1)
-        mm_w(2,2)
+        mm_w(2,2,(0,1,2,3),4)
         cp_c(3,0,"s")
-        load_pc(7)
+        load_pr(6,0,1024)
         cp_c(3,1,"s")
         quant_c(3,0,256)
-        sub(4,0,1024)
+        inter_r(0,0,"v",0,256)
         ev_w(1,2,"s")
-        mm_w(3,0,(0,1))
-        quant_c(3,256,512)
+        mm_w(3,0,(0,1),5)
+        load_pr(6,1024,2048)
         ev_w(2,2,"s")
-        mm_w(3,1,(0,1))
-        sub(4,1024,2048)
-        mm_w(3,2,(0,1))
-        load_pr(7,0,1024)
-        inter_r(0,0,"v")
-        tr_c(4,0)
-        tr_c(4,1)
+        mm_w(3,1,(0,1),6)
+        quant_c(3,256,512)
+        mm_w(3,2,(0,1),7)
+        load_h(0)
+        sub(4,0,1024)
         mm_w(3,0,(2,3))
-        load_pr(7,1024,2048)
-        cp_c(4,0,"s")
+        load_pc(7)
+        sub(4,1024,2048)
+        tr_c(4,0)
+        inter_r(0,0,"v",256,512)
+        ev_w(3,0,"s")
+        tr_c(4,1)
+        load_pr(7,0,1024)
         mm_w(3,1,(2,3))
-        cp_c(4,1,"s")
-        load_r(1)
+        cp_c(4,0,"s")
+        load_pr(7,1024,2048)
         sub(5,0,1024)
         mm_w(3,2,(2,3))
-        ev_w(3,0,"s")
-        quant_c(4,0,256)
-        load_h(0)
+        cp_c(4,1,"s")
+        load_r(1)
         sub(5,1024,2048)
         tr_c(5,0)
         ev_w(3,1,"s")
-        quant_c(4,256,512)
+        quant_c(4,0,256)
         tr_c(5,1)
         ev_w(3,2,"s")
+        quant_c(4,256,512)
+        mm_w(4,1,(0,1,2,3),4)
         load_r(2)
         inter_r(0,1,"v",0,256)
-        mm_tile(4)
         cp_c(5,0,"s")
         load_h(1)
-        sub(6,0,1024)
         cp_c(5,1,"s")
+        sub(6,0,1024)
+        mm_ts(4,0,(0,1,2,3),2)
         load_beta()
-        sub(6,1024,2048)
         inter_b(0,0,"s",0,256)
+        sub(6,1024,2048)
+        mm_ts(4,1,(0,1,2,3),3)
+        mm_ts(4,2,(0,1,2,3),5)
         quant_c(5)
+        mm_ts(4,3,(0,1,2,3),6)
         tr_c(6,0)
-        quant_r(0,0)
-        tr_c(6,1)
-        mm_tile(5)
-        sub(7,0,1024)
-        cp_c(6,0,"s")
-        sub(7,1024,2048)
-        cp_c(6,1,"s")
-        inter_b(0,0,"s",256,512)
-        quant_c(6)
-        tr_c(7,0)
         inter_r(0,1,"v",256,512)
-        tr_c(7,1)
-        mm_tile(6)
-        cp_c(7,0,"s")
-        quant_r(0,1)
-        cp_c(7,1,"s")
-        quant_w(0,0,0,256)
-        quant_c(7,0,256)
-        inter_r(1,1,"s",0,256)
-        quant_c(7,256,512)
-        mm_ts(7,0,(0,1,2,3))
+        ev_w(4,1,"s")
+        tr_c(6,1)
+        mm_w(5,1,(0,1,2,3),7)
         re_h(0,"v")
-        mm_ts(7,1,(0,1,2,3))
-        mm_ts(7,2,(0,1,2,3))
-        ev_b(1,0,"s")
+        cp_c(6,0,"s")
+        cp_c(6,1,"s")
+        quant_r(0,0)
+        mm_tile(5)
+        inter_b(0,0,"s",256,512)
+        sub(7,0,1024)
+        sub(7,1024,2048)
+        tr_c(7,0)
+        ev_w(5,1,"s")
+        quant_c(6,0,256)
+        tr_c(7,1)
+        quant_c(6,256,512)
+        mm_w(6,1,(0,1,2,3),4)
+        quant_r(0,1)
+        cp_c(7,0,"s")
+        cp_c(7,1,"s")
+        inter_b(0,1,"v",0,256)
+        mm_tile(6)
         inter_r(1,0,"v")
-        mm_ts(7,3,(0,1,2,3))
-        mm_ts(7,4,(0,1,2,3))
-        ev_b(1,1,"s")
-        mm_ts(7,5,(0,1,2,3))
-        rings["tp"], rings["acc"] = [0, 1, 2], [3, 4, 5, 6, 7]
-        tr_h(0,0)
-        ev_b(1,2,"s")
+        ev_w(6,1,"s")
+        inter_r(1,1,"s",0,256)
+        tr_h(0,0,0)
+        quant_c(7)
+        tr_h(1,0,1)
+        tr_h(2,0,4)
         inter_r(2,0,"v")
-        tr_h(1,0)
-        tr_h(2,0)
         cp_h(0,0,"s")
-        mm_strip(1,6)
+        mm_w(7,1,(0,1,2,3),7)
         cp_h(1,0,"s")
         quant_r(1,0)
-        ev_b(1,3,"s")
-        re_h(1,"v")
-        mm_strip(1,7)
         cp_h(2,0,"s")
+        mm_ts(7,0)
+        mm_ts(7,1)
+        re_h(1,"v")
+        mm_ts(7,2)
+        ev_b(1,0,"s")
+        mm_ts(7,3)
         quant_r(2,0)
-        ev_b(1,4,"s")
-        mm_strip(1,8)
-        inter_r(1,1,"v",256,512)
-        ev_b(1,5,"s")
-        ev_b(1,6,"s")
+        ev_b(1,1,"s")
+        tr_h(0,1,0)
+        tr_h(1,1,1)
         quant_h(0,0)
+        inter_r(1,1,"s",256,512)
+        tr_h(2,1,4)
         quant_h(1,0)
-        tr_h(0,1)
-        ev_b(1,7,"s")
+        mm_strip(1,8,2)
         quant_h(2,0)
-        tr_h(1,1)
-        quant_r(1,1)
-        tr_h(2,1)
-        rings["tp"], rings["acc"] = [], [6, 7, 3, 4, 5, 0, 1, 2]
-        cp_h(0,1,"s")
-        mm_m(0,0,0)
         inter_r(2,1,"v")
-        cp_h(1,1,"s")
-        mm_m(0,0,1)
-        cp_h(2,1,"s")
-        quant_w(0,0,256,512)
-        sig_m(0,0,0)
-        mm_strip(1,9)
-        quant_b(1,0,4)
-        sig_m(0,0,1)
+        ev_w(7,1,"s")
+        cp_h(0,1,"s")
+        mm_strip(1,9,3)
+        rings["tp"], rings["acc"] = [], [7, 5, 6, 0, 1, 4, 2, 3]
+        quant_r(1,1)
+        ev_b(1,2,"s")
         quant_r(2,1)
-        ev_b(1,8,"s")
-        mm_m(1,0,0)
+        cp_h(1,1,"s")
+        mm_m(0,0,0)
+        inter_b(0,1,"v",256,512)
+        ev_b(1,3,"s")
+        mm_m(0,0,1)
         quant_h(0,1)
+        cp_h(2,1,"s")
         quant_h(1,1)
-        ev_b(1,9,"s")
+        sig_m(0,0,0)
+        mm_m(1,0,0)
         quant_h(2,1)
+        quant_w(0,0)
+        sig_m(0,0,1)
         mm_m(1,0,1)
-        mul_a(0,0)
+        inter_b(1,1,"v")
+        ev_b(1,8,"s")
         sig_m(1,0,0)
         mm_m(0,1,0)
         sig_m(1,0,1)
-        inter_b(0,1,"v",0,256)
+        mul_a(0,0)
         mm_m(0,1,1)
-        inter_b(0,2,"s",0,256)
-        quant_a(0,0)
-        mul_a(1,0)
+        ev_b(1,9,"s")
         mm_m(1,1,0)
+        inter_b(0,2,"s",0,256)
+        quant_b(1,0,4)
+        quant_a(0,0)
         mm_m(1,1,1)
+        mul_a(1,0)
         sig_m(0,1,0)
-        quant_w(0,1,0,256)
-        quant_a(1,0)
-        sig_m(0,1,1)
-        mm_o(0,0,512)
-        inter_b(0,1,"v",256,512)
-        sig_m(1,1,0)
-        mm_o(1,0,512)
-        quant_b(1,4,4)
-        sig_m(1,1,1)
         mm_strip(1,10)
-        quant_w(0,1,256,512)
-        ev_o(0,0,512,"s")
+        sig_m(0,1,1)
+        quant_w(0,1)
+        sig_m(1,1,0)
+        quant_a(1,0)
+        mm_o(0,0,512)
+        quant_w(1,1)
+        sig_m(1,1,1)
+        mm_o(1,0,512)
         mul_a(0,1)
-        ev_o(1,0,512,"s")
+        ev_o(0,0,512,"s")
         mm_o(0,512,512)
-        ev_b(1,10,"s")
-        mul_a(1,1)
+        ev_o(1,0,512,"s")
         mm_o(1,512,512)
-        ev_o(0,512,512,"s")
+        mul_a(1,1)
+        ev_b(1,10,"s")
         mm_strip(1,11)
+        ev_o(0,512,512,"s")
         quant_a(0,1)
-        ev_o(1,512,512,"s")
         quant_b(1,8,2)
+        inter_b(0,2,"s",256,512)
         quant_a(1,1)
         mm_o(2,0,512)
-        inter_b(0,2,"v",256,512)
-        ev_b(1,11,"s")
+        ev_o(1,512,512,"v")
         mm_o(3,0,512)
-        quant_w(0,2,0,256)
-        ev_o(2,0,512,"s")
+        ev_b(1,11,"s")
+        ev_o(2,0,512,"v")
         mm_o(2,512,512)
-        quant_b(1,10,2)
-        quant_w(0,2,256,512)
         ev_o(3,0,512,"s")
+        quant_w(0,2)
         mm_o(3,512,512)
+        quant_b(1,10,2)
         mm_o(0,1024,512)
-        ev_o(2,512,512,"s")
-        ev_o(3,512,512,"v")
+        ev_o(2,512,512,"v")
+        ev_o(3,512,512,"s")
         mm_o(1,1024,512)
-        ev_o(0,1024,512,"s")
+        ev_o(0,1024,512,"v")
         mm_o(2,1024,512)
-        ev_o(1,1024,512,"v")
+        ev_o(1,1024,512,"s")
         mm_o(3,1024,256)
         mm_o(3,1280,256)
-        ev_o(2,1024,512,"s")
-        ev_o(3,1024,256,"v")
-        ev_o(3,1280,256,"s")
+        ev_o(2,1024,512,"v")
+        ev_o(3,1024,256,"s")
+        ev_o(3,1280,256,"v")

@@ -178,9 +178,9 @@ def tile_dpo_like_hidden_step_s11_kernel(tc, h, r, beta, p_chosen, p_rejected, u
                 x = work.tile([P, 2, V // 4, 2], BF16, name="diff", tag="diff", bufs=DIFF_BUFS, align_bytes=64)
                 diff[q] = x
             nc.vector.tensor_tensor(
-                out=diff[q][:, :, lo // 4 : hi // 4, :],
-                in0=pc[q][:, lo:hi].rearrange("p (w u e) -> p u w e", u=2, e=2),
-                in1=pr[q][:, lo:hi].rearrange("p (w u e) -> p u w e", u=2, e=2),
+                out=diff[q][:, :, lo // 4 : hi // 4, :].rearrange("p u w e -> p w u e"),
+                in0=pc[q][:, lo:hi].rearrange("p (w u e) -> p w u e", u=2, e=2),
+                in1=pr[q][:, lo:hi].rearrange("p (w u e) -> p w u e", u=2, e=2),
                 op=ALU.subtract,
             )
 

@@ -288,8 +288,8 @@ def tile_dpo_like_hidden_step_s11_kernel(tc, h, r, beta, p_chosen, p_rejected, u
                 rst[k, g] = stage()
             move(
                 eng,
-                rst[k, g][:].rearrange("p (t a b) j -> p a t b j", t=4, b=2)[:, lo // 8 : hi // 8, :, :, :],
-                rraw[k][:, :, g * 512 + lo : g * 512 + hi].rearrange("p j (a b t) -> p a t b j", t=4, b=2),
+                rst[k, g][:].rearrange("p (t a b) j -> p a j b t", t=4, b=2)[:, lo // 8 : hi // 8, :, :, :],
+                rraw[k][:, :, g * 512 + lo : g * 512 + hi].rearrange("p j (a b t) -> p a j b t", t=4, b=2),
             )
 
         def quant_r(k, g):
@@ -298,8 +298,8 @@ def tile_dpo_like_hidden_step_s11_kernel(tc, h, r, beta, p_chosen, p_rejected, u
         def re_h(b, eng):
             move(
                 eng,
-                hre[b][:],
-                hraw[b][:].rearrange("p i (w u e) -> p i u w e", u=2, e=2),
+                hre[b][:].rearrange("p i u w e -> p i w u e"),
+                hraw[b][:].rearrange("p i (w u e) -> p i w u e", u=2, e=2),
             )
 
         def tr_h(k, b, pool="tp"):

@@ -20,15 +20,15 @@ ALU = mybir.AluOpType
 NV = V // 512
 ND = D // 512
 NJ = J // 512
-NT = T // P
-NS = D // P
+FRONT = 1024
+ALL_V, FIRST_V, LAST_V = (0, 1, 2, 3), (0, 1), (2, 3)
 P_BUFS = 4
-STAGE_BUFS = 5
-BST_BUFS = 3
-OUT_BUFS = 4
-C_BUFS = 4
-R_BUFS = 3
 DIFF_BUFS = 3
+C_BUFS = 4
+STAGE_BUFS = 5
+HALF_BUFS = 3
+R_BUFS = 3
+OUT_BUFS = 4
 
 
 def tile_dpo_like_hidden_step_s11_kernel(tc, h, r, beta, p_chosen, p_rejected, ut_words, ut_scales, out):
@@ -43,36 +43,33 @@ def tile_dpo_like_hidden_step_s11_kernel(tc, h, r, beta, p_chosen, p_rejected, u
             x = keep.tile(shape, dtype, name=name, align_bytes=64)
             return x
 
-        ident = kept([P, P], F32, "ident")
-        beta_sb = kept([P, NJ, 4], BF16, "beta_sb")
-        usc = [kept([P, NV, 1024], U8, "usc0"), kept([P, NV, 512], U8, "usc1")]
-        ut = [kept([P, 2048], U8, "ut%d" % v) for v in range(NV)]
-        utc = kept([P, NV, 1024], U8, "utc")
-        braw = [kept([P, 4, D], BF16, "braw0"), kept([P, 4, 512], BF16, "braw1")]
-        bstage = kept([P, D, 4], BF16, "bstage")
-        wstage = kept([P, D, 4], BF16, "wstage")
-        hraw = [kept([P, 2, D], BF16, "hraw%d" % b) for b in range(2)]
-        hre = [kept([P, 2, 2, D // 4, 2], BF16, "hre%d" % b) for b in range(2)]
-        hcodes = [kept([P, T], U32, "hc%d" % k) for k in range(ND)]
-        hscales = [kept([P, T], U8, "hs%d" % k) for k in range(ND)]
-        rcodes = [kept([P, J], U32, "rc%d" % k) for k in range(ND)]
-        rscales = [kept([P, J], U8, "rs%d" % k) for k in range(ND)]
-        acodes = [kept([P, T], U32, "ac%d" % g) for g in range(NJ)]
-        ascales = [kept([P, T], U8, "as%d" % g) for g in range(NJ)]
-        bcodes = [kept([P, D], U32, "bc%d" % g) for g in range(NJ)]
-        bscales = [kept([P, D], U8, "bs%d" % g) for g in range(NJ)]
+        def streamed(shape, dtype, tag, bufs):
+            x = work.tile(shape, dtype, name=tag, tag=tag, bufs=bufs, align_bytes=64)
+            return x
 
-        rings = {"tp": [0, 1], "acc": [2, 3, 4, 5, 6, 7]}
-
-        def bank(pool, shape):
-            if isinstance(pool, int):
-                b = pool
-            else:
-                ring = rings[pool]
-                b = ring[0]
-                rings[pool] = ring[1:] + ring[:1]
+        def bank(b, shape):
             x = psum.tile(shape, F32, name="bank%d" % b, tag="bank%d" % b)
             return x
+
+        ident = kept([P, P], F32, "ident")
+        beta_sb = kept([P, NJ, 4], BF16, "beta_sb")
+        ut_sc = [kept([P, NV, FRONT], U8, "usc0"), kept([P, NV, D - FRONT], U8, "usc1")]
+        ut_front = [kept([P, 2 * FRONT], U8, "ut%d" % v) for v in range(NV)]
+        ut_back = kept([P, NV, 2 * (D - FRONT)], U8, "utc")
+        b_slots = [kept([P, 4, D], BF16, "braw0"), kept([P, 4, 512], BF16, "braw1")]
+        b_staged1 = kept([P, D, 4], BF16, "bstage")
+        b_staged0 = kept([P, D, 4], BF16, "wstage")
+        b_staged = [b_staged0, b_staged1]
+        h_rows = [kept([P, 2, D], BF16, "hraw%d" % b) for b in range(2)]
+        h_sorted = [kept([P, 2, 2, D // 4, 2], BF16, "hre%d" % b) for b in range(2)]
+        h_codes = [kept([P, T], U32, "hc%d" % k) for k in range(ND)]
+        h_scales = [kept([P, T], U8, "hs%d" % k) for k in range(ND)]
+        r_codes = [kept([P, J], U32, "rc%d" % k) for k in range(ND)]
+        r_scales = [kept([P, J], U8, "rs%d" % k) for k in range(ND)]
+        a_codes = [kept([P, T], U32, "ac%d" % g) for g in range(NJ)]
+        a_scales = [kept([P, T], U8, "as%d" % g) for g in range(NJ)]
+        b_codes = [kept([P, D], U32, "bc%d" % g) for g in range(NJ)]
+        b_scales = [kept([P, D], U8, "bs%d" % g) for g in range(NJ)]
 
         def move(eng, dst, src):
             if eng == "s":
@@ -80,612 +77,469 @@ def tile_dpo_like_hidden_step_s11_kernel(tc, h, r, beta, p_chosen, p_rejected, u
             else:
                 nc.vector.tensor_copy(out=dst, in_=src)
 
-        def quantize(codes, scales, lo, n, grouped):
-            nc.vector.quantize_mx(out=codes[:, lo : lo + n].bitcast(FP8X4), scales=scales[:, lo : lo + n], in_=grouped)
+        def quantize(codes, scales, cols, staged):
+            nc.vector.quantize_mx(out=codes[:, cols].bitcast(FP8X4), scales=scales[:, cols], in_=staged.rearrange("p c j -> p (c j)"))
 
-        def stage():
-            x = work.tile([P, 512, 4], BF16, name="stage", tag="stage", bufs=STAGE_BUFS, align_bytes=64)
-            return x
+        def mx_pass(dst, stationary, moving, first, last):
+            nc.tensor.matmul_mx(
+                out=dst, lhsT=stationary[0], lhsT_scale=stationary[1], rhs=moving[0], rhs_scale=moving[1], start=first, stop=last
+            )
 
-        def half_stage():
-            x = work.tile([P, 256, 4], BF16, name="bst", tag="bst", bufs=BST_BUFS, align_bytes=64)
-            return x
+        def fp8(codes, scales, lo, n):
+            return codes[:, lo : lo + n].bitcast(FP8X4), scales[:, lo : lo + n]
+
+        def span(half, width):
+            return slice(0, width) if half is None else slice(half * width // 2, (half + 1) * width // 2)
 
         warm = {}
 
         def warm_table():
-            x = half_stage()
+            x = streamed([P, 256, 4], BF16, "bst", HALF_BUFS)
             nc.scalar.activation(out=x[:, 0:1, 0:1], in_=ident[:, 0:1].unsqueeze(2), func=ACT.Sigmoid)
 
-        def warm_zero():
-            warm["in"] = stage()
-            nc.vector.memset(warm["in"][:].rearrange("p c j -> p (c j)").bitcast(I32), 0)
+        def warm_zeros():
+            warm["zeros"] = streamed([P, 512, 4], BF16, "stage", STAGE_BUFS)
+            nc.vector.memset(warm["zeros"][:].rearrange("p c j -> p (c j)").bitcast(I32), 0)
 
-        def warm_quant():
-            quantize(acodes[1], ascales[1], 0, 512, warm["in"][:].rearrange("p c j -> p (c j)"))
+        def warm_operand():
+            quantize(a_codes[1], a_scales[1], slice(0, T), warm["zeros"][:])
 
-        def warm_pe(n):
-            x = psum.tile([P, 512], F32, name="bank7", tag="bank7")
+        def warm_passes(n):
+            x = bank(7, [P, 512])
             for i in range(n):
-                nc.tensor.matmul_mx(
-                    out=x[:],
-                    lhsT=acodes[1][:, 0:P].bitcast(FP8X4),
-                    lhsT_scale=ascales[1][:, 0:P],
-                    rhs=acodes[1][:].bitcast(FP8X4),
-                    rhs_scale=ascales[1][:],
-                    start=True,
-                    stop=True,
-                )
+                mx_pass(x[:], fp8(a_codes[1], a_scales[1], 0, P), fp8(a_codes[1], a_scales[1], 0, T), True, True)
 
-        pc, pr = {}, {}
+        pc, pr, r_rows = {}, {}, {}
 
-        def load_p(q, lo=0, hi=V):
+        def tile_rows(src, q):
             g, t = divmod(q, 4)
-            if q not in pc:
-                a = work.tile([P, V], BF16, name="pc", tag="pc", bufs=P_BUFS, align_bytes=64)
-                b = work.tile([P, V], BF16, name="pr", tag="pr", bufs=P_BUFS, align_bytes=64)
-                pc[q], pr[q] = a, b
-            rows = slice(g * 512, (g + 1) * 512)
-            nc.sync.dma_start(out=pc[q][:, lo:hi], in_=p_chosen[rows, :].rearrange("(m t) v -> m t v", t=4)[:, t, lo:hi])
-            nc.sync.dma_start(out=pr[q][:, lo:hi], in_=p_rejected[rows, :].rearrange("(m t) v -> m t v", t=4)[:, t, lo:hi])
+            return src[g * 512 : (g + 1) * 512, :].rearrange("(m t) v -> m t v", t=4)[:, t, :]
 
-        def load_pc(q):
-            g, t = divmod(q, 4)
-            a = work.tile([P, V], BF16, name="pc", tag="pc", bufs=P_BUFS, align_bytes=64)
-            b = work.tile([P, V], BF16, name="pr", tag="pr", bufs=P_BUFS, align_bytes=64)
-            pc[q], pr[q] = a, b
-            nc.sync.dma_start(out=a[:], in_=p_chosen[g * 512 : (g + 1) * 512, :].rearrange("(m t) v -> m t v", t=4)[:, t, :])
+        def new_p(q):
+            pc[q] = streamed([P, V], BF16, "pc", P_BUFS)
+            pr[q] = streamed([P, V], BF16, "pr", P_BUFS)
 
-        def load_pr(q, lo, hi):
-            g, t = divmod(q, 4)
-            src = p_rejected[g * 512 : (g + 1) * 512, :].rearrange("(m t) v -> m t v", t=4)
-            nc.sync.dma_start(out=pr[q][:, lo:hi], in_=src[:, t, lo:hi])
+        def load_half(q, a):
+            if a == 0:
+                new_p(q)
+            cols = span(a, V)
+            nc.sync.dma_start(out=pc[q][:, cols], in_=tile_rows(p_chosen, q)[:, cols])
+            nc.sync.dma_start(out=pr[q][:, cols], in_=tile_rows(p_rejected, q)[:, cols])
 
-        def load_utv(v):
-            nc.sync.dma_start(out=ut[v][:].bitcast(I32), in_=ut_words[v, :, 0:2048].bitcast(I32))
+        def load_tile(q):
+            new_p(q)
+            nc.sync.dma_start(out=pc[q][:], in_=tile_rows(p_chosen, q))
+            for a in range(2):
+                nc.sync.dma_start(out=pr[q][:, span(a, V)], in_=tile_rows(p_rejected, q)[:, span(a, V)])
 
-        def load_utc():
-            nc.sync.dma_start(out=utc[:].bitcast(I32), in_=ut_words[:, :, 2048:3072].rearrange("g p n -> p g n").bitcast(I32))
+        def load_ut_front(v):
+            nc.sync.dma_start(out=ut_front[v][:].bitcast(I32), in_=ut_words[v, :, 0 : 2 * FRONT].bitcast(I32))
 
-        def zero_usc(a):
-            nc.vector.memset(usc[a][:].bitcast(I32), 0)
+        def load_ut_back():
+            src = ut_words[:, :, 2 * FRONT : 2 * D].rearrange("g p n -> p g n")
+            nc.sync.dma_start(out=ut_back[:].bitcast(I32), in_=src.bitcast(I32))
 
-        def load_usc(a):
-            for rr in range(4):
-                src = ut_scales[:, rr:16:4, 0:1024] if a == 0 else ut_scales[:, rr:16:4, 1024:D]
-                nc.sync.dma_start(out=usc[a][rr:P:32, :, :].bitcast(I32), in_=src.rearrange("g q n -> q g n").bitcast(I32))
+        def zero_scales(part):
+            nc.vector.memset(ut_sc[part][:].bitcast(I32), 0)
 
-        rraw = {}
+        def load_scales(part):
+            cols = (slice(0, FRONT), slice(FRONT, D))[part]
+            for i in range(4):
+                src = ut_scales[:, i:16:4, cols].rearrange("g q n -> q g n")
+                nc.sync.dma_start(out=ut_sc[part][i:P:32, :, :].bitcast(I32), in_=src.bitcast(I32))
 
-        def load_r(k, gs=(0, 1)):
-            if k not in rraw:
-                x = work.tile([P, 4, J], BF16, name="rraw", tag="rraw", bufs=R_BUFS, align_bytes=64)
-                rraw[k] = x
-            cols = slice(512 * gs[0], 512 * (gs[-1] + 1))
-            src = r[k * 512 : (k + 1) * 512, :].rearrange("(p j) c -> p j c", j=4)
-            nc.sync.dma_start(out=rraw[k][:, :, cols], in_=src[:, :, cols])
+        def load_r(k):
+            r_rows[k] = streamed([P, 4, J], BF16, "rraw", R_BUFS)
+            nc.sync.dma_start(out=r_rows[k][:], in_=r[k * 512 : (k + 1) * 512, :].rearrange("(p j) c -> p j c", j=4))
 
         def load_h(b):
-            nc.sync.dma_start(out=hraw[b][:], in_=h[256 * b : 256 * (b + 1), :].rearrange("(i p) k -> p i k", p=P))
+            nc.sync.dma_start(out=h_rows[b][:], in_=h[256 * b : 256 * (b + 1), :].rearrange("(i p) k -> p i k", p=P))
 
         def load_beta():
             nc.sync.dma_start(out=beta_sb[:], in_=beta.rearrange("(g p t) -> p g t", g=NJ, t=4))
 
-        diff, ct, cbank = {}, {}, {}
+        diff, c_turned, c_staged, c_codes, c_scales = {}, {}, {}, {}, {}
 
-        def sub(q, lo=0, hi=V):
-            if q not in diff:
-                x = work.tile([P, 2, V // 4, 2], BF16, name="diff", tag="diff", bufs=DIFF_BUFS, align_bytes=64)
-                diff[q] = x
+        def sub(q, a):
+            if a == 0:
+                diff[q] = streamed([P, 2, V // 4, 2], BF16, "diff", DIFF_BUFS)
             nc.vector.tensor_tensor(
-                out=diff[q][:, :, lo // 4 : hi // 4, :].rearrange("p u w e -> p w u e"),
-                in0=pc[q][:, lo:hi].rearrange("p (w u e) -> p w u e", u=2, e=2),
-                in1=pr[q][:, lo:hi].rearrange("p (w u e) -> p w u e", u=2, e=2),
+                out=diff[q][:, :, span(a, V // 4), :].rearrange("p u w e -> p w u e"),
+                in0=pc[q][:, span(a, V)].rearrange("p (w u e) -> p w u e", u=2, e=2),
+                in1=pr[q][:, span(a, V)].rearrange("p (w u e) -> p w u e", u=2, e=2),
                 op=ALU.subtract,
             )
 
-        def tr_c(q, b, pool="tp"):
+        def turn_c(q, a, b):
             words = diff[q][:].rearrange("p u w e -> p (u w e)").bitcast(F32)
-            x = bank(pool, [P, 2, 2, P])
-            for a in range(2):
+            c_turned[q, a] = bank(b, [P, 2, 2, P])
+            for i in range(2):
                 for u in range(2):
-                    lo = u * 512 + (2 * b + a) * P
-                    nc.tensor.transpose(x[:, a, u, :], words[:, lo : lo + P], ident[:])
-            cbank[q, b] = x
+                    lo = u * (V // 4) + (2 * a + i) * P
+                    nc.tensor.transpose(c_turned[q, a][:, i, u, :], words[:, lo : lo + P], ident[:])
 
-        def out_words(eng, dst, src):
+        def copy_words(dst, src):
             words = dst.rearrange("p c j -> p (c j)").bitcast(F32)
-            move(eng, words.rearrange("p (a r u) -> p a r u", a=2, u=2), src[:].rearrange("p a u r -> p a r u"))
+            move("s", words.rearrange("p (i r u) -> p i r u", i=2, u=2), src[:].rearrange("p i u r -> p i r u"))
 
-        def cp_c(q, b, eng):
-            if q not in ct:
-                ct[q] = stage()
-            out_words(eng, ct[q][:, 256 * b : 256 * (b + 1), :], cbank[q, b])
+        def stage_c(q, a):
+            if a == 0:
+                c_staged[q] = streamed([P, 512, 4], BF16, "stage", STAGE_BUFS)
+            copy_words(c_staged[q][:, span(a, 512), :], c_turned[q, a])
 
-        ccodes, cscales = {}, {}
+        def quant_c(q, a=None):
+            if q not in c_codes:
+                c_codes[q] = streamed([P, NV * P], U32, "cc", C_BUFS)
+                c_scales[q] = streamed([P, NV * P], U8, "cs", C_BUFS)
+            quantize(c_codes[q], c_scales[q], span(a, 512), c_staged[q][:, span(a, 512), :])
 
-        def quant_c(q, lo=0, hi=512):
-            if q not in ccodes:
-                x = work.tile([P, NV * P], U32, name="cc", tag="cc", bufs=C_BUFS, align_bytes=64)
-                y = work.tile([P, NV * P], U8, name="cs", tag="cs", bufs=C_BUFS, align_bytes=64)
-                ccodes[q], cscales[q] = x, y
-            quantize(ccodes[q], cscales[q], lo, hi - lo, ct[q][:, lo:hi, :].rearrange("p c j -> p (c j)"))
+        chunk_acc, strip_acc = {}, {}
 
-        bacc, bst = {}, {}
-
-        def pass_any(dst, q, v, lo, n):
-            if lo < 1024:
-                codes, scales = ut[v][:, 2 * lo : 2 * (lo + n)], usc[0][:, v, lo : lo + n]
+        def pass_b(dst, q, v, lo, n):
+            if lo < FRONT:
+                codes, scales = ut_front[v][:, 2 * lo : 2 * (lo + n)], ut_sc[0][:, v, lo : lo + n]
             else:
-                codes, scales = utc[:, v, 2 * (lo - 1024) : 2 * (lo - 1024 + n)], usc[1][:, v, lo - 1024 : lo - 1024 + n]
-            nc.tensor.matmul_mx(
-                out=dst,
-                lhsT=ccodes[q][:, v * P : (v + 1) * P].bitcast(FP8X4),
-                lhsT_scale=cscales[q][:, v * P : (v + 1) * P],
-                rhs=codes.bitcast(FP4X4),
-                rhs_scale=scales,
-                start=(v == 0),
-                stop=(v == NV - 1),
-            )
+                at = lo - FRONT
+                codes, scales = ut_back[:, v, 2 * at : 2 * (at + n)], ut_sc[1][:, v, at : at + n]
+            mx_pass(dst, fp8(c_codes[q], c_scales[q], v * P, P), (codes.bitcast(FP4X4), scales), v == 0, v == NV - 1)
 
-        def pass_b(g, s, t, v, pool="acc"):
-            if (g, s) not in bacc:
-                bacc[g, s] = bank(pool, [P, 4, P])
-            pass_any(bacc[g, s][:, t, :], 4 * g + t, v, s * P, P)
-
-        wacc = {}
-
-        def mm_w(q, c, vs=(0, 1, 2, 3), pool="acc"):
-            if (q, c) not in wacc:
-                wacc[q, c] = bank(pool, [P, 512])
+        def chunk(q, c, vs, b=None):
+            if vs[0] == 0:
+                chunk_acc[q, c] = bank(b, [P, 512])
             for v in vs:
-                pass_any(wacc[q, c][:], q, v, 512 * c, 512)
+                pass_b(chunk_acc[q, c][:], q, v, 512 * c, 512)
 
-        def ev_w(q, c, eng):
-            move(eng, braw[q // 4][:, q % 4, 512 * c : 512 * (c + 1)] if q < 4 else braw[1][:, q % 4, :], wacc[q, c][:])
+        def slots_of(g, c):
+            return b_slots[0][:, :, 512 * c : 512 * (c + 1)] if g == 0 else b_slots[1][:]
 
-        def inter_b(g, c, eng, lo=0, hi=512):
-            src = braw[g][:, :, 512 * c + lo : 512 * c + hi] if g == 0 else braw[1][:, :, lo:hi]
-            move(eng, (wstage, bstage)[g][:, 512 * c + lo : 512 * c + hi, :].rearrange("p (c i) t -> p c t i", i=4), src.rearrange("p t (c i) -> p c t i", i=4))
+        def copy_chunk(q, c, eng="s"):
+            move(eng, slots_of(q // 4, c)[:, q % 4, :], chunk_acc[q, c][:])
 
-        def quant_w(g, c, lo=0, hi=512):
-            quantize(bcodes[g], bscales[g], 512 * c + lo, hi - lo, (wstage, bstage)[g][:, 512 * c + lo : 512 * c + hi, :].rearrange("p c j -> p (c j)"))
+        def weave_b(g, c, eng, half=None):
+            dst = b_staged[g][:, 512 * c : 512 * (c + 1), :][:, span(half, 512), :]
+            src = slots_of(g, c)[:, :, span(half, 512)]
+            move(eng, dst.rearrange("p (c i) t -> p c t i", i=4), src.rearrange("p t (c i) -> p c t i", i=4))
 
-        def mm_ts(q, s, vs=(0, 1, 2, 3), pool="acc"):
-            g, t = divmod(q, 4)
-            for v in vs:
-                pass_b(g, s, t, v, pool)
+        def strip_slot(s, t, b=None):
+            if t == 0:
+                strip_acc[s] = late_bank([P, 4, P]) if b is None else bank(b, [P, 4, P])
+            for v in ALL_V:
+                pass_b(strip_acc[s][:, t, :], 4 + t, v, s * P, P)
 
-        def mm_tile(q, vs=(0, 1, 2, 3)):
-            g, t = divmod(q, 4)
-            for v in vs:
-                for s in range(4):
-                    pass_b(g, s, t, v, 2 + s)
-
-        def mm_strips(g, s0, n):
+        def strip(s, b=None):
             for t in range(4):
-                for v in range(NV):
-                    for s in range(s0, s0 + n):
-                        pass_b(g, s, t, v)
+                strip_slot(s, t, b)
 
-        def mm_strip(g, s, pool="acc"):
-            for t in range(4):
-                for v in range(NV):
-                    pass_b(g, s, t, v, pool)
+        def copy_strip(s):
+            dst = b_staged[1][:, s * P : (s + 1) * P, :].rearrange("p (c i) t -> p c t i", i=2)
+            move("s", dst, strip_acc[s][:].rearrange("p t (c i) -> p c t i", i=2))
 
-        def ev_b(g, s, eng):
-            dst = bstage[:, s * P : (s + 1) * P, :].rearrange("p (c i) t -> p c t i", i=2)
-            move(eng, dst, bacc[g, s][:].rearrange("p t (c i) -> p c t i", i=2))
+        def quant_b(g, lo, n):
+            quantize(b_codes[g], b_scales[g], slice(lo, lo + n), b_staged[g][:, lo : lo + n, :])
 
-        def quant_b(g, s, n):
-            src = bstage[:, s * P : (s + n) * P, :].rearrange("p c j -> p (c j)")
-            quantize(bcodes[g], bscales[g], s * P, n * P, src)
+        r_staged, h_turned, h_staged = {}, {}, {}
 
-        rst, hst, hbank = {}, {}, {}
-
-        def inter_r(k, g, eng, lo=0, hi=512):
-            if (k, g) not in rst:
-                rst[k, g] = stage()
-            move(
-                eng,
-                rst[k, g][:].rearrange("p (t a b) j -> p a j b t", t=4, b=2)[:, lo // 8 : hi // 8, :, :, :],
-                rraw[k][:, :, g * 512 + lo : g * 512 + hi].rearrange("p j (a b t) -> p a j b t", t=4, b=2),
-            )
+        def weave_r(k, g, eng, half=None):
+            if (k, g) not in r_staged:
+                r_staged[k, g] = streamed([P, 512, 4], BF16, "stage", STAGE_BUFS)
+            dst = r_staged[k, g][:].rearrange("p (t a b) j -> p a j b t", t=4, b=2)
+            src = r_rows[k][:, :, g * 512 : (g + 1) * 512][:, :, span(half, 512)]
+            move(eng, dst[:, span(half, 64), :, :, :], src.rearrange("p j (a b t) -> p a j b t", t=4, b=2))
 
         def quant_r(k, g):
-            quantize(rcodes[k], rscales[k], g * 512, 512, rst[k, g][:].rearrange("p c j -> p (c j)"))
+            quantize(r_codes[k], r_scales[k], slice(g * 512, (g + 1) * 512), r_staged[k, g][:])
 
-        def re_h(b, eng):
-            move(
-                eng,
-                hre[b][:].rearrange("p i u w e -> p i w u e"),
-                hraw[b][:].rearrange("p i (w u e) -> p i w u e", u=2, e=2),
-            )
+        def sort_h(b):
+            dst = h_sorted[b][:].rearrange("p i u w e -> p i w u e")
+            move("v", dst, h_rows[b][:].rearrange("p i (w u e) -> p i w u e", u=2, e=2))
 
-        def tr_h(k, b, pool="tp"):
-            x = bank(pool, [P, 2, 2, P])
-            for a in range(2):
-                words = hre[b][:, a, :, :, :].rearrange("p u w e -> p (u w e)").bitcast(F32)
-                for u in range(2):
-                    lo = u * (D // 4) + P * k
-                    nc.tensor.transpose(x[:, a, u, :], words[:, lo : lo + P], ident[:])
-            hbank[k, b] = x
+        def turn_h(b, banks):
+            for k in range(ND):
+                h_turned[k, b] = bank(banks[k], [P, 2, 2, P])
+                for i in range(2):
+                    words = h_sorted[b][:, i, :, :, :].rearrange("p u w e -> p (u w e)").bitcast(F32)
+                    for u in range(2):
+                        lo = u * (D // 4) + P * k
+                        nc.tensor.transpose(h_turned[k, b][:, i, u, :], words[:, lo : lo + P], ident[:])
 
-        def cp_h(k, b, eng):
-            hst[k, b] = half_stage()
-            out_words(eng, hst[k, b][:], hbank[k, b])
+        def stage_h(k, b):
+            h_staged[k, b] = streamed([P, 256, 4], BF16, "bst", HALF_BUFS)
+            copy_words(h_staged[k, b][:], h_turned[k, b])
 
         def quant_h(k, b):
-            quantize(hcodes[k], hscales[k], 256 * b, 256, hst[k, b][:].rearrange("p c j -> p (c j)"))
+            quantize(h_codes[k], h_scales[k], span(b, T), h_staged[k, b][:])
 
-        macc, sig, ast = {}, {}, {}
+        m_acc, sig, a_staged = {}, {}, {}
+        late_banks = (7, 5, 6, 0, 1, 4, 2, 3)
+        late_sums = []
 
-        def mm_m(g, b, w, pool="acc"):
-            x = bank(pool, [P, 2, 256])
-            toks = slice(256 * b, 256 * (b + 1))
+        def late_bank(shape):
+            late_sums.append(shape)
+            return bank(late_banks[(len(late_sums) - 1) % 8], shape)
+
+        def margins(g, b, w):
+            m_acc[g, b, w] = late_bank([P, 2, 256])
             for e in range(2):
-                lo = g * 512 + (2 * w + e) * P
                 for k in range(ND):
-                    nc.tensor.matmul_mx(
-                        out=x[:, e, :],
-                        lhsT=rcodes[k][:, lo : lo + P].bitcast(FP8X4),
-                        lhsT_scale=rscales[k][:, lo : lo + P],
-                        rhs=hcodes[k][:, toks].bitcast(FP8X4),
-                        rhs_scale=hscales[k][:, toks],
-                        start=(k == 0),
-                        stop=(k == ND - 1),
-                    )
-            macc[g, b, w] = x
+                    stationary = fp8(r_codes[k], r_scales[k], g * 512 + (2 * w + e) * P, P)
+                    mx_pass(m_acc[g, b, w][:, e, :], stationary, fp8(h_codes[k], h_scales[k], 256 * b, 256), k == 0, k == ND - 1)
 
-        def sig_m(g, b, w):
-            if (g, b) not in sig:
-                x = work.tile([P, 2, 256, 2], F32, name="sig", tag="pc", bufs=P_BUFS, align_bytes=64)
-                sig[g, b] = x
-            nc.scalar.activation(out=sig[g, b][:, w, :, :], in_=macc[g, b, w][:].rearrange("p e n -> p n e"), func=ACT.Sigmoid)
+        def sigmoid(g, b, w):
+            if w == 0:
+                sig[g, b] = streamed([P, 2, 256, 2], F32, "pc", P_BUFS)
+            nc.scalar.activation(out=sig[g, b][:, w, :, :], in_=m_acc[g, b, w][:].rearrange("p e n -> p n e"), func=ACT.Sigmoid)
 
-        def mul_a(g, b):
-            ast[g, b] = half_stage()
+        def times_beta(g, b):
+            a_staged[g, b] = streamed([P, 256, 4], BF16, "bst", HALF_BUFS)
             nc.vector.tensor_tensor(
-                out=ast[g, b][:].rearrange("p n (w e) -> p n w e", w=2),
+                out=a_staged[g, b][:].rearrange("p n (w e) -> p n w e", w=2),
                 in0=sig[g, b][:].rearrange("p w n e -> p n w e"),
                 in1=beta_sb[:, g : g + 1, :].to_broadcast([P, 256, 4]).rearrange("p n (w e) -> p n w e", w=2),
                 op=ALU.mult,
             )
 
         def quant_a(g, b):
-            src = ast[g, b][:].rearrange("p c j -> p (c j)")
-            quantize(acodes[g], ascales[g], 256 * b, 256, src)
+            quantize(a_codes[g], a_scales[g], span(b, T), a_staged[g, b][:])
 
-        oacc, stores = {}, []
+        o_acc, stores = {}, []
 
-        def mm_o(i, c0, w, pool="acc", groups=(0, 1)):
-            if (i, c0) not in oacc:
-                oacc[i, c0] = bank(pool, [P, 512])
-            x = oacc[i, c0]
-            rows, cols = slice(i * P, (i + 1) * P), slice(c0, c0 + w)
-            for g in groups:
-                nc.tensor.matmul_mx(
-                    out=x[:, 0:w],
-                    lhsT=acodes[g][:, rows].bitcast(FP8X4),
-                    lhsT_scale=ascales[g][:, rows],
-                    rhs=bcodes[g][:, cols].bitcast(FP8X4),
-                    rhs_scale=bscales[g][:, cols],
-                    start=(g == 0),
-                    stop=(g == NJ - 1),
-                )
-
-        def out_tile(shape):
-            stores.append(shape)
-            if len(stores) % 3 == 1:
-                x = work.tile(shape, F32, name="osb", tag="osb", bufs=OUT_BUFS, align_bytes=64)
-            elif len(stores) % 3 == 2:
-                x = work.tile(shape, F32, name="osb", tag="diff", bufs=DIFF_BUFS, align_bytes=64)
-            else:
-                x = work.tile(shape, F32, name="osb", tag="pr", bufs=P_BUFS, align_bytes=64)
-            return x
-
-        def ev_o(i, c0, w, eng):
-            x = out_tile([P, 512])
-            move(eng, x[:, 0:w], oacc[i, c0][:, 0:w])
-            nc.sync.dma_start(out=out[i * P : (i + 1) * P, c0 : c0 + w], in_=x[:, 0:w])
-
-        def mm_o2(i0, c0, pool="acc"):
-            x = bank(pool, [P, 2, 256])
-            cols = slice(c0, c0 + 256)
-            for a in range(2):
-                rows = slice((i0 + a) * P, (i0 + a + 1) * P)
+        def result(i, c0, n, tiles=1):
+            o_acc[i, c0] = late_bank([P, 512])
+            for a in range(tiles):
                 for g in range(NJ):
-                    nc.tensor.matmul_mx(
-                        out=x[:, a, :],
-                        lhsT=acodes[g][:, rows].bitcast(FP8X4),
-                        lhsT_scale=ascales[g][:, rows],
-                        rhs=bcodes[g][:, cols].bitcast(FP8X4),
-                        rhs_scale=bscales[g][:, cols],
-                        start=(g == 0),
-                        stop=(g == NJ - 1),
-                    )
-            oacc[i0, c0] = x
+                    stationary = fp8(a_codes[g], a_scales[g], (i + a) * P, P)
+                    mx_pass(o_acc[i, c0][:, a * n : (a + 1) * n], stationary, fp8(b_codes[g], b_scales[g], c0, n), g == 0, g == NJ - 1)
 
-        def ev_o2(i0, c0, eng):
-            x = out_tile([P, 2, 256])
-            move(eng, x[:], oacc[i0, c0][:])
-            dst = out[i0 * P : (i0 + 2) * P, c0 : c0 + 256].rearrange("(a p) c -> p a c", a=2)
-            nc.sync.dma_start(out=dst, in_=x[:])
+        def store(i, c0, n, eng, tiles=1):
+            tag, bufs = (("osb", OUT_BUFS), ("diff", DIFF_BUFS), ("pr", P_BUFS))[len(stores) % 3]
+            stores.append(tag)
+            x = streamed([P, 512], F32, tag, bufs)
+            move(eng, x[:, 0 : tiles * n], o_acc[i, c0][:, 0 : tiles * n])
+            dst = out[i * P : (i + tiles) * P, c0 : c0 + n].rearrange("(a p) c -> p a c", a=tiles)
+            nc.sync.dma_start(out=dst, in_=x[:, 0 : tiles * n].rearrange("p (a c) -> p a c", a=tiles))
 
         make_identity(nc, ident[:])
-        load_p(0,0,1024)
-        zero_usc(0)
-        load_p(1,0,1024)
+        load_half(0, 0)
+        load_half(1, 0)
+        zero_scales(0)
         warm_table()
-        warm_zero()
-        load_usc(0)
-        zero_usc(1)
-        load_utv(0)
-        load_p(2,0,1024)
-        sub(0,0,1024)
-        warm_quant()
-        tr_c(0,0)
-        load_utv(1)
-        sub(1,0,1024)
-        warm_pe(2)
-        load_p(0,1024,2048)
-        cp_c(0,0,"s")
-        quant_c(0,0,256)
-        tr_c(1,0)
-        load_p(1,1024,2048)
-        warm_pe(1)
-        cp_c(1,0,"s")
-        mm_w(0,0,(0,))
-        load_utv(2)
-        mm_w(0,1,(0,))
-        quant_c(1,0,256)
-        load_p(2,1024,2048)
-        mm_w(1,0,(0,))
-        sub(2,0,1024)
-        mm_w(1,1,(0,))
-        load_utv(3)
-        tr_c(2,0)
-        mm_w(0,0,(1,))
-        load_utc()
-        mm_w(0,1,(1,))
-        cp_c(2,0,"s")
-        mm_w(1,0,(1,))
-        load_usc(1)
-        sub(0,1024,2048)
-        mm_w(1,1,(1,))
-        quant_c(2,0,256)
-        tr_c(0,1)
-        mm_w(2,0,(0,))
-        sub(1,1024,2048)
-        mm_w(2,1,(0,))
-        cp_c(0,1,"s")
-        tr_c(1,1)
-        quant_c(0,256,512)
-        mm_w(2,0,(1,))
-        load_pc(3)
-        mm_w(2,1,(1,))
-        cp_c(1,1,"s")
-        mm_w(0,0,(2,))
-        load_pr(3,0,1024)
-        sub(2,1024,2048)
-        mm_w(0,1,(2,))
-        quant_c(1,256,512)
-        load_pr(3,1024,2048)
-        tr_c(2,1)
-        mm_w(1,0,(2,))
-        mm_w(1,1,(2,))
-        cp_c(2,1,"s")
-        mm_w(0,0,(3,))
-        mm_w(0,1,(3,))
+        warm_zeros()
+        load_scales(0)
+        zero_scales(1)
+        load_ut_front(0)
+        load_half(2, 0)
+        load_ut_front(1)
+        load_half(0, 1)
+        load_half(1, 1)
+        load_ut_front(2)
+        load_half(2, 1)
+        load_ut_front(3)
+        load_ut_back()
+        load_scales(1)
+        load_tile(3)
         load_r(0)
-        quant_c(2,256,512)
-        load_pc(4)
-        mm_w(1,0,(3,))
-        ev_w(0,0,"s")
-        load_pr(4,0,1024)
-        mm_w(1,1,(3,))
-        load_pr(4,1024,2048)
-        ev_w(0,1,"v")
-        mm_w(2,0,(2,3))
-        load_pc(5)
-        ev_w(1,0,"s")
-        ev_w(1,1,"v")
-        mm_w(2,1,(2,3))
-        ev_w(2,0,"s")
-        mm_w(0,2,(0,1,2,3),2)
-        load_pr(5,0,1024)
-        ev_w(2,1,"s")
-        load_pr(5,1024,2048)
-        sub(3,0,1024)
-        mm_w(1,2,(0,1,2,3),3)
-        load_pc(6)
-        sub(3,1024,2048)
-        ev_w(0,2,"s")
-        tr_c(3,0)
-        tr_c(3,1)
-        mm_w(2,2,(0,1,2,3),4)
-        cp_c(3,0,"s")
-        load_pr(6,0,1024)
-        cp_c(3,1,"s")
-        quant_c(3,0,256)
-        inter_r(0,0,"v",0,256)
-        ev_w(1,2,"s")
-        mm_w(3,0,(0,1),5)
-        load_pr(6,1024,2048)
-        ev_w(2,2,"s")
-        mm_w(3,1,(0,1),6)
-        quant_c(3,256,512)
-        mm_w(3,2,(0,1),7)
+
+        def front(q, vs):
+            for c in range(2):
+                chunk(q, c, vs, 2 + 2 * q + c)
+
+        def turn_half(q, a):
+            sub(q, a)
+            turn_c(q, a, (q + a) % 2)
+
+        turn_half(0, 0)
+        warm_operand()
+        warm_passes(2)
+        stage_c(0, 0)
+        turn_half(1, 0)
+        warm_passes(1)
+        stage_c(1, 0)
+        for q in range(2):
+            quant_c(q, 0)
+            front(q, (0,))
+        turn_half(2, 0)
+        stage_c(2, 0)
+        for q in range(2):
+            front(q, (1,))
+        turn_half(0, 1)
+        load_tile(4)
+        quant_c(2, 0)
+        stage_c(0, 1)
+        front(2, (0,))
+        turn_half(1, 1)
+        load_tile(5)
+        stage_c(1, 1)
+        front(2, (1,))
+        quant_c(0, 1)
+        front(0, (2,))
+        turn_half(2, 1)
+        load_tile(6)
+        stage_c(2, 1)
+        quant_c(1, 1)
+        front(1, (2,))
+        for q in range(2):
+            front(q, (3,))
+        quant_c(2, 1)
+        front(2, LAST_V)
+        for q in range(2):
+            copy_chunk(q, 0)
+            copy_chunk(q, 1, "v")
+
+        def sub_tile(q):
+            for a in range(2):
+                sub(q, a)
+
+        def turn_tile(q):
+            for a in range(2):
+                turn_c(q, a, a)
+
+        def stage_tile(q):
+            for a in range(2):
+                stage_c(q, a)
+
+        chunk(0, 2, ALL_V, 2)
+        for c in range(2):
+            copy_chunk(2, c)
+        chunk(1, 2, FIRST_V, 3)
+        sub_tile(3)
+        load_tile(7)
         load_h(0)
-        sub(4,0,1024)
-        mm_w(3,0,(2,3))
-        load_pc(7)
-        sub(4,1024,2048)
-        tr_c(4,0)
-        inter_r(0,0,"v",256,512)
-        ev_w(3,0,"s")
-        tr_c(4,1)
-        load_pr(7,0,1024)
-        mm_w(3,1,(2,3))
-        cp_c(4,0,"s")
-        load_pr(7,1024,2048)
-        sub(5,0,1024)
-        mm_w(3,2,(2,3))
-        cp_c(4,1,"s")
         load_r(1)
-        sub(5,1024,2048)
-        tr_c(5,0)
-        ev_w(3,1,"s")
-        quant_c(4,0,256)
-        tr_c(5,1)
-        ev_w(3,2,"s")
-        quant_c(4,256,512)
-        mm_w(4,1,(0,1,2,3),4)
-        load_r(2)
-        inter_r(0,1,"v",0,256)
-        cp_c(5,0,"s")
         load_h(1)
-        cp_c(5,1,"s")
-        sub(6,0,1024)
-        mm_ts(4,0,(0,1,2,3),2)
+        load_r(2)
         load_beta()
-        inter_b(0,0,"s",0,256)
-        sub(6,1024,2048)
-        mm_ts(4,1,(0,1,2,3),3)
-        mm_ts(4,2,(0,1,2,3),5)
+        copy_chunk(0, 2)
+        turn_tile(3)
+        stage_tile(3)
+        chunk(1, 2, LAST_V)
+        chunk(2, 2, ALL_V, 4)
+        quant_c(3, 0)
+        weave_r(0, 0, "v", 0)
+        quant_c(3, 1)
+        for c in range(ND):
+            chunk(3, c, FIRST_V, 5 + c)
+        copy_chunk(1, 2)
+        copy_chunk(2, 2)
+        weave_r(0, 1, "s", 0)
+        chunk(3, 0, LAST_V)
+        sub_tile(4)
+        weave_r(0, 0, "v", 1)
+        turn_tile(4)
+        copy_chunk(3, 0)
+        stage_tile(4)
+        for c in range(1, ND):
+            chunk(3, c, LAST_V)
+            copy_chunk(3, c)
+
+        def passes_of(q):
+            chunk(q, 1, ALL_V, (4, 7)[q % 2])
+            for s in range(4):
+                strip_slot(s, q - 4, (2, 3, 5, 6)[s])
+
+        sub_tile(5)
+        turn_tile(5)
+        stage_tile(5)
+        for a in range(2):
+            quant_c(4, a)
+        passes_of(4)
+        weave_r(0, 1, "v", 1)
+        weave_b(0, 0, "s", 0)
+        copy_chunk(4, 1)
+        sub_tile(6)
+        turn_tile(6)
+        stage_tile(6)
         quant_c(5)
-        mm_ts(4,3,(0,1,2,3),6)
-        tr_c(6,0)
-        inter_r(0,1,"v",256,512)
-        ev_w(4,1,"s")
-        tr_c(6,1)
-        mm_w(5,1,(0,1,2,3),7)
-        re_h(0,"v")
-        cp_c(6,0,"s")
-        cp_c(6,1,"s")
-        quant_r(0,0)
-        mm_tile(5)
-        inter_b(0,0,"s",256,512)
-        sub(7,0,1024)
-        sub(7,1024,2048)
-        tr_c(7,0)
-        ev_w(5,1,"s")
-        quant_c(6,0,256)
-        tr_c(7,1)
-        quant_c(6,256,512)
-        mm_w(6,1,(0,1,2,3),4)
-        quant_r(0,1)
-        cp_c(7,0,"s")
-        cp_c(7,1,"s")
-        inter_b(0,1,"v",0,256)
-        mm_tile(6)
-        inter_r(1,0,"v")
-        ev_w(6,1,"s")
-        inter_r(1,1,"s",0,256)
-        tr_h(0,0,0)
+        passes_of(5)
+        for g in range(NJ):
+            quant_r(0, g)
+        weave_b(0, 0, "s", 1)
+        copy_chunk(5, 1)
+        sub_tile(7)
+        turn_tile(7)
+        stage_tile(7)
+        quant_c(6)
+        passes_of(6)
+        copy_chunk(6, 1)
+        sort_h(0)
+        weave_b(0, 1, "v")
+        weave_r(1, 0, "v", 0)
         quant_c(7)
-        tr_h(1,0,1)
-        tr_h(2,0,4)
-        inter_r(2,0,"v")
-        cp_h(0,0,"s")
-        mm_w(7,1,(0,1,2,3),7)
-        cp_h(1,0,"s")
-        quant_r(1,0)
-        cp_h(2,0,"s")
-        mm_ts(7,0)
-        mm_ts(7,1)
-        re_h(1,"v")
-        mm_ts(7,2)
-        ev_b(1,0,"s")
-        mm_ts(7,3)
-        quant_r(2,0)
-        ev_b(1,1,"s")
-        tr_h(0,1,0)
-        tr_h(1,1,1)
-        quant_h(0,0)
-        inter_r(1,1,"s",256,512)
-        tr_h(2,1,4)
-        quant_h(1,0)
-        mm_strip(1,8,2)
-        quant_h(2,0)
-        inter_r(2,1,"v")
-        ev_w(7,1,"s")
-        cp_h(0,1,"s")
-        mm_strip(1,9,3)
-        rings["tp"], rings["acc"] = [], [7, 5, 6, 0, 1, 4, 2, 3]
-        quant_r(1,1)
-        ev_b(1,2,"s")
-        quant_r(2,1)
-        cp_h(1,1,"s")
-        mm_m(0,0,0)
-        inter_b(0,1,"v",256,512)
-        ev_b(1,3,"s")
-        mm_m(0,0,1)
-        quant_h(0,1)
-        cp_h(2,1,"s")
-        quant_h(1,1)
-        sig_m(0,0,0)
-        mm_m(1,0,0)
-        quant_h(2,1)
-        quant_w(0,0)
-        sig_m(0,0,1)
-        mm_m(1,0,1)
-        inter_b(1,1,"v")
-        ev_b(1,8,"s")
-        sig_m(1,0,0)
-        mm_m(0,1,0)
-        sig_m(1,0,1)
-        mul_a(0,0)
-        mm_m(0,1,1)
-        ev_b(1,9,"s")
-        mm_m(1,1,0)
-        inter_b(0,2,"s",0,256)
-        quant_b(1,0,4)
-        quant_a(0,0)
-        mm_m(1,1,1)
-        mul_a(1,0)
-        sig_m(0,1,0)
-        mm_strip(1,10)
-        sig_m(0,1,1)
-        quant_w(0,1)
-        sig_m(1,1,0)
-        quant_a(1,0)
-        mm_o(0,0,512)
-        quant_w(1,1)
-        sig_m(1,1,1)
-        mm_o(1,0,512)
-        mul_a(0,1)
-        ev_o(0,0,512,"s")
-        mm_o(0,512,512)
-        ev_o(1,0,512,"s")
-        mm_o(1,512,512)
-        mul_a(1,1)
-        ev_b(1,10,"s")
-        mm_strip(1,11)
-        ev_o(0,512,512,"s")
-        quant_a(0,1)
-        quant_b(1,8,2)
-        inter_b(0,2,"s",256,512)
-        quant_a(1,1)
-        mm_o(2,0,512)
-        ev_o(1,512,512,"v")
-        mm_o(3,0,512)
-        ev_b(1,11,"s")
-        ev_o(2,0,512,"v")
-        mm_o(2,512,512)
-        ev_o(3,0,512,"s")
-        quant_w(0,2)
-        mm_o(3,512,512)
-        quant_b(1,10,2)
-        mm_o(0,1024,512)
-        ev_o(2,512,512,"v")
-        ev_o(3,512,512,"s")
-        mm_o(1,1024,512)
-        ev_o(0,1024,512,"v")
-        mm_o(2,1024,512)
-        ev_o(1,1024,512,"s")
-        mm_o(3,1024,256)
-        mm_o(3,1280,256)
-        ev_o(2,1024,512,"v")
-        ev_o(3,1024,256,"s")
-        ev_o(3,1280,256,"v")
+        weave_r(1, 1, "s", 0)
+        weave_r(1, 0, "v", 1)
+
+        h_banks = (0, 1, 4)
+        turn_h(0, h_banks)
+        passes_of(7)
+        for k in range(ND):
+            stage_h(k, 0)
+        sort_h(1)
+        turn_h(1, h_banks)
+        quant_r(1, 0)
+        quant_b(0, 0, 512)
+        weave_r(2, 0, "v")
+        for s in range(2):
+            copy_strip(s)
+        weave_r(1, 1, "s", 1)
+        copy_chunk(7, 1)
+        strip(8, 2)
+        strip(9, 3)
+        for k in range(ND):
+            quant_h(k, 0)
+        quant_r(2, 0)
+        weave_r(2, 1, "v")
+        for k in range(1, ND):
+            quant_r(k, 1)
+        for k in range(ND):
+            stage_h(k, 1)
+            if k < 2:
+                copy_strip(2 + k)
+            quant_h(k, 1)
+
+        for g in range(NJ):
+            for w in range(2):
+                margins(g, 0, w)
+                sigmoid(g, 0, w)
+            copy_strip(8 + g)
+        weave_b(1, 1, "v")
+        quant_b(0, 512, 512)
+        times_beta(0, 0)
+        quant_b(1, 0, 512)
+        quant_a(0, 0)
+        times_beta(1, 0)
+        quant_b(1, 512, 512)
+        quant_a(1, 0)
+        weave_b(0, 2, "s", 0)
+        for g in range(NJ):
+            for w in range(2):
+                margins(g, 1, w)
+                sigmoid(g, 1, w)
+
+        strip(10)
+        times_beta(0, 1)
+        quant_b(1, 1024, 256)
+        quant_b(0, 1024, 256)
+        times_beta(1, 1)
+        quant_a(0, 1)
+        for c0, i, eng in ((0, 0, "s"), (0, 1, "s"), (512, 0, "s"), (512, 1, "v")):
+            result(i, c0, 512)
+            store(i, c0, 512, eng)
+        result(0, 1024, 256, 2)
+        copy_strip(10)
+        store(0, 1024, 256, "s", 2)
+        strip(11)
+        copy_strip(11)
+        quant_a(1, 1)
+        weave_b(0, 2, "v", 1)
+        quant_b(1, 1280, P)
+        quant_b(0, 1280, 256)
+        quant_b(1, 1408, P)
+        for c0, i, eng in ((0, 2, "s"), (0, 3, "s"), (512, 2, "v"), (512, 3, "s")):
+            result(i, c0, 512)
+            store(i, c0, 512, eng)
+        result(0, 1280, 256, 2)
+        store(0, 1280, 256, "v", 2)
+        result(2, 1024, 512)
+        store(2, 1024, 512, "s")
+        for c0, eng in ((1024, "v"), (1280, "s")):
+            result(3, c0, 256)
+            store(3, c0, 256, eng)

@@ -39,12 +39,12 @@ def tile_dpo_like_hidden_step_s11_kernel(tc, h, r, beta, p_chosen, p_rejected, u
         psum = ctx.enter_context(tc.psum_pool(name="psum", bufs=1))
         ctx.enter_context(tc.manual_schedule())
 
-        def kept(shape, dtype, name):
-            x = keep.tile(shape, dtype, name=name, align_bytes=64)
+        def kept(shape, dtype, name, align=64):
+            x = keep.tile(shape, dtype, name=name, align_bytes=align)
             return x
 
-        def streamed(shape, dtype, tag, bufs):
-            x = work.tile(shape, dtype, name=tag, tag=tag, bufs=bufs, align_bytes=64)
+        def streamed(shape, dtype, tag, bufs, align=64):
+            x = work.tile(shape, dtype, name=tag, tag=tag, bufs=bufs, align_bytes=align)
             return x
 
         def bank(b, shape):
@@ -53,7 +53,7 @@ def tile_dpo_like_hidden_step_s11_kernel(tc, h, r, beta, p_chosen, p_rejected, u
 
         ident = kept([P, P], F32, "ident")
         beta_sb = kept([P, NJ, 4], BF16, "beta_sb")
-        ut_sc = [kept([P, NV, FRONT], U8, "usc0"), kept([P, NV, D - FRONT], U8, "usc1")]
+        ut_sc = [kept([P, NV, FRONT], U8, "usc0", 256), kept([P, NV, D - FRONT], U8, "usc1")]
         ut_front = [kept([P, 2 * FRONT], U8, "ut%d" % v) for v in range(NV)]
         ut_back = kept([P, NV, 2 * (D - FRONT)], U8, "utc")
         b_slots = [kept([P, 4, D], BF16, "braw0"), kept([P, 4, 512], BF16, "braw1")]
@@ -189,8 +189,8 @@ def tile_dpo_like_hidden_step_s11_kernel(tc, h, r, beta, p_chosen, p_rejected, u
 
         def quant_c(q, a=None):
             if q not in c_codes:
-                c_codes[q] = streamed([P, NV * P], U32, "cc", C_BUFS)
-                c_scales[q] = streamed([P, NV * P], U8, "cs", C_BUFS)
+                c_codes[q] = streamed([P, NV * P], U32, "cc", C_BUFS, 256)
+                c_scales[q] = streamed([P, NV * P], U8, "cs", C_BUFS, 256)
             quantize(c_codes[q], c_scales[q], span(a, 512), c_staged[q][:, span(a, 512), :])
 
         chunk_acc, strip_acc = {}, {}
@@ -506,8 +506,9 @@ def tile_dpo_like_hidden_step_s11_kernel(tc, h, r, beta, p_chosen, p_rejected, u
         quant_b(1, 0, 512)
         quant_a(0, 0)
         times_beta(1, 0)
-        quant_b(1, 512, 512)
+        quant_b(1, 512, 256)
         quant_a(1, 0)
+        quant_b(1, 768, 256)
         weave_b(0, 2, "s", 0)
         for g in range(NJ):
             for w in range(2):

@@ -20,14 +20,13 @@ ALU = mybir.AluOpType
 NV = V // 512
 ND = D // 512
 NJ = J // 512
-FRONT = 1024
-ALL_V, FIRST_V, LAST_V = (0, 1, 2, 3), (0, 1), (2, 3)
-P_BUFS = 4
-DIFF_BUFS = 3
-C_BUFS = 4
-STAGE_BUFS = 5
+W = 256
+NB = D // W
+P_BUFS = 3
+PIECE_BUFS = 3
+C_BUFS = 3
+STAGE_BUFS = 3
 HALF_BUFS = 3
-R_BUFS = 3
 OUT_BUFS = 4
 
 
@@ -53,15 +52,11 @@ def tile_dpo_like_hidden_step_s11_kernel(tc, h, r, beta, p_chosen, p_rejected, u
 
         ident = kept([P, P], F32, "ident")
         beta_sb = kept([P, NJ, 4], BF16, "beta_sb")
-        ut_sc = [kept([P, NV, FRONT], U8, "usc0", 256), kept([P, NV, D - FRONT], U8, "usc1")]
-        ut_front = [kept([P, 2 * FRONT], U8, "ut%d" % v) for v in range(NV)]
-        ut_back = kept([P, NV, 2 * (D - FRONT)], U8, "utc")
-        b_slots = [kept([P, 4, D], BF16, "braw0"), kept([P, 4, 512], BF16, "braw1")]
-        b_staged1 = kept([P, D, 4], BF16, "bstage")
-        b_staged0 = kept([P, D, 4], BF16, "wstage")
-        b_staged = [b_staged0, b_staged1]
+        ut_sc = kept([P, NV, D], U8, "usc", 256)
+        ut_codes = [kept([P, 2 * D], U8, "ut%d" % v) for v in range(NV)]
+        b_pairs = [kept([P, 2, D, 2], BF16, "bp%d" % g) for g in range(NJ)]
+        r_rows = [kept([P, 4, J], BF16, "rraw%d" % k) for k in range(ND)]
         h_rows = [kept([P, 2, D], BF16, "hraw%d" % b) for b in range(2)]
-        h_sorted = [kept([P, 2, 2, D // 4, 2], BF16, "hre%d" % b) for b in range(2)]
         h_codes = [kept([P, T], U32, "hc%d" % k) for k in range(ND)]
         h_scales = [kept([P, T], U8, "hs%d" % k) for k in range(ND)]
         r_codes = [kept([P, J], U32, "rc%d" % k) for k in range(ND)]
@@ -91,65 +86,36 @@ def tile_dpo_like_hidden_step_s11_kernel(tc, h, r, beta, p_chosen, p_rejected, u
         def span(half, width):
             return slice(0, width) if half is None else slice(half * width // 2, (half + 1) * width // 2)
 
-        warm = {}
-
         def warm_table():
-            x = streamed([P, 256, 4], BF16, "bst", HALF_BUFS)
+            x = streamed([P, 512, 4], BF16, "half", HALF_BUFS)
             nc.scalar.activation(out=x[:, 0:1, 0:1], in_=ident[:, 0:1].unsqueeze(2), func=ACT.Sigmoid)
 
-        def warm_zeros():
-            warm["zeros"] = streamed([P, 512, 4], BF16, "stage", STAGE_BUFS)
-            nc.vector.memset(warm["zeros"][:].rearrange("p c j -> p (c j)").bitcast(I32), 0)
-
-        def warm_operand():
-            quantize(a_codes[1], a_scales[1], slice(0, T), warm["zeros"][:])
-
-        def warm_passes(n):
-            x = bank(7, [P, 512])
-            for i in range(n):
-                mx_pass(x[:], fp8(a_codes[1], a_scales[1], 0, P), fp8(a_codes[1], a_scales[1], 0, T), True, True)
-
-        pc, pr, r_rows = {}, {}, {}
+        pc, pr = {}, {}
 
         def tile_rows(src, q):
             g, t = divmod(q, 4)
             return src[g * 512 : (g + 1) * 512, :].rearrange("(m t) v -> m t v", t=4)[:, t, :]
 
-        def new_p(q):
-            pc[q] = streamed([P, V], BF16, "pc", P_BUFS)
-            pr[q] = streamed([P, V], BF16, "pr", P_BUFS)
-
-        def load_half(q, a):
-            if a == 0:
-                new_p(q)
+        def load_p(q, a=None):
+            if q not in pc:
+                pc[q] = streamed([P, V], BF16, "pc", P_BUFS)
+                pr[q] = streamed([P, V], BF16, "pr", P_BUFS)
             cols = span(a, V)
             nc.sync.dma_start(out=pc[q][:, cols], in_=tile_rows(p_chosen, q)[:, cols])
             nc.sync.dma_start(out=pr[q][:, cols], in_=tile_rows(p_rejected, q)[:, cols])
 
-        def load_tile(q):
-            new_p(q)
-            nc.sync.dma_start(out=pc[q][:], in_=tile_rows(p_chosen, q))
-            for a in range(2):
-                nc.sync.dma_start(out=pr[q][:, span(a, V)], in_=tile_rows(p_rejected, q)[:, span(a, V)])
+        def load_ut(v):
+            nc.sync.dma_start(out=ut_codes[v][:].bitcast(I32), in_=ut_words[v].bitcast(I32))
 
-        def load_ut_front(v):
-            nc.sync.dma_start(out=ut_front[v][:].bitcast(I32), in_=ut_words[v, :, 0 : 2 * FRONT].bitcast(I32))
+        def zero_scales():
+            nc.vector.memset(ut_sc[:].bitcast(I32), 0)
 
-        def load_ut_back():
-            src = ut_words[:, :, 2 * FRONT : 2 * D].rearrange("g p n -> p g n")
-            nc.sync.dma_start(out=ut_back[:].bitcast(I32), in_=src.bitcast(I32))
-
-        def zero_scales(part):
-            nc.vector.memset(ut_sc[part][:].bitcast(I32), 0)
-
-        def load_scales(part):
-            cols = (slice(0, FRONT), slice(FRONT, D))[part]
+        def load_scales():
             for i in range(4):
-                src = ut_scales[:, i:16:4, cols].rearrange("g q n -> q g n")
-                nc.sync.dma_start(out=ut_sc[part][i:P:32, :, :].bitcast(I32), in_=src.bitcast(I32))
+                src = ut_scales[:, i:16:4, :].rearrange("g q n -> q g n")
+                nc.sync.dma_start(out=ut_sc[i:P:32, :, :].bitcast(I32), in_=src.bitcast(I32))
 
         def load_r(k):
-            r_rows[k] = streamed([P, 4, J], BF16, "rraw", R_BUFS)
             nc.sync.dma_start(out=r_rows[k][:], in_=r[k * 512 : (k + 1) * 512, :].rearrange("(p j) c -> p j c", j=4))
 
         def load_h(b):
@@ -160,122 +126,105 @@ def tile_dpo_like_hidden_step_s11_kernel(tc, h, r, beta, p_chosen, p_rejected, u
 
         diff, c_turned, c_staged, c_codes, c_scales = {}, {}, {}, {}, {}
 
-        def sub(q, a):
-            if a == 0:
-                diff[q] = streamed([P, 2, V // 4, 2], BF16, "diff", DIFF_BUFS)
+        def sub(q, v, n=2):
+            diff[q, v] = streamed([P, 2, n * P, 2], BF16, "diff", PIECE_BUFS)
+            cols = slice(512 * v, 512 * (v + n))
             nc.vector.tensor_tensor(
-                out=diff[q][:, :, span(a, V // 4), :].rearrange("p u w e -> p w u e"),
-                in0=pc[q][:, span(a, V)].rearrange("p (w u e) -> p w u e", u=2, e=2),
-                in1=pr[q][:, span(a, V)].rearrange("p (w u e) -> p w u e", u=2, e=2),
+                out=diff[q, v][:].rearrange("p u w e -> p w u e"),
+                in0=pc[q][:, cols].rearrange("p (w u e) -> p w u e", u=2, e=2),
+                in1=pr[q][:, cols].rearrange("p (w u e) -> p w u e", u=2, e=2),
                 op=ALU.subtract,
             )
 
-        def turn_c(q, a, b):
-            words = diff[q][:].rearrange("p u w e -> p (u w e)").bitcast(F32)
-            c_turned[q, a] = bank(b, [P, 2, 2, P])
-            for i in range(2):
+        def turn_c(q, v, b, n=2):
+            words = diff[q, v][:].rearrange("p u w e -> p (u w e)").bitcast(F32)
+            for i in range(n):
+                if i % 2 == 0:
+                    c_turned[q, v + i] = bank(b + i // 2, [P, min(n, 2), 2, P])
                 for u in range(2):
-                    lo = u * (V // 4) + (2 * a + i) * P
-                    nc.tensor.transpose(c_turned[q, a][:, i, u, :], words[:, lo : lo + P], ident[:])
+                    lo = (u * n + i) * P
+                    nc.tensor.transpose(c_turned[q, v + i - i % 2][:, i % 2, u, :], words[:, lo : lo + P], ident[:])
 
-        def copy_words(dst, src):
+        def copy_words(eng, dst, src):
             words = dst.rearrange("p c j -> p (c j)").bitcast(F32)
-            move("s", words.rearrange("p (i r u) -> p i r u", i=2, u=2), src[:].rearrange("p i u r -> p i r u"))
+            move(eng, words.rearrange("p (i r u) -> p i r u", r=P, u=2), src[:].rearrange("p i u r -> p i r u"))
 
-        def stage_c(q, a):
-            if a == 0:
-                c_staged[q] = streamed([P, 512, 4], BF16, "stage", STAGE_BUFS)
-            copy_words(c_staged[q][:, span(a, 512), :], c_turned[q, a])
+        def stage_c(q, v, n=2, banks=None):
+            if (q, v) not in c_staged:
+                c_staged[q, v] = streamed([P, n * P, 4], BF16, "cst", PIECE_BUFS)
+            for i in banks or range(0, n, 2):
+                copy_words("s", c_staged[q, v][:, i * P : min(n, i + 2) * P, :], c_turned[q, v + i])
 
-        def quant_c(q, a=None):
+        def quant_c(q, v, n=2, half=None):
             if q not in c_codes:
                 c_codes[q] = streamed([P, NV * P], U32, "cc", C_BUFS, 256)
                 c_scales[q] = streamed([P, NV * P], U8, "cs", C_BUFS, 256)
-            quantize(c_codes[q], c_scales[q], span(a, 512), c_staged[q][:, span(a, 512), :])
+            cols = span(half, n * P)
+            quantize(c_codes[q], c_scales[q], slice(v * P + cols.start, v * P + cols.stop), c_staged[q, v][:, cols, :])
 
-        chunk_acc, strip_acc = {}, {}
+        b_acc, b_staged, late_sums = {}, {}, []
 
-        def pass_b(dst, q, v, lo, n):
-            if lo < FRONT:
-                codes, scales = ut_front[v][:, 2 * lo : 2 * (lo + n)], ut_sc[0][:, v, lo : lo + n]
-            else:
-                at = lo - FRONT
-                codes, scales = ut_back[:, v, 2 * at : 2 * (at + n)], ut_sc[1][:, v, at : at + n]
-            mx_pass(dst, fp8(c_codes[q], c_scales[q], v * P, P), (codes.bitcast(FP4X4), scales), v == 0, v == NV - 1)
+        def late_bank(shape):
+            late_sums.append(shape)
+            return bank((1, 6, 7, 0, 2, 3, 4, 5)[(len(late_sums) - 1) % 8], shape)
 
-        def chunk(q, c, vs, b=None):
-            if vs[0] == 0:
-                chunk_acc[q, c] = bank(b, [P, 512])
-            for v in vs:
-                pass_b(chunk_acc[q, c][:], q, v, 512 * c, 512)
+        def pass_b(q, v, j, first, last):
+            if (q // 2, j) not in b_acc:
+                b_acc[q // 2, j] = late_bank([P, 2, W]) if late_sums else bank(2 + j, [P, 2, W])
+            lo = W * j
+            moving = ut_codes[v][:, 2 * lo : 2 * (lo + W)].bitcast(FP4X4), ut_sc[:, v, lo : lo + W]
+            mx_pass(b_acc[q // 2, j][:, q % 2, :], fp8(c_codes[q], c_scales[q], v * P, P), moving, first, last)
 
-        def slots_of(g, c):
-            return b_slots[0][:, :, 512 * c : 512 * (c + 1)] if g == 0 else b_slots[1][:]
+        def sweep(q, v):
+            for j in range(NB):
+                pass_b(q, v, j, (q, v) == (0, 0), (q, v) == (1, NV - 1))
 
-        def copy_chunk(q, c, eng="s"):
-            move(eng, slots_of(q // 4, c)[:, q % 4, :], chunk_acc[q, c][:])
+        def blocks(q, js, vs=range(NV)):
+            for j in js:
+                for v in vs:
+                    pass_b(q, v, j, v == 0, v == NV - 1)
 
-        def weave_b(g, c, eng, half=None):
-            dst = b_staged[g][:, 512 * c : 512 * (c + 1), :][:, span(half, 512), :]
-            src = slots_of(g, c)[:, :, span(half, 512)]
-            move(eng, dst.rearrange("p (c i) t -> p c t i", i=4), src.rearrange("p t (c i) -> p c t i", i=4))
+        def copy_b(pair, j, eng="s"):
+            dst = b_pairs[pair // 2][:, pair % 2, W * j : W * (j + 1), :]
+            move(eng, dst.rearrange("p (n i) e -> p n e i", i=2), b_acc[pair, j][:].rearrange("p e (n i) -> p n e i", i=2))
 
-        def strip_slot(s, t, b=None):
-            if t == 0:
-                strip_acc[s] = late_bank([P, 4, P]) if b is None else bank(b, [P, 4, P])
-            for v in ALL_V:
-                pass_b(strip_acc[s][:, t, :], 4 + t, v, s * P, P)
-
-        def strip(s, b=None):
-            for t in range(4):
-                strip_slot(s, t, b)
-
-        def copy_strip(s):
-            dst = b_staged[1][:, s * P : (s + 1) * P, :].rearrange("p (c i) t -> p c t i", i=2)
-            move("s", dst, strip_acc[s][:].rearrange("p t (c i) -> p c t i", i=2))
+        def weave_b(g, lo, n, eng="v"):
+            b_staged[g, lo] = streamed([P, n, 4], BF16, "stage", STAGE_BUFS)
+            dst = b_staged[g, lo][:].rearrange("p (n i) (u e) -> p n u i e", u=2, i=2)
+            move(eng, dst, b_pairs[g][:, :, lo : lo + n, :].rearrange("p u (n i) e -> p n u i e", i=2))
 
         def quant_b(g, lo, n):
-            quantize(b_codes[g], b_scales[g], slice(lo, lo + n), b_staged[g][:, lo : lo + n, :])
+            quantize(b_codes[g], b_scales[g], slice(lo, lo + n), b_staged[g, lo][:])
 
         r_staged, h_turned, h_staged = {}, {}, {}
 
-        def weave_r(k, g, eng, half=None):
-            if (k, g) not in r_staged:
-                r_staged[k, g] = streamed([P, 512, 4], BF16, "stage", STAGE_BUFS)
-            dst = r_staged[k, g][:].rearrange("p (t a b) j -> p a j b t", t=4, b=2)
+        def weave_r(k, g, eng="v", half=None):
+            if k not in r_staged:
+                r_staged[k] = streamed([P, J, 4], BF16, "stage", STAGE_BUFS)
+            dst = r_staged[k][:, span(g, J), :].rearrange("p (t a b) j -> p a j b t", t=4, b=2)
             src = r_rows[k][:, :, g * 512 : (g + 1) * 512][:, :, span(half, 512)]
             move(eng, dst[:, span(half, 64), :, :, :], src.rearrange("p j (a b t) -> p a j b t", t=4, b=2))
 
-        def quant_r(k, g):
-            quantize(r_codes[k], r_scales[k], slice(g * 512, (g + 1) * 512), r_staged[k, g][:])
-
-        def sort_h(b):
-            dst = h_sorted[b][:].rearrange("p i u w e -> p i w u e")
-            move("v", dst, h_rows[b][:].rearrange("p i (w u e) -> p i w u e", u=2, e=2))
+        def quant_r(k, g=None):
+            quantize(r_codes[k], r_scales[k], span(g, J), r_staged[k][:, span(g, J), :])
 
         def turn_h(b, banks):
             for k in range(ND):
                 h_turned[k, b] = bank(banks[k], [P, 2, 2, P])
                 for i in range(2):
-                    words = h_sorted[b][:, i, :, :, :].rearrange("p u w e -> p (u w e)").bitcast(F32)
+                    words = h_rows[b][:, i, :].bitcast(F32)
                     for u in range(2):
-                        lo = u * (D // 4) + P * k
-                        nc.tensor.transpose(h_turned[k, b][:, i, u, :], words[:, lo : lo + P], ident[:])
+                        nc.tensor.transpose(h_turned[k, b][:, i, u, :], words[:, 256 * k + u : 256 * (k + 1) : 2], ident[:])
 
-        def stage_h(k, b):
-            h_staged[k, b] = streamed([P, 256, 4], BF16, "bst", HALF_BUFS)
-            copy_words(h_staged[k, b][:], h_turned[k, b])
+        def stage_h(k, b, eng="s"):
+            if b == 0:
+                h_staged[k] = streamed([P, T, 4], BF16, "half", HALF_BUFS)
+            copy_words(eng, h_staged[k][:, span(b, T), :], h_turned[k, b])
 
-        def quant_h(k, b):
-            quantize(h_codes[k], h_scales[k], span(b, T), h_staged[k, b][:])
+        def quant_h(k, b=None):
+            quantize(h_codes[k], h_scales[k], span(b, T), h_staged[k][:, span(b, T), :])
 
         m_acc, sig, a_staged = {}, {}, {}
-        late_banks = (7, 5, 6, 0, 1, 4, 2, 3)
-        late_sums = []
-
-        def late_bank(shape):
-            late_sums.append(shape)
-            return bank(late_banks[(len(late_sums) - 1) % 8], shape)
 
         def margins(g, b, w):
             m_acc[g, b, w] = late_bank([P, 2, 256])
@@ -286,11 +235,11 @@ def tile_dpo_like_hidden_step_s11_kernel(tc, h, r, beta, p_chosen, p_rejected, u
 
         def sigmoid(g, b, w):
             if w == 0:
-                sig[g, b] = streamed([P, 2, 256, 2], F32, "pc", P_BUFS)
+                sig[g, b] = streamed([P, 2, 256, 2], F32, ("pc", "pr")[g], P_BUFS)
             nc.scalar.activation(out=sig[g, b][:, w, :, :], in_=m_acc[g, b, w][:].rearrange("p e n -> p n e"), func=ACT.Sigmoid)
 
         def times_beta(g, b):
-            a_staged[g, b] = streamed([P, 256, 4], BF16, "bst", HALF_BUFS)
+            a_staged[g, b] = streamed([P, 256, 4], BF16, "half", HALF_BUFS)
             nc.vector.tensor_tensor(
                 out=a_staged[g, b][:].rearrange("p n (w e) -> p n w e", w=2),
                 in0=sig[g, b][:].rearrange("p w n e -> p n w e"),
@@ -303,244 +252,210 @@ def tile_dpo_like_hidden_step_s11_kernel(tc, h, r, beta, p_chosen, p_rejected, u
 
         o_acc, stores = {}, []
 
-        def result(i, c0, n, tiles=1):
-            o_acc[i, c0] = late_bank([P, 512])
+        def result(i, c0, n=512, tiles=1):
+            o_acc[i, c0] = late_bank([P, tiles, n])
             for a in range(tiles):
                 for g in range(NJ):
                     stationary = fp8(a_codes[g], a_scales[g], (i + a) * P, P)
-                    mx_pass(o_acc[i, c0][:, a * n : (a + 1) * n], stationary, fp8(b_codes[g], b_scales[g], c0, n), g == 0, g == NJ - 1)
+                    mx_pass(o_acc[i, c0][:, a, :], stationary, fp8(b_codes[g], b_scales[g], c0, n), g == 0, g == NJ - 1)
 
-        def store(i, c0, n, eng, tiles=1):
-            tag, bufs = (("osb", OUT_BUFS), ("diff", DIFF_BUFS), ("pr", P_BUFS))[len(stores) % 3]
+        def store(i, c0, eng, n=512, tiles=1):
+            tag, bufs = (("osb", OUT_BUFS), ("diff", PIECE_BUFS), ("cst", PIECE_BUFS))[len(stores) % 3]
             stores.append(tag)
-            x = streamed([P, 512], F32, tag, bufs)
-            move(eng, x[:, 0 : tiles * n], o_acc[i, c0][:, 0 : tiles * n])
-            dst = out[i * P : (i + tiles) * P, c0 : c0 + n].rearrange("(a p) c -> p a c", a=tiles)
-            nc.sync.dma_start(out=dst, in_=x[:, 0 : tiles * n].rearrange("p (a c) -> p a c", a=tiles))
+            x = streamed([P, tiles, n], F32, tag, bufs)
+            move(eng, x[:], o_acc[i, c0][:])
+            nc.sync.dma_start(out=out[i * P : (i + tiles) * P, c0 : c0 + n].rearrange("(a p) c -> p a c", a=tiles), in_=x[:])
 
-        make_identity(nc, ident[:])
-        load_half(0, 0)
-        load_half(1, 0)
-        zero_scales(0)
-        warm_table()
-        warm_zeros()
-        load_scales(0)
-        zero_scales(1)
-        load_ut_front(0)
-        load_half(2, 0)
-        load_ut_front(1)
-        load_half(0, 1)
-        load_half(1, 1)
-        load_ut_front(2)
-        load_half(2, 1)
-        load_ut_front(3)
-        load_ut_back()
-        load_scales(1)
-        load_tile(3)
-        load_r(0)
+        ALL_J, FIRST_V, LAST_V = range(NB), (0, 1), (2, 3)
 
-        def front(q, vs):
-            for c in range(2):
-                chunk(q, c, vs, 2 + 2 * q + c)
-
-        def turn_half(q, a):
-            sub(q, a)
-            turn_c(q, a, (q + a) % 2)
-
-        turn_half(0, 0)
-        warm_operand()
-        warm_passes(2)
-        stage_c(0, 0)
-        turn_half(1, 0)
-        warm_passes(1)
-        stage_c(1, 0)
-        for q in range(2):
-            quant_c(q, 0)
-            front(q, (0,))
-        turn_half(2, 0)
-        stage_c(2, 0)
-        for q in range(2):
-            front(q, (1,))
-        turn_half(0, 1)
-        load_tile(4)
-        quant_c(2, 0)
-        stage_c(0, 1)
-        front(2, (0,))
-        turn_half(1, 1)
-        load_tile(5)
-        stage_c(1, 1)
-        front(2, (1,))
-        quant_c(0, 1)
-        front(0, (2,))
-        turn_half(2, 1)
-        load_tile(6)
-        stage_c(2, 1)
-        quant_c(1, 1)
-        front(1, (2,))
-        for q in range(2):
-            front(q, (3,))
-        quant_c(2, 1)
-        front(2, LAST_V)
-        for q in range(2):
-            copy_chunk(q, 0)
-            copy_chunk(q, 1, "v")
-
-        def sub_tile(q):
-            for a in range(2):
-                sub(q, a)
+        def ready(q, v, b, n=2):
+            sub(q, v, n)
+            turn_c(q, v, b, n)
+            stage_c(q, v, n)
 
         def turn_tile(q):
-            for a in range(2):
-                turn_c(q, a, a)
+            turn_c(q, 0, 0, NV)
+            stage_c(q, 0, NV)
 
-        def stage_tile(q):
-            for a in range(2):
-                stage_c(q, a)
+        def first_blocks(q):
+            blocks(q, (0, 1, 2), FIRST_V)
+            blocks(q, (0, 1, 2), LAST_V)
 
-        chunk(0, 2, ALL_V, 2)
-        for c in range(2):
-            copy_chunk(2, c)
-        chunk(1, 2, FIRST_V, 3)
-        sub_tile(3)
-        load_tile(7)
-        load_h(0)
+        make_identity(nc, ident[:])
+        zero_scales()
+        load_p(0, 0)
+        load_scales()
+        warm_table()
+        load_ut(0)
+        load_p(1, 0)
+        load_ut(1)
+        load_p(0, 1)
+        load_p(1, 1)
+        load_ut(2)
+        load_p(2, 0)
+        load_ut(3)
+        load_p(2, 1)
+
+        ready(0, 0, 0, 1)
+        ready(0, 1, 1, 1)
+        quant_c(0, 0, 1)
+        sweep(0, 0)
+        quant_c(0, 1, 1)
+        ready(1, 0, 0, 1)
+        ready(1, 1, 1, 1)
+        sweep(0, 1)
+        quant_c(1, 0, 1)
+        sweep(1, 0)
+        ready(0, 2, 0)
+        load_p(3)
+        load_r(0)
+        quant_c(1, 1, 1)
+        sweep(1, 1)
+        ready(1, 2, 1, 1)
+        ready(1, 3, 0, 1)
+        load_p(4)
+        quant_c(0, 2)
+        sweep(0, 2)
+        quant_c(1, 2, 1)
+        quant_c(1, 3, 1)
+        sweep(1, 2)
+        ready(2, 0, 1)
+        for j in ALL_J:
+            pass_b(0, 3, j, False, False)
+            pass_b(1, 3, j, False, True)
+        sub(2, 2)
+        load_p(5)
         load_r(1)
+        turn_c(2, 2, 0)
+        quant_c(2, 0)
+        for j in ALL_J:
+            copy_b(0, j, "sssvvs"[j])
+        stage_c(2, 2)
+        sub(3, 0, NV)
+        load_p(6)
+        load_h(0)
+
+        blocks(2, ALL_J, FIRST_V)
+        quant_c(2, 2)
+        turn_tile(3)
+        blocks(2, ALL_J, LAST_V)
+        weave_r(0, 0)
+        weave_r(0, 1, "s", 0)
+        quant_c(3, 0, NV, 0)
+        quant_c(3, 0, NV, 1)
+
+        first_blocks(3)
+        sub(4, 0, NV)
+        load_p(7)
         load_h(1)
         load_r(2)
         load_beta()
-        copy_chunk(0, 2)
-        turn_tile(3)
-        stage_tile(3)
-        chunk(1, 2, LAST_V)
-        chunk(2, 2, ALL_V, 4)
-        quant_c(3, 0)
-        weave_r(0, 0, "v", 0)
-        quant_c(3, 1)
-        for c in range(ND):
-            chunk(3, c, FIRST_V, 5 + c)
-        copy_chunk(1, 2)
-        copy_chunk(2, 2)
-        weave_r(0, 1, "s", 0)
-        chunk(3, 0, LAST_V)
-        sub_tile(4)
-        weave_r(0, 0, "v", 1)
+        for j in (0, 1):
+            copy_b(1, j)
         turn_tile(4)
-        copy_chunk(3, 0)
-        stage_tile(4)
-        for c in range(1, ND):
-            chunk(3, c, LAST_V)
-            copy_chunk(3, c)
-
-        def passes_of(q):
-            chunk(q, 1, ALL_V, (4, 7)[q % 2])
-            for s in range(4):
-                strip_slot(s, q - 4, (2, 3, 5, 6)[s])
-
-        sub_tile(5)
-        turn_tile(5)
-        stage_tile(5)
-        for a in range(2):
-            quant_c(4, a)
-        passes_of(4)
+        blocks(3, (3, 4, 5))
         weave_r(0, 1, "v", 1)
-        weave_b(0, 0, "s", 0)
-        copy_chunk(4, 1)
-        sub_tile(6)
-        turn_tile(6)
-        stage_tile(6)
-        quant_c(5)
-        passes_of(5)
-        for g in range(NJ):
-            quant_r(0, g)
-        weave_b(0, 0, "s", 1)
-        copy_chunk(5, 1)
-        sub_tile(7)
-        turn_tile(7)
-        stage_tile(7)
-        quant_c(6)
-        passes_of(6)
-        copy_chunk(6, 1)
-        sort_h(0)
-        weave_b(0, 1, "v")
-        weave_r(1, 0, "v", 0)
-        quant_c(7)
-        weave_r(1, 1, "s", 0)
-        weave_r(1, 0, "v", 1)
+        quant_r(0)
+        quant_c(4, 0, NV, 0)
+        quant_c(4, 0, NV, 1)
+        for j in range(2, NB):
+            copy_b(1, j)
 
-        h_banks = (0, 1, 4)
-        turn_h(0, h_banks)
-        passes_of(7)
-        for k in range(ND):
-            stage_h(k, 0)
-        sort_h(1)
-        turn_h(1, h_banks)
-        quant_r(1, 0)
+        first_blocks(4)
+        sub(5, 0, NV)
+        turn_tile(5)
+        blocks(4, (3, 4, 5))
+        weave_r(1, 1, "s", 0)
+        weave_b(0, 0, 512)
+        weave_r(1, 0)
+        quant_c(5, 0, NV, 0)
+        weave_r(1, 1, "v", 1)
+        quant_c(5, 0, NV, 1)
+
+        first_blocks(5)
+        blocks(5, (3, 4, 5))
+        sub(6, 0, NV)
+        for j in range(4):
+            copy_b(2, j)
+        quant_r(1)
+        weave_b(0, 512, 512)
         quant_b(0, 0, 512)
-        weave_r(2, 0, "v")
-        for s in range(2):
-            copy_strip(s)
-        weave_r(1, 1, "s", 1)
-        copy_chunk(7, 1)
-        strip(8, 2)
-        strip(9, 3)
-        for k in range(ND):
-            quant_h(k, 0)
-        quant_r(2, 0)
-        weave_r(2, 1, "v")
-        for k in range(1, ND):
-            quant_r(k, 1)
+        quant_b(0, 512, 512)
+        turn_tile(6)
+        turn_h(0, (2, 3, 4))
+        for a in range(2):
+            quant_c(6, 0, NV, a)
+            stage_h(a, 0)
+        for j in (4, 5):
+            copy_b(2, j)
+        sub(7, 0, NV)
+
+        blocks(6, (3, 0), FIRST_V)
+        blocks(6, (3, 0), LAST_V)
+        blocks(6, (1,))
+        turn_c(7, 0, 0, NV)
+        stage_c(7, 0, NV, (0,))
+        stage_h(2, 0)
+        stage_c(7, 0, NV, (2,))
+        turn_h(1, (6, 7, 0))
+        blocks(6, (2,))
+        weave_r(2, 0)
+        weave_r(2, 1, "v", 0)
+        quant_c(7, 0, NV, 0)
+        quant_h(0, 0)
+        quant_h(1, 0)
+        quant_c(7, 0, NV, 1)
+        quant_h(2, 0)
         for k in range(ND):
             stage_h(k, 1)
-            if k < 2:
-                copy_strip(2 + k)
+        quant_r(2, 0)
+        weave_r(2, 1, "v", 1)
+        for k in range(ND):
             quant_h(k, 1)
+        quant_r(2, 1)
 
-        for g in range(NJ):
-            for w in range(2):
-                margins(g, 0, w)
-                sigmoid(g, 0, w)
-            copy_strip(8 + g)
-        weave_b(1, 1, "v")
-        quant_b(0, 512, 512)
+        first_blocks(7)
+        blocks(7, (3,))
+        for j in range(3):
+            copy_b(3, j)
+
+        for b in range(2):
+            for g in range(NJ):
+                for w in range(2):
+                    margins(g, b, w)
+                    sigmoid(g, b, w)
+                if (g, b) == (0, 0):
+                    copy_b(3, 3)
+        weave_b(1, 0, 512)
+        weave_b(0, 1024, 512)
         times_beta(0, 0)
         quant_b(1, 0, 512)
-        quant_a(0, 0)
         times_beta(1, 0)
-        quant_b(1, 512, 256)
+        quant_a(0, 0)
         quant_a(1, 0)
-        quant_b(1, 768, 256)
-        weave_b(0, 2, "s", 0)
-        for g in range(NJ):
-            for w in range(2):
-                margins(g, 1, w)
-                sigmoid(g, 1, w)
-
-        strip(10)
+        weave_b(1, 512, 512)
         times_beta(0, 1)
-        quant_b(1, 1024, 256)
-        quant_b(0, 1024, 256)
+        quant_b(1, 512, 512)
         times_beta(1, 1)
-        quant_a(0, 1)
-        for c0, i, eng in ((0, 0, "s"), (0, 1, "s"), (512, 0, "s"), (512, 1, "v")):
-            result(i, c0, 512)
-            store(i, c0, 512, eng)
-        result(0, 1024, 256, 2)
-        copy_strip(10)
-        store(0, 1024, 256, "s", 2)
-        strip(11)
-        copy_strip(11)
-        quant_a(1, 1)
-        weave_b(0, 2, "v", 1)
-        quant_b(1, 1280, P)
-        quant_b(0, 1280, 256)
-        quant_b(1, 1408, P)
-        for c0, i, eng in ((0, 2, "s"), (0, 3, "s"), (512, 2, "v"), (512, 3, "s")):
-            result(i, c0, 512)
-            store(i, c0, 512, eng)
-        result(0, 1280, 256, 2)
-        store(0, 1280, 256, "v", 2)
-        result(2, 1024, 512)
-        store(2, 1024, 512, "s")
+        for g in range(NJ):
+            quant_a(g, 1)
+
+        for i in range(2):
+            result(i, 0)
+            store(i, 0, "s")
+        for j in (4, 5):
+            for q in (6, 7):
+                blocks(q, (j,))
+            copy_b(3, j)
+        weave_b(1, 1024, 512)
+        quant_b(0, 1024, 512)
+        quant_b(1, 1024, 512)
+        for i, c0 in ((0, 512), (1, 512), (2, 0), (3, 0), (2, 512)):
+            result(i, c0)
+            store(i, c0, "s")
+        for i, c0, eng in ((3, 512, "v"), (0, 1024, "s"), (1, 1024, "v"), (2, 1024, "s")):
+            result(i, c0)
+            store(i, c0, eng)
         for c0, eng in ((1024, "v"), (1280, "s")):
-            result(3, c0, 256)
-            store(3, c0, 256, eng)
+            result(3, c0, W)
+            store(3, c0, eng, W)

@@ -55,7 +55,7 @@ def tile_dpo_like_hidden_step_s11_kernel(tc, h, r, beta, p_chosen, p_rejected, u
         ut_sc = kept([P, NV, D], U8, "usc", 256)
         ut_codes = [kept([P, 2 * D], U8, "ut%d" % v) for v in range(NV)]
         b_pairs = [kept([P, 2, D, 2], BF16, "bp%d" % g) for g in range(NJ)]
-        r_rows = [kept([P, 4, J], BF16, "rraw%d" % k) for k in range(ND)]
+        r_rows = {}
         h_rows = [kept([P, 2, D], BF16, "hraw%d" % b) for b in range(2)]
         h_codes = [kept([P, T], U32, "hc%d" % k) for k in range(ND)]
         h_scales = [kept([P, T], U8, "hs%d" % k) for k in range(ND)]
@@ -104,6 +104,13 @@ def tile_dpo_like_hidden_step_s11_kernel(tc, h, r, beta, p_chosen, p_rejected, u
             nc.sync.dma_start(out=pc[q][:, cols], in_=tile_rows(p_chosen, q)[:, cols])
             nc.sync.dma_start(out=pr[q][:, cols], in_=tile_rows(p_rejected, q)[:, cols])
 
+        def load_tile(q):
+            pc[q] = streamed([P, V], BF16, "pc", P_BUFS)
+            pr[q] = streamed([P, V], BF16, "pr", P_BUFS)
+            nc.sync.dma_start(out=pc[q][:], in_=tile_rows(p_chosen, q))
+            for a in range(2):
+                nc.sync.dma_start(out=pr[q][:, span(a, V)], in_=tile_rows(p_rejected, q)[:, span(a, V)])
+
         def load_ut(v):
             nc.sync.dma_start(out=ut_codes[v][:].bitcast(I32), in_=ut_words[v].bitcast(I32))
 
@@ -115,11 +122,18 @@ def tile_dpo_like_hidden_step_s11_kernel(tc, h, r, beta, p_chosen, p_rejected, u
                 src = ut_scales[:, i:16:4, :].rearrange("g q n -> q g n")
                 nc.sync.dma_start(out=ut_sc[i:P:32, :, :].bitcast(I32), in_=src.bitcast(I32))
 
-        def load_r(k):
-            nc.sync.dma_start(out=r_rows[k][:], in_=r[k * 512 : (k + 1) * 512, :].rearrange("(p j) c -> p j c", j=4))
+        def load_r(k, g=None):
+            cols = span(g, J)
+            x = kept([P, 4, cols.stop - cols.start], BF16, "rraw%d%s" % (k, g))
+            nc.sync.dma_start(out=x[:], in_=r[k * 512 : (k + 1) * 512, cols].rearrange("(p j) c -> p j c", j=4))
+            for a in range(NJ):
+                if g is None:
+                    r_rows[k, a] = x[:, :, span(a, J)]
+                elif a == g:
+                    r_rows[k, a] = x[:]
 
         def load_h(b):
-            nc.sync.dma_start(out=h_rows[b][:], in_=h[256 * b : 256 * (b + 1), :].rearrange("(i p) k -> p i k", p=P))
+            nc.sync.dma_start(out=h_rows[b][:], in_=h[256 * b : 256 * (b + 1), :].rearrange("(p i) k -> p i k", i=2))
 
         def load_beta():
             nc.sync.dma_start(out=beta_sb[:], in_=beta.rearrange("(g p t) -> p g t", g=NJ, t=4))
@@ -188,13 +202,17 @@ def tile_dpo_like_hidden_step_s11_kernel(tc, h, r, beta, p_chosen, p_rejected, u
             dst = b_pairs[pair // 2][:, pair % 2, W * j : W * (j + 1), :]
             move(eng, dst.rearrange("p (n i) e -> p n e i", i=2), b_acc[pair, j][:].rearrange("p e (n i) -> p n e i", i=2))
 
-        def weave_b(g, lo, n, eng="v"):
-            b_staged[g, lo] = streamed([P, n, 4], BF16, "stage", STAGE_BUFS)
-            dst = b_staged[g, lo][:].rearrange("p (n i) (u e) -> p n u i e", u=2, i=2)
-            move(eng, dst, b_pairs[g][:, :, lo : lo + n, :].rearrange("p u (n i) e -> p n u i e", i=2))
+        def weave_b(g, lo, n, eng="v", half=None):
+            if not half:
+                x = kept([P, n, 4], BF16, "late") if eng == "s" else streamed([P, n, 4], BF16, "stage", STAGE_BUFS)
+                for at in range(0, n, W):
+                    b_staged[g, lo + at] = x[:, at:n, :]
+            dst = b_staged[g, lo][:, span(half, n), :].rearrange("p (n i) (u e) -> p n u i e", u=2, i=2)
+            src = b_pairs[g][:, :, lo : lo + n, :][:, :, span(half, n), :]
+            move(eng, dst, src.rearrange("p u (n i) e -> p n u i e", i=2))
 
         def quant_b(g, lo, n):
-            quantize(b_codes[g], b_scales[g], slice(lo, lo + n), b_staged[g, lo][:])
+            quantize(b_codes[g], b_scales[g], slice(lo, lo + n), b_staged[g, lo][:, 0:n, :])
 
         r_staged, h_turned, h_staged = {}, {}, {}
 
@@ -202,7 +220,7 @@ def tile_dpo_like_hidden_step_s11_kernel(tc, h, r, beta, p_chosen, p_rejected, u
             if k not in r_staged:
                 r_staged[k] = streamed([P, J, 4], BF16, "stage", STAGE_BUFS)
             dst = r_staged[k][:, span(g, J), :].rearrange("p (t a b) j -> p a j b t", t=4, b=2)
-            src = r_rows[k][:, :, g * 512 : (g + 1) * 512][:, :, span(half, 512)]
+            src = r_rows[k, g][:, :, span(half, 512)]
             move(eng, dst[:, span(half, 64), :, :, :], src.rearrange("p j (a b t) -> p a j b t", t=4, b=2))
 
         def quant_r(k, g=None):
@@ -264,7 +282,8 @@ def tile_dpo_like_hidden_step_s11_kernel(tc, h, r, beta, p_chosen, p_rejected, u
             stores.append(tag)
             x = streamed([P, tiles, n], F32, tag, bufs)
             move(eng, x[:], o_acc[i, c0][:])
-            nc.sync.dma_start(out=out[i * P : (i + tiles) * P, c0 : c0 + n].rearrange("(a p) c -> p a c", a=tiles), in_=x[:])
+            rows = out[256 * (i // 2) : 256 * (i // 2 + 1), c0 : c0 + n].rearrange("(p a) c -> p a c", a=2)
+            nc.sync.dma_start(out=rows[:, i % 2 : i % 2 + tiles, :], in_=x[:])
 
         ALL_J, FIRST_V, LAST_V = range(NB), (0, 1), (2, 3)
 
@@ -307,13 +326,15 @@ def tile_dpo_like_hidden_step_s11_kernel(tc, h, r, beta, p_chosen, p_rejected, u
         quant_c(1, 0, 1)
         sweep(1, 0)
         ready(0, 2, 0)
-        load_p(3)
+        load_tile(3)
         load_r(0)
         quant_c(1, 1, 1)
         sweep(1, 1)
         ready(1, 2, 1, 1)
         ready(1, 3, 0, 1)
         load_p(4)
+        load_h(0)
+        load_r(1, 0)
         quant_c(0, 2)
         sweep(0, 2)
         quant_c(1, 2, 1)
@@ -324,95 +345,102 @@ def tile_dpo_like_hidden_step_s11_kernel(tc, h, r, beta, p_chosen, p_rejected, u
             pass_b(0, 3, j, False, False)
             pass_b(1, 3, j, False, True)
         sub(2, 2)
-        load_p(5)
-        load_r(1)
+        load_tile(5)
+        load_r(1, 1)
         turn_c(2, 2, 0)
         quant_c(2, 0)
         for j in ALL_J:
-            copy_b(0, j, "sssvvs"[j])
+            copy_b(0, j, "ssvvss"[j])
         stage_c(2, 2)
-        sub(3, 0, NV)
+        sub(3, 0)
+        sub(3, 2)
         load_p(6)
-        load_h(0)
 
         blocks(2, ALL_J, FIRST_V)
         quant_c(2, 2)
-        turn_tile(3)
+        for v in (0, 2):
+            turn_c(3, v, 1 - v // 2)
+        for v in (0, 2):
+            stage_c(3, v)
         blocks(2, ALL_J, LAST_V)
-        weave_r(0, 0)
+        weave_r(0, 0, "v", 0)
         weave_r(0, 1, "s", 0)
-        quant_c(3, 0, NV, 0)
-        quant_c(3, 0, NV, 1)
+        for v in (0, 2):
+            quant_c(3, v)
+        weave_r(0, 0, "v", 1)
 
         first_blocks(3)
-        sub(4, 0, NV)
-        load_p(7)
-        load_h(1)
-        load_r(2)
-        load_beta()
-        for j in (0, 1):
-            copy_b(1, j)
-        turn_tile(4)
         blocks(3, (3, 4, 5))
         weave_r(0, 1, "v", 1)
+        sub(4, 0, NV)
+        load_p(7)
+        load_r(2)
+        load_h(1)
+        load_beta()
         quant_r(0)
-        quant_c(4, 0, NV, 0)
-        quant_c(4, 0, NV, 1)
-        for j in range(2, NB):
-            copy_b(1, j)
-
-        first_blocks(4)
-        sub(5, 0, NV)
-        turn_tile(5)
-        blocks(4, (3, 4, 5))
-        weave_r(1, 1, "s", 0)
-        weave_b(0, 0, 512)
-        weave_r(1, 0)
-        quant_c(5, 0, NV, 0)
-        weave_r(1, 1, "v", 1)
-        quant_c(5, 0, NV, 1)
-
-        first_blocks(5)
-        blocks(5, (3, 4, 5))
-        sub(6, 0, NV)
+        weave_r(1, 0, "v", 0)
         for j in range(4):
-            copy_b(2, j)
-        quant_r(1)
-        weave_b(0, 512, 512)
-        quant_b(0, 0, 512)
-        quant_b(0, 512, 512)
-        turn_tile(6)
+            copy_b(1, j)
+        turn_tile(4)
         turn_h(0, (2, 3, 4))
         for a in range(2):
-            quant_c(6, 0, NV, a)
+            quant_c(4, 0, NV, a)
             stage_h(a, 0)
-        for j in (4, 5):
+        copy_b(1, 4)
+        stage_h(2, 0)
+        copy_b(1, 5)
+        sub(5, 0)
+        sub(5, 2)
+
+        blocks(4, (3, 0), FIRST_V)
+        blocks(4, (3, 0), LAST_V)
+        blocks(4, (1,))
+        for v in (0, 2):
+            turn_c(5, v, v // 2)
+        for v in (0, 2):
+            stage_c(5, v)
+        blocks(4, (2, 4, 5))
+        weave_r(1, 1, "s", 0)
+        weave_b(0, 1024, 512, "s", 0)
+        weave_r(1, 0, "v", 1)
+        weave_b(0, 0, 1024)
+        quant_h(0, 0)
+        quant_c(5, 0)
+        quant_c(5, 2)
+
+        first_blocks(5)
+        sub(6, 0, NV)
+        for j in (0, 1):
+            copy_b(2, j)
+        turn_tile(6)
+        blocks(5, (3, 4, 5))
+        weave_r(1, 1, "v", 1)
+        quant_b(0, 0, 1024)
+        quant_c(6, 0, NV, 0)
+        quant_c(6, 0, NV, 1)
+        for j in range(2, NB):
             copy_b(2, j)
         sub(7, 0, NV)
 
-        blocks(6, (3, 0), FIRST_V)
-        blocks(6, (3, 0), LAST_V)
-        blocks(6, (1,))
-        turn_c(7, 0, 0, NV)
-        stage_c(7, 0, NV, (0,))
-        stage_h(2, 0)
-        stage_c(7, 0, NV, (2,))
+        first_blocks(6)
+        turn_tile(7)
         turn_h(1, (6, 7, 0))
-        blocks(6, (2,))
+        blocks(6, (3,))
         weave_r(2, 0)
-        weave_r(2, 1, "v", 0)
+        quant_r(1)
         quant_c(7, 0, NV, 0)
-        quant_h(0, 0)
         quant_h(1, 0)
         quant_c(7, 0, NV, 1)
         quant_h(2, 0)
         for k in range(ND):
             stage_h(k, 1)
+        weave_b(0, 1024, 512, "s", 1)
         quant_r(2, 0)
-        weave_r(2, 1, "v", 1)
-        for k in range(ND):
-            quant_h(k, 1)
+        weave_r(2, 1)
+        quant_h(0, 1)
         quant_r(2, 1)
+        for k in (1, 2):
+            quant_h(k, 1)
 
         first_blocks(7)
         blocks(7, (3,))
@@ -427,7 +455,6 @@ def tile_dpo_like_hidden_step_s11_kernel(tc, h, r, beta, p_chosen, p_rejected, u
                 if (g, b) == (0, 0):
                     copy_b(3, 3)
         weave_b(1, 0, 512)
-        weave_b(0, 1024, 512)
         times_beta(0, 0)
         quant_b(1, 0, 512)
         times_beta(1, 0)

@@ -23,11 +23,10 @@ NJ = J // 512
 W = 256
 NB = D // W
 P_BUFS = 3
-PIECE_BUFS = 3
+PIECE_BUFS = 4
 C_BUFS = 3
 STAGE_BUFS = 3
 HALF_BUFS = 3
-OUT_BUFS = 4
 
 
 def tile_dpo_like_hidden_step_s11_kernel(tc, h, r, beta, p_chosen, p_rejected, ut_words, ut_scales, out):
@@ -57,6 +56,7 @@ def tile_dpo_like_hidden_step_s11_kernel(tc, h, r, beta, p_chosen, p_rejected, u
         b_pairs = [kept([P, 2, D, 2], BF16, "bp%d" % g) for g in range(NJ)]
         r_rows = {}
         h_rows = [kept([P, 2, D], BF16, "hraw%d" % b) for b in range(2)]
+        h_sorted = kept([P, 2, 2, D // 4, 2], BF16, "hre")
         h_codes = [kept([P, T], U32, "hc%d" % k) for k in range(ND)]
         h_scales = [kept([P, T], U8, "hs%d" % k) for k in range(ND)]
         r_codes = [kept([P, J], U32, "rc%d" % k) for k in range(ND)]
@@ -161,13 +161,24 @@ def tile_dpo_like_hidden_step_s11_kernel(tc, h, r, beta, p_chosen, p_rejected, u
 
         def copy_words(eng, dst, src):
             words = dst.rearrange("p c j -> p (c j)").bitcast(F32)
-            move(eng, words.rearrange("p (i r u) -> p i r u", r=P, u=2), src[:].rearrange("p i u r -> p i r u"))
+            move(eng, words.rearrange("p (i r u) -> p i r u", r=P, u=2), src.rearrange("p i u r -> p i r u"))
 
-        def stage_c(q, v, n=2, banks=None):
+        def stage_c(q, v, n=2, banks=None, eng="s"):
             if (q, v) not in c_staged:
                 c_staged[q, v] = streamed([P, n * P, 4], BF16, "cst", PIECE_BUFS)
             for i in banks or range(0, n, 2):
-                copy_words("s", c_staged[q, v][:, i * P : min(n, i + 2) * P, :], c_turned[q, v + i])
+                copy_words(eng, c_staged[q, v][:, i * P : min(n, i + 2) * P, :], c_turned[q, v + i][:])
+
+        def turn_pass(q, v, b):
+            if v % 2 == 0:
+                c_turned[q, v] = bank(b, [P, 2, 2, P])
+            words = diff[q, v][:].rearrange("p u w e -> p (u w e)").bitcast(F32)
+            for u in range(2):
+                nc.tensor.transpose(c_turned[q, v - v % 2][:, v % 2, u, :], words[:, u * P : (u + 1) * P], ident[:])
+
+        def stage_pass(q, v):
+            c_staged[q, v] = streamed([P, P, 4], BF16, "cst", PIECE_BUFS)
+            copy_words("s", c_staged[q, v][:], c_turned[q, v - v % 2][:, v % 2 : v % 2 + 1, :, :])
 
         def quant_c(q, v, n=2, half=None):
             if q not in c_codes:
@@ -189,8 +200,8 @@ def tile_dpo_like_hidden_step_s11_kernel(tc, h, r, beta, p_chosen, p_rejected, u
             moving = ut_codes[v][:, 2 * lo : 2 * (lo + W)].bitcast(FP4X4), ut_sc[:, v, lo : lo + W]
             mx_pass(b_acc[q // 2, j][:, q % 2, :], fp8(c_codes[q], c_scales[q], v * P, P), moving, first, last)
 
-        def sweep(q, v):
-            for j in range(NB):
+        def sweep(q, v, js=range(NB)):
+            for j in js:
                 pass_b(q, v, j, (q, v) == (0, 0), (q, v) == (1, NV - 1))
 
         def blocks(q, js, vs=range(NV)):
@@ -226,18 +237,25 @@ def tile_dpo_like_hidden_step_s11_kernel(tc, h, r, beta, p_chosen, p_rejected, u
         def quant_r(k, g=None):
             quantize(r_codes[k], r_scales[k], span(g, J), r_staged[k][:, span(g, J), :])
 
+        def sort_h():
+            dst = h_sorted[:].rearrange("p i u w e -> p i w u e")
+            move("v", dst, h_rows[0][:].rearrange("p i (w u e) -> p i w u e", u=2, e=2))
+
         def turn_h(b, banks):
             for k in range(ND):
                 h_turned[k, b] = bank(banks[k], [P, 2, 2, P])
                 for i in range(2):
-                    words = h_rows[b][:, i, :].bitcast(F32)
                     for u in range(2):
-                        nc.tensor.transpose(h_turned[k, b][:, i, u, :], words[:, 256 * k + u : 256 * (k + 1) : 2], ident[:])
+                        if b == 0:
+                            words = h_sorted[:, i, u, P * k : P * (k + 1), :].rearrange("p w e -> p (w e)").bitcast(F32)
+                        else:
+                            words = h_rows[b][:, i, :].bitcast(F32)[:, 256 * k + u : 256 * (k + 1) : 2]
+                        nc.tensor.transpose(h_turned[k, b][:, i, u, :], words, ident[:])
 
         def stage_h(k, b, eng="s"):
             if b == 0:
                 h_staged[k] = streamed([P, T, 4], BF16, "half", HALF_BUFS)
-            copy_words(eng, h_staged[k][:, span(b, T), :], h_turned[k, b])
+            copy_words(eng, h_staged[k][:, span(b, T), :], h_turned[k, b][:])
 
         def quant_h(k, b=None):
             quantize(h_codes[k], h_scales[k], span(b, T), h_staged[k][:, span(b, T), :])
@@ -278,7 +296,8 @@ def tile_dpo_like_hidden_step_s11_kernel(tc, h, r, beta, p_chosen, p_rejected, u
                     mx_pass(o_acc[i, c0][:, a, :], stationary, fp8(b_codes[g], b_scales[g], c0, n), g == 0, g == NJ - 1)
 
         def store(i, c0, eng, n=512, tiles=1):
-            tag, bufs = (("osb", OUT_BUFS), ("diff", PIECE_BUFS), ("cst", PIECE_BUFS))[len(stores) % 3]
+            free = (("diff", PIECE_BUFS), ("cst", PIECE_BUFS)) if len(stores) < 2 * PIECE_BUFS else (("pc", P_BUFS), ("pr", P_BUFS))
+            tag, bufs = free[len(stores) % 2]
             stores.append(tag)
             x = streamed([P, tiles, n], F32, tag, bufs)
             move(eng, x[:], o_acc[i, c0][:])
@@ -325,29 +344,37 @@ def tile_dpo_like_hidden_step_s11_kernel(tc, h, r, beta, p_chosen, p_rejected, u
         sweep(0, 1)
         quant_c(1, 0, 1)
         sweep(1, 0)
-        ready(0, 2, 0)
+        for v in (2, 3):
+            sub(0, v, 1)
+        quant_c(1, 1, 1)
+        for v in (2, 3):
+            sub(1, v, 1)
+        for q in range(2):
+            for v in (2, 3):
+                turn_pass(q, v, q)
+            for v in (2, 3):
+                stage_pass(q, v)
+            sweep(1, 1, range(3 * q, 3 * q + 3))
         load_tile(3)
         load_r(0)
-        quant_c(1, 1, 1)
-        sweep(1, 1)
-        ready(1, 2, 1, 1)
-        ready(1, 3, 0, 1)
         load_p(4)
         load_h(0)
-        load_r(1, 0)
-        quant_c(0, 2)
+        for v in (2, 3):
+            quant_c(0, v, 1)
         sweep(0, 2)
         quant_c(1, 2, 1)
+        sub(2, 0)
         quant_c(1, 3, 1)
         sweep(1, 2)
-        ready(2, 0, 1)
+        turn_c(2, 0, 0)
+        stage_c(2, 0)
         for j in ALL_J:
             pass_b(0, 3, j, False, False)
             pass_b(1, 3, j, False, True)
         sub(2, 2)
-        load_tile(5)
-        load_r(1, 1)
-        turn_c(2, 2, 0)
+        load_p(5)
+        load_r(1)
+        turn_c(2, 2, 1)
         quant_c(2, 0)
         for j in ALL_J:
             copy_b(0, j, "ssvvss"[j])
@@ -359,7 +386,7 @@ def tile_dpo_like_hidden_step_s11_kernel(tc, h, r, beta, p_chosen, p_rejected, u
         blocks(2, ALL_J, FIRST_V)
         quant_c(2, 2)
         for v in (0, 2):
-            turn_c(3, v, 1 - v // 2)
+            turn_c(3, v, v // 2)
         for v in (0, 2):
             stage_c(3, v)
         blocks(2, ALL_J, LAST_V)
@@ -370,59 +397,57 @@ def tile_dpo_like_hidden_step_s11_kernel(tc, h, r, beta, p_chosen, p_rejected, u
         weave_r(0, 0, "v", 1)
 
         first_blocks(3)
-        blocks(3, (3, 4, 5))
+        blocks(3, (3, 4))
         weave_r(0, 1, "v", 1)
         sub(4, 0, NV)
         load_p(7)
         load_r(2)
         load_h(1)
         load_beta()
-        quant_r(0)
-        weave_r(1, 0, "v", 0)
+        sort_h()
         for j in range(4):
             copy_b(1, j)
-        turn_tile(4)
+        turn_c(4, 0, 0, NV)
+        stage_c(4, 0, NV, (0,), "v")
+        stage_c(4, 0, NV, (2,))
         turn_h(0, (2, 3, 4))
+        blocks(3, (5,))
         for a in range(2):
             quant_c(4, 0, NV, a)
             stage_h(a, 0)
         copy_b(1, 4)
         stage_h(2, 0)
         copy_b(1, 5)
-        sub(5, 0)
-        sub(5, 2)
+        sub(5, 0, NV)
 
         blocks(4, (3, 0), FIRST_V)
         blocks(4, (3, 0), LAST_V)
         blocks(4, (1,))
-        for v in (0, 2):
-            turn_c(5, v, v // 2)
-        for v in (0, 2):
-            stage_c(5, v)
+        turn_tile(5)
         blocks(4, (2, 4, 5))
-        weave_r(1, 1, "s", 0)
-        weave_b(0, 1024, 512, "s", 0)
-        weave_r(1, 0, "v", 1)
-        weave_b(0, 0, 1024)
-        quant_h(0, 0)
-        quant_c(5, 0)
-        quant_c(5, 2)
+        weave_r(1, 1, "s")
+        quant_r(0)
+        weave_r(1, 0)
+        quant_c(5, 0, NV, 0)
+        quant_c(5, 0, NV, 1)
 
         first_blocks(5)
         sub(6, 0, NV)
-        for j in (0, 1):
-            copy_b(2, j)
+        copy_b(2, 0)
         turn_tile(6)
         blocks(5, (3, 4, 5))
-        weave_r(1, 1, "v", 1)
-        quant_b(0, 0, 1024)
+        weave_b(0, 0, 1024)
+        quant_h(0, 0)
+        quant_b(0, 0, 512)
         quant_c(6, 0, NV, 0)
         quant_c(6, 0, NV, 1)
-        for j in range(2, NB):
+        for j in range(1, NB):
             copy_b(2, j)
         sub(7, 0, NV)
 
-        first_blocks(6)
+        blocks(6, (0, 1), FIRST_V)
+        blocks(6, (0, 1), LAST_V)
+        blocks(6, (2,))
         turn_tile(7)
         turn_h(1, (6, 7, 0))
         blocks(6, (3,))
@@ -434,11 +459,12 @@ def tile_dpo_like_hidden_step_s11_kernel(tc, h, r, beta, p_chosen, p_rejected, u
         quant_h(2, 0)
         for k in range(ND):
             stage_h(k, 1)
-        weave_b(0, 1024, 512, "s", 1)
+        weave_b(0, 1024, 512, "s", 0)
         quant_r(2, 0)
         weave_r(2, 1)
-        quant_h(0, 1)
+        quant_b(0, 512, 512)
         quant_r(2, 1)
+        quant_h(0, 1)
         for k in (1, 2):
             quant_h(k, 1)
 
@@ -455,6 +481,7 @@ def tile_dpo_like_hidden_step_s11_kernel(tc, h, r, beta, p_chosen, p_rejected, u
                 if (g, b) == (0, 0):
                     copy_b(3, 3)
         weave_b(1, 0, 512)
+        weave_b(0, 1024, 512, "v", 1)
         times_beta(0, 0)
         quant_b(1, 0, 512)
         times_beta(1, 0)

@@ -26,7 +26,7 @@ P_BUFS = 3
 PIECE_BUFS = 4
 C_BUFS = 3
 STAGE_BUFS = 3
-HALF_BUFS = 3
+HALF_BUFS = 4
 
 
 def tile_dpo_like_hidden_step_s11_kernel(tc, h, r, beta, p_chosen, p_rejected, ut_words, ut_scales, out):
@@ -57,8 +57,8 @@ def tile_dpo_like_hidden_step_s11_kernel(tc, h, r, beta, p_chosen, p_rejected, u
         r_rows = {}
         h_rows = [kept([P, 2, D], BF16, "hraw%d" % b) for b in range(2)]
         h_sorted = kept([P, 2, 2, D // 4, 2], BF16, "hre")
-        h_codes = [kept([P, T], U32, "hc%d" % k) for k in range(ND)]
-        h_scales = [kept([P, T], U8, "hs%d" % k) for k in range(ND)]
+        h_codes = [kept([P, ND * 256], U32, "hc%d" % b) for b in range(2)]
+        h_scales = [kept([P, ND * 256], U8, "hs%d" % b) for b in range(2)]
         r_codes = [kept([P, J], U32, "rc%d" % k) for k in range(ND)]
         r_scales = [kept([P, J], U8, "rs%d" % k) for k in range(ND)]
         a_codes = [kept([P, T], U32, "ac%d" % g) for g in range(NJ)]
@@ -133,7 +133,7 @@ def tile_dpo_like_hidden_step_s11_kernel(tc, h, r, beta, p_chosen, p_rejected, u
                     r_rows[k, a] = x[:]
 
         def load_h(b):
-            nc.sync.dma_start(out=h_rows[b][:], in_=h[256 * b : 256 * (b + 1), :].rearrange("(p i) k -> p i k", i=2))
+            nc.sync.dma_start(out=h_rows[b][:], in_=h[256 * b : 256 * (b + 1), :].rearrange("(i p) k -> p i k", p=P))
 
         def load_beta():
             nc.sync.dma_start(out=beta_sb[:], in_=beta.rearrange("(g p t) -> p g t", g=NJ, t=4))
@@ -237,28 +237,33 @@ def tile_dpo_like_hidden_step_s11_kernel(tc, h, r, beta, p_chosen, p_rejected, u
         def quant_r(k, g=None):
             quantize(r_codes[k], r_scales[k], span(g, J), r_staged[k][:, span(g, J), :])
 
-        def sort_h():
-            dst = h_sorted[:].rearrange("p i u w e -> p i w u e")
-            move("v", dst, h_rows[0][:].rearrange("p i (w u e) -> p i w u e", u=2, e=2))
+        def sort_h(i):
+            dst = h_sorted[:, i, :, :, :].rearrange("p u w e -> p w u e")
+            move("v", dst, h_rows[0][:, i, :].rearrange("p (w u e) -> p w u e", u=2, e=2))
 
         def turn_h(b, banks):
             for k in range(ND):
                 h_turned[k, b] = bank(banks[k], [P, 2, 2, P])
+            if b == 0:
                 for i in range(2):
-                    for u in range(2):
-                        if b == 0:
+                    for k in range(ND):
+                        for u in range(2):
                             words = h_sorted[:, i, u, P * k : P * (k + 1), :].rearrange("p w e -> p (w e)").bitcast(F32)
-                        else:
+                            nc.tensor.transpose(h_turned[k, b][:, i, u, :], words, ident[:])
+            else:
+                for k in range(ND):
+                    for i in range(2):
+                        for u in range(2):
                             words = h_rows[b][:, i, :].bitcast(F32)[:, 256 * k + u : 256 * (k + 1) : 2]
-                        nc.tensor.transpose(h_turned[k, b][:, i, u, :], words, ident[:])
+                            nc.tensor.transpose(h_turned[k, b][:, i, u, :], words, ident[:])
 
         def stage_h(k, b, eng="s"):
-            if b == 0:
-                h_staged[k] = streamed([P, T, 4], BF16, "half", HALF_BUFS)
-            copy_words(eng, h_staged[k][:, span(b, T), :], h_turned[k, b][:])
+            if k != 1:
+                h_staged[k, b] = streamed([P, 512 if k == 0 else 256, 4], BF16, "half", HALF_BUFS)
+            copy_words(eng, h_staged[k - k % 2, b][:, 256 * (k % 2) : 256 * (k % 2 + 1), :], h_turned[k, b][:])
 
-        def quant_h(k, b=None):
-            quantize(h_codes[k], h_scales[k], span(b, T), h_staged[k][:, span(b, T), :])
+        def quant_h(k, b):
+            quantize(h_codes[b], h_scales[b], slice(256 * k, 512 if k == 0 else 768), h_staged[k, b][:])
 
         m_acc, sig, a_staged = {}, {}, {}
 
@@ -267,7 +272,7 @@ def tile_dpo_like_hidden_step_s11_kernel(tc, h, r, beta, p_chosen, p_rejected, u
             for e in range(2):
                 for k in range(ND):
                     stationary = fp8(r_codes[k], r_scales[k], g * 512 + (2 * w + e) * P, P)
-                    mx_pass(m_acc[g, b, w][:, e, :], stationary, fp8(h_codes[k], h_scales[k], 256 * b, 256), k == 0, k == ND - 1)
+                    mx_pass(m_acc[g, b, w][:, e, :], stationary, fp8(h_codes[b], h_scales[b], 256 * k, 256), k == 0, k == ND - 1)
 
         def sigmoid(g, b, w):
             if w == 0:
@@ -301,8 +306,7 @@ def tile_dpo_like_hidden_step_s11_kernel(tc, h, r, beta, p_chosen, p_rejected, u
             stores.append(tag)
             x = streamed([P, tiles, n], F32, tag, bufs)
             move(eng, x[:], o_acc[i, c0][:])
-            rows = out[256 * (i // 2) : 256 * (i // 2 + 1), c0 : c0 + n].rearrange("(p a) c -> p a c", a=2)
-            nc.sync.dma_start(out=rows[:, i % 2 : i % 2 + tiles, :], in_=x[:])
+            nc.sync.dma_start(out=out[i * P : (i + tiles) * P, c0 : c0 + n].rearrange("(a p) c -> p a c", a=tiles), in_=x[:])
 
         ALL_J, FIRST_V, LAST_V = range(NB), (0, 1), (2, 3)
 
@@ -343,7 +347,7 @@ def tile_dpo_like_hidden_step_s11_kernel(tc, h, r, beta, p_chosen, p_rejected, u
         ready(1, 1, 1, 1)
         sweep(0, 1)
         quant_c(1, 0, 1)
-        sweep(1, 0)
+        sweep(1, 0, (0, 1, 2))
         for v in (2, 3):
             sub(0, v, 1)
         quant_c(1, 1, 1)
@@ -354,7 +358,9 @@ def tile_dpo_like_hidden_step_s11_kernel(tc, h, r, beta, p_chosen, p_rejected, u
                 turn_pass(q, v, q)
             for v in (2, 3):
                 stage_pass(q, v)
-            sweep(1, 1, range(3 * q, 3 * q + 3))
+            if q == 0:
+                sweep(1, 0, (3, 4, 5))
+            sweep(1, 1, ((0, 1), (2, 3, 4, 5))[q])
         load_tile(3)
         load_r(0)
         load_p(4)
@@ -401,10 +407,11 @@ def tile_dpo_like_hidden_step_s11_kernel(tc, h, r, beta, p_chosen, p_rejected, u
         weave_r(0, 1, "v", 1)
         sub(4, 0, NV)
         load_p(7)
-        load_r(2)
         load_h(1)
+        load_r(2)
         load_beta()
-        sort_h()
+        for i in range(2):
+            sort_h(i)
         for j in range(4):
             copy_b(1, j)
         turn_c(4, 0, 0, NV)
@@ -425,7 +432,7 @@ def tile_dpo_like_hidden_step_s11_kernel(tc, h, r, beta, p_chosen, p_rejected, u
         blocks(4, (1,))
         turn_tile(5)
         blocks(4, (2, 4, 5))
-        weave_r(1, 1, "s")
+        weave_r(1, 1, "s", 0)
         quant_r(0)
         weave_r(1, 0)
         quant_c(5, 0, NV, 0)
@@ -437,8 +444,8 @@ def tile_dpo_like_hidden_step_s11_kernel(tc, h, r, beta, p_chosen, p_rejected, u
         turn_tile(6)
         blocks(5, (3, 4, 5))
         weave_b(0, 0, 1024)
-        quant_h(0, 0)
-        quant_b(0, 0, 512)
+        weave_r(1, 1, "v", 1)
+        quant_h(2, 0)
         quant_c(6, 0, NV, 0)
         quant_c(6, 0, NV, 1)
         for j in range(1, NB):
@@ -451,22 +458,22 @@ def tile_dpo_like_hidden_step_s11_kernel(tc, h, r, beta, p_chosen, p_rejected, u
         turn_tile(7)
         turn_h(1, (6, 7, 0))
         blocks(6, (3,))
-        weave_r(2, 0)
         quant_r(1)
+        quant_h(0, 0)
+        weave_r(2, 0, "v", 0)
         quant_c(7, 0, NV, 0)
-        quant_h(1, 0)
         quant_c(7, 0, NV, 1)
-        quant_h(2, 0)
+        weave_r(2, 0, "v", 1)
         for k in range(ND):
             stage_h(k, 1)
         weave_b(0, 1024, 512, "s", 0)
+        weave_r(2, 1, "v", 0)
         quant_r(2, 0)
-        weave_r(2, 1)
-        quant_b(0, 512, 512)
-        quant_r(2, 1)
+        weave_r(2, 1, "v", 1)
         quant_h(0, 1)
-        for k in (1, 2):
-            quant_h(k, 1)
+        quant_r(2, 1)
+        quant_h(2, 1)
+        quant_b(0, 0, 1024)
 
         first_blocks(7)
         blocks(7, (3,))
@@ -480,8 +487,9 @@ def tile_dpo_like_hidden_step_s11_kernel(tc, h, r, beta, p_chosen, p_rejected, u
                     sigmoid(g, b, w)
                 if (g, b) == (0, 0):
                     copy_b(3, 3)
+                if (g, b) == (1, 0):
+                    weave_b(0, 1024, 512, "s", 1)
         weave_b(1, 0, 512)
-        weave_b(0, 1024, 512, "v", 1)
         times_beta(0, 0)
         quant_b(1, 0, 512)
         times_beta(1, 0)
@@ -507,9 +515,6 @@ def tile_dpo_like_hidden_step_s11_kernel(tc, h, r, beta, p_chosen, p_rejected, u
         for i, c0 in ((0, 512), (1, 512), (2, 0), (3, 0), (2, 512)):
             result(i, c0)
             store(i, c0, "s")
-        for i, c0, eng in ((3, 512, "v"), (0, 1024, "s"), (1, 1024, "v"), (2, 1024, "s")):
+        for i, c0, eng in ((3, 512, "v"), (0, 1024, "s"), (1, 1024, "v"), (2, 1024, "s"), (3, 1024, "v")):
             result(i, c0)
             store(i, c0, eng)
-        for c0, eng in ((1024, "v"), (1280, "s")):
-            result(3, c0, W)
-            store(3, c0, eng, W)

@@ -96,20 +96,20 @@ def tile_dpo_like_hidden_step_s11_kernel(tc, h, r, beta, p_chosen, p_rejected, u
             g, t = divmod(q, 4)
             return src[g * 512 : (g + 1) * 512, :].rearrange("(m t) v -> m t v", t=4)[:, t, :]
 
+        def load_part(q, src, a):
+            tiles, tag = (pc, "pc") if src is p_chosen else (pr, "pr")
+            if q not in tiles:
+                tiles[q] = streamed([P, V], BF16, tag, P_BUFS)
+            nc.sync.dma_start(out=tiles[q][:, span(a, V)], in_=tile_rows(src, q)[:, span(a, V)])
+
         def load_p(q, a=None):
-            if q not in pc:
-                pc[q] = streamed([P, V], BF16, "pc", P_BUFS)
-                pr[q] = streamed([P, V], BF16, "pr", P_BUFS)
-            cols = span(a, V)
-            nc.sync.dma_start(out=pc[q][:, cols], in_=tile_rows(p_chosen, q)[:, cols])
-            nc.sync.dma_start(out=pr[q][:, cols], in_=tile_rows(p_rejected, q)[:, cols])
+            for src in (p_chosen, p_rejected):
+                load_part(q, src, a)
 
         def load_tile(q):
-            pc[q] = streamed([P, V], BF16, "pc", P_BUFS)
-            pr[q] = streamed([P, V], BF16, "pr", P_BUFS)
-            nc.sync.dma_start(out=pc[q][:], in_=tile_rows(p_chosen, q))
+            load_part(q, p_chosen, None)
             for a in range(2):
-                nc.sync.dma_start(out=pr[q][:, span(a, V)], in_=tile_rows(p_rejected, q)[:, span(a, V)])
+                load_part(q, p_rejected, a)
 
         def load_ut(v):
             nc.sync.dma_start(out=ut_codes[v][:].bitcast(I32), in_=ut_words[v].bitcast(I32))
@@ -334,9 +334,10 @@ def tile_dpo_like_hidden_step_s11_kernel(tc, h, r, beta, p_chosen, p_rejected, u
         load_p(0, 1)
         load_p(1, 1)
         load_ut(2)
-        load_p(2, 0)
+        load_part(2, p_chosen, None)
+        load_part(2, p_rejected, 0)
+        load_part(2, p_rejected, 1)
         load_ut(3)
-        load_p(2, 1)
 
         ready(0, 0, 0, 1)
         ready(0, 1, 1, 1)
@@ -370,32 +371,32 @@ def tile_dpo_like_hidden_step_s11_kernel(tc, h, r, beta, p_chosen, p_rejected, u
         sweep(0, 2)
         quant_c(1, 2, 1)
         sub(2, 0)
+        sub(2, 2)
         quant_c(1, 3, 1)
         sweep(1, 2)
-        turn_c(2, 0, 0)
-        stage_c(2, 0)
+        for v in (0, 2):
+            turn_c(2, v, v // 2)
+            stage_c(2, v, eng="sv"[v // 2])
+        load_p(5)
+        load_r(1)
         for j in ALL_J:
             pass_b(0, 3, j, False, False)
             pass_b(1, 3, j, False, True)
-        sub(2, 2)
-        load_p(5)
-        load_r(1)
-        turn_c(2, 2, 1)
-        quant_c(2, 0)
-        for j in ALL_J:
-            copy_b(0, j, "ssvvss"[j])
-        stage_c(2, 2)
-        sub(3, 0)
-        sub(3, 2)
-        load_p(6)
+        for v in (0, 2):
+            quant_c(2, v)
+        for j in range(5):
+            copy_b(0, j)
 
-        blocks(2, ALL_J, FIRST_V)
-        quant_c(2, 2)
+        blocks(2, (0, 1, 2))
+        for v in (0, 2):
+            sub(3, v)
+        load_p(6)
+        copy_b(0, 5, "v")
         for v in (0, 2):
             turn_c(3, v, v // 2)
         for v in (0, 2):
             stage_c(3, v)
-        blocks(2, ALL_J, LAST_V)
+        blocks(2, (3, 4, 5))
         weave_r(0, 0, "v", 0)
         weave_r(0, 1, "s", 0)
         for v in (0, 2):

@@ -22,10 +22,12 @@ ND = D // 512
 NJ = J // 512
 W = 256
 NB = D // W
+MOVING_SCALES, STATIONARY_CODES, STATIONARY_SCALES = 128, 64, 192
 P_BUFS = 3
 PIECE_BUFS = 4
 C_BUFS = 3
 STAGE_BUFS = 3
+R_BUFS = 2
 HALF_BUFS = 4
 
 
@@ -45,26 +47,36 @@ def tile_dpo_like_hidden_step_s11_kernel(tc, h, r, beta, p_chosen, p_rejected, u
             x = work.tile(shape, dtype, name=tag, tag=tag, bufs=bufs, align_bytes=align)
             return x
 
+        def shifted(cols, dtype, name, shift, tag_bufs=None):
+            size = 4 if dtype == U32 else 1
+            shape = [P, cols + 256 // size]
+            x = kept(shape, dtype, name, 256) if tag_bufs is None else streamed(shape, dtype, name, tag_bufs, 256)
+            return x[:, shift // size : shift // size + cols]
+
+        def shifted_row(n, cols, dtype, name, shift):
+            x = shifted(n * cols, dtype, name, shift)
+            return [x[:, a * cols : (a + 1) * cols] for a in range(n)]
+
         def bank(b, shape):
             x = psum.tile(shape, F32, name="bank%d" % b, tag="bank%d" % b)
             return x
 
         ident = kept([P, P], F32, "ident")
         beta_sb = kept([P, NJ, 4], BF16, "beta_sb")
-        ut_sc = kept([P, NV, D], U8, "usc", 256)
-        ut_codes = [kept([P, 2 * D], U8, "ut%d" % v) for v in range(NV)]
+        ut_sc = shifted(NV * D, U8, "usc", MOVING_SCALES).rearrange("p (v n) -> p v n", v=NV)
+        ut_codes = [kept([P, 2 * D], U8, "ut%d" % v, 256) for v in range(NV)]
         b_pairs = [kept([P, 2, D, 2], BF16, "bp%d" % g) for g in range(NJ)]
         r_rows = {}
         h_rows = [kept([P, 2, D], BF16, "hraw%d" % b) for b in range(2)]
         h_sorted = kept([P, 2, 2, D // 4, 2], BF16, "hre")
-        h_codes = [kept([P, ND * 256], U32, "hc%d" % b) for b in range(2)]
-        h_scales = [kept([P, ND * 256], U8, "hs%d" % b) for b in range(2)]
-        r_codes = [kept([P, J], U32, "rc%d" % k) for k in range(ND)]
-        r_scales = [kept([P, J], U8, "rs%d" % k) for k in range(ND)]
-        a_codes = [kept([P, T], U32, "ac%d" % g) for g in range(NJ)]
-        a_scales = [kept([P, T], U8, "as%d" % g) for g in range(NJ)]
-        b_codes = [kept([P, D], U32, "bc%d" % g) for g in range(NJ)]
-        b_scales = [kept([P, D], U8, "bs%d" % g) for g in range(NJ)]
+        h_codes = [kept([P, ND * 256], U32, "hc%d" % b, 256) for b in range(2)]
+        h_scales = shifted_row(2, ND * 256, U8, "hs", MOVING_SCALES)
+        r_codes = shifted_row(ND, J, U32, "rc", STATIONARY_CODES)
+        r_scales = shifted_row(ND, J, U8, "rs", STATIONARY_SCALES)
+        a_codes = shifted_row(NJ, T, U32, "ac", STATIONARY_CODES)
+        a_scales = shifted_row(NJ, T, U8, "as", STATIONARY_SCALES)
+        b_codes = [kept([P, D], U32, "bc%d" % g, 256) for g in range(NJ)]
+        b_scales = shifted_row(NJ, D, U8, "bs", MOVING_SCALES)
 
         def move(eng, dst, src):
             if eng == "s":
@@ -114,9 +126,6 @@ def tile_dpo_like_hidden_step_s11_kernel(tc, h, r, beta, p_chosen, p_rejected, u
         def load_ut(v):
             nc.sync.dma_start(out=ut_codes[v][:].bitcast(I32), in_=ut_words[v].bitcast(I32))
 
-        def zero_scales():
-            nc.vector.memset(ut_sc[:].bitcast(I32), 0)
-
         def load_scales():
             for i in range(4):
                 src = ut_scales[:, i:16:4, :].rearrange("g q n -> q g n")
@@ -124,7 +133,7 @@ def tile_dpo_like_hidden_step_s11_kernel(tc, h, r, beta, p_chosen, p_rejected, u
 
         def load_r(k, g=None):
             cols = span(g, J)
-            x = kept([P, 4, cols.stop - cols.start], BF16, "rraw%d%s" % (k, g))
+            x = streamed([P, 4, cols.stop - cols.start], BF16, "rraw", R_BUFS)
             nc.sync.dma_start(out=x[:], in_=r[k * 512 : (k + 1) * 512, cols].rearrange("(p j) c -> p j c", j=4))
             for a in range(NJ):
                 if g is None:
@@ -182,8 +191,8 @@ def tile_dpo_like_hidden_step_s11_kernel(tc, h, r, beta, p_chosen, p_rejected, u
 
         def quant_c(q, v, n=2, half=None):
             if q not in c_codes:
-                c_codes[q] = streamed([P, NV * P], U32, "cc", C_BUFS, 256)
-                c_scales[q] = streamed([P, NV * P], U8, "cs", C_BUFS, 256)
+                c_codes[q] = shifted(NV * P, U32, "cc", STATIONARY_CODES, C_BUFS)
+                c_scales[q] = shifted(NV * P, U8, "cs", STATIONARY_SCALES, C_BUFS)
             cols = span(half, n * P)
             quantize(c_codes[q], c_scales[q], slice(v * P + cols.start, v * P + cols.stop), c_staged[q, v][:, cols, :])
 
@@ -324,7 +333,6 @@ def tile_dpo_like_hidden_step_s11_kernel(tc, h, r, beta, p_chosen, p_rejected, u
             blocks(q, (0, 1, 2), LAST_V)
 
         make_identity(nc, ident[:])
-        zero_scales()
         load_p(0, 0)
         load_scales()
         warm_table()

@@ -22,7 +22,7 @@ ND = D // 512
 NJ = J // 512
 W = 256
 NB = D // W
-MOVING_SCALES, STATIONARY_CODES, STATIONARY_SCALES = 128, 64, 192
+B_RUNS = (((0, 1024), (1024, 512)), ((0, 512), (512, 512), (1024, 512)))
 P_BUFS = 3
 PIECE_BUFS = 4
 C_BUFS = 3
@@ -47,36 +47,31 @@ def tile_dpo_like_hidden_step_s11_kernel(tc, h, r, beta, p_chosen, p_rejected, u
             x = work.tile(shape, dtype, name=tag, tag=tag, bufs=bufs, align_bytes=align)
             return x
 
-        def shifted(cols, dtype, name, shift, tag_bufs=None):
-            size = 4 if dtype == U32 else 1
-            shape = [P, cols + 256 // size]
-            x = kept(shape, dtype, name, 256) if tag_bufs is None else streamed(shape, dtype, name, tag_bufs, 256)
-            return x[:, shift // size : shift // size + cols]
-
-        def shifted_row(n, cols, dtype, name, shift):
-            x = shifted(n * cols, dtype, name, shift)
-            return [x[:, a * cols : (a + 1) * cols] for a in range(n)]
-
         def bank(b, shape):
             x = psum.tile(shape, F32, name="bank%d" % b, tag="bank%d" % b)
             return x
 
         ident = kept([P, P], F32, "ident")
         beta_sb = kept([P, NJ, 4], BF16, "beta_sb")
-        ut_sc = shifted(NV * D, U8, "usc", MOVING_SCALES).rearrange("p (v n) -> p v n", v=NV)
-        ut_codes = [kept([P, 2 * D], U8, "ut%d" % v, 256) for v in range(NV)]
-        b_pairs = [kept([P, 2, D, 2], BF16, "bp%d" % g) for g in range(NJ)]
+        ut_sc = kept([P, NV, D], U8, "usc", 256)
+        ut_codes = [kept([P, 2 * D], U8, "ut%d" % v) for v in range(NV)]
+        b_pairs = {}
+        for g, runs in enumerate(B_RUNS):
+            for lo, n in runs:
+                x = kept([P, 2, n, 2], BF16, "bp%d_%d" % (g, lo))
+                for at in range(0, n, W):
+                    b_pairs[g, lo + at] = x[:, :, at:n, :]
         r_rows = {}
         h_rows = [kept([P, 2, D], BF16, "hraw%d" % b) for b in range(2)]
         h_sorted = kept([P, 2, 2, D // 4, 2], BF16, "hre")
-        h_codes = [kept([P, ND * 256], U32, "hc%d" % b, 256) for b in range(2)]
-        h_scales = shifted_row(2, ND * 256, U8, "hs", MOVING_SCALES)
-        r_codes = shifted_row(ND, J, U32, "rc", STATIONARY_CODES)
-        r_scales = shifted_row(ND, J, U8, "rs", STATIONARY_SCALES)
-        a_codes = shifted_row(NJ, T, U32, "ac", STATIONARY_CODES)
-        a_scales = shifted_row(NJ, T, U8, "as", STATIONARY_SCALES)
-        b_codes = [kept([P, D], U32, "bc%d" % g, 256) for g in range(NJ)]
-        b_scales = shifted_row(NJ, D, U8, "bs", MOVING_SCALES)
+        h_codes = [kept([P, ND * 256], U32, "hc%d" % b) for b in range(2)]
+        h_scales = [kept([P, ND * 256], U8, "hs%d" % b) for b in range(2)]
+        r_codes = [kept([P, J], U32, "rc%d" % k) for k in range(ND)]
+        r_scales = [kept([P, J], U8, "rs%d" % k) for k in range(ND)]
+        a_codes = [kept([P, T], U32, "ac%d" % g) for g in range(NJ)]
+        a_scales = [kept([P, T], U8, "as%d" % g) for g in range(NJ)]
+        b_codes = [kept([P, D], U32, "bc%d" % g) for g in range(NJ)]
+        b_scales = [kept([P, D], U8, "bs%d" % g) for g in range(NJ)]
 
         def move(eng, dst, src):
             if eng == "s":
@@ -191,8 +186,8 @@ def tile_dpo_like_hidden_step_s11_kernel(tc, h, r, beta, p_chosen, p_rejected, u
 
         def quant_c(q, v, n=2, half=None):
             if q not in c_codes:
-                c_codes[q] = shifted(NV * P, U32, "cc", STATIONARY_CODES, C_BUFS)
-                c_scales[q] = shifted(NV * P, U8, "cs", STATIONARY_SCALES, C_BUFS)
+                c_codes[q] = streamed([P, NV * P], U32, "cc", C_BUFS, 256)
+                c_scales[q] = streamed([P, NV * P], U8, "cs", C_BUFS, 256)
             cols = span(half, n * P)
             quantize(c_codes[q], c_scales[q], slice(v * P + cols.start, v * P + cols.stop), c_staged[q, v][:, cols, :])
 
@@ -219,7 +214,7 @@ def tile_dpo_like_hidden_step_s11_kernel(tc, h, r, beta, p_chosen, p_rejected, u
                     pass_b(q, v, j, v == 0, v == NV - 1)
 
         def copy_b(pair, j, eng="s"):
-            dst = b_pairs[pair // 2][:, pair % 2, W * j : W * (j + 1), :]
+            dst = b_pairs[pair // 2, W * j][:, pair % 2, 0:W, :]
             move(eng, dst.rearrange("p (n i) e -> p n e i", i=2), b_acc[pair, j][:].rearrange("p e (n i) -> p n e i", i=2))
 
         def weave_b(g, lo, n, eng="v", half=None):
@@ -227,9 +222,9 @@ def tile_dpo_like_hidden_step_s11_kernel(tc, h, r, beta, p_chosen, p_rejected, u
                 x = kept([P, n, 4], BF16, "late") if eng == "s" else streamed([P, n, 4], BF16, "stage", STAGE_BUFS)
                 for at in range(0, n, W):
                     b_staged[g, lo + at] = x[:, at:n, :]
-            dst = b_staged[g, lo][:, span(half, n), :].rearrange("p (n i) (u e) -> p n u i e", u=2, i=2)
-            src = b_pairs[g][:, :, lo : lo + n, :][:, :, span(half, n), :]
-            move(eng, dst, src.rearrange("p u (n i) e -> p n u i e", i=2))
+            dst = b_staged[g, lo][:, span(half, n), :].bitcast(F32)
+            src = b_pairs[g, lo][:, :, span(half, n), :].rearrange("p u n e -> p u (n e)").bitcast(F32)
+            move(eng, dst, src.rearrange("p u n -> p n u"))
 
         def quant_b(g, lo, n):
             quantize(b_codes[g], b_scales[g], slice(lo, lo + n), b_staged[g, lo][:, 0:n, :])
@@ -247,8 +242,9 @@ def tile_dpo_like_hidden_step_s11_kernel(tc, h, r, beta, p_chosen, p_rejected, u
             quantize(r_codes[k], r_scales[k], span(g, J), r_staged[k][:, span(g, J), :])
 
         def sort_h(i):
-            dst = h_sorted[:, i, :, :, :].rearrange("p u w e -> p w u e")
-            move("v", dst, h_rows[0][:, i, :].rearrange("p (w u e) -> p w u e", u=2, e=2))
+            dst = h_sorted[:, i, :, :, :].rearrange("p u w e -> p u (w e)").bitcast(F32)
+            src = h_rows[0][:, i, :].bitcast(F32)
+            move("v", dst.rearrange("p u (a c) -> p a u c", c=4), src.rearrange("p (a c u) -> p a u c", c=4, u=2))
 
         def turn_h(b, banks):
             for k in range(ND):

@@ -215,7 +215,7 @@ def tile_dpo_like_hidden_step_s11_kernel(tc, h, r, beta, p_chosen, p_rejected, u
 
         def copy_b(pair, j, eng="s"):
             dst = b_pairs[pair // 2, W * j][:, pair % 2, 0:W, :]
-            move(eng, dst.rearrange("p (n i) e -> p n e i", i=2), b_acc[pair, j][:].rearrange("p e (n i) -> p n e i", i=2))
+            move(eng, dst, b_acc[pair, j][:].rearrange("p e n -> p n e"))
 
         def weave_b(g, lo, n, eng="v", half=None):
             if not half:

from contextlib import ExitStack

import concourse.mybir as mybir
from concourse.masks import make_identity

T, D, J, V = 512, 1536, 1024, 2048
P = 128
FLOPS = 2 * (T * D * J + J * V * D + T * J * D)

F32 = mybir.dt.float32
BF16 = mybir.dt.bfloat16
I32 = mybir.dt.int32
U32 = mybir.dt.uint32
U8 = mybir.dt.uint8
FP8X4 = mybir.dt.float8_e4m3fn_x4
FP4X4 = mybir.dt.float4_e2m1fn_x4
ACT = mybir.ActivationFunctionType
ALU = mybir.AluOpType

NV = V // 512
ND = D // 512
NJ = J // 512
W = 256
NB = D // W
B_RUNS = (((0, 1024), (1024, 512)), ((0, 512), (512, 512), (1024, 512)))
P_BUFS = 3
PIECE_BUFS = 4
C_BUFS = 3
STAGE_BUFS = 3
R_BUFS = 2
HALF_BUFS = 4


def tile_dpo_like_hidden_step_s11_kernel(tc, h, r, beta, p_chosen, p_rejected, ut_words, ut_scales, out):
    nc = tc.nc
    with ExitStack() as ctx:
        keep = ctx.enter_context(tc.tile_pool(name="keep", bufs=1))
        work = ctx.enter_context(tc.tile_pool(name="work", bufs=2))
        psum = ctx.enter_context(tc.psum_pool(name="psum", bufs=1))
        ctx.enter_context(tc.manual_schedule())

        def kept(shape, dtype, name, align=64):
            x = keep.tile(shape, dtype, name=name, align_bytes=align)
            return x

        def streamed(shape, dtype, tag, bufs, align=64):
            x = work.tile(shape, dtype, name=tag, tag=tag, bufs=bufs, align_bytes=align)
            return x

        def bank(b, shape):
            x = psum.tile(shape, F32, name="bank%d" % b, tag="bank%d" % b)
            return x

        ident = kept([P, P], F32, "ident")
        beta_sb = kept([P, NJ, 4], BF16, "beta_sb")
        ut_sc = kept([P, NV, D], U8, "usc", 256)
        ut_codes = [kept([P, 2 * D], U8, "ut%d" % v) for v in range(NV)]
        b_pairs = {}
        for g, runs in enumerate(B_RUNS):
            for lo, n in runs:
                x = kept([P, 2, n, 2], BF16, "bp%d_%d" % (g, lo))
                for at in range(0, n, W):
                    b_pairs[g, lo + at] = x[:, :, at:n, :]
        r_rows = {}
        h_rows = [kept([P, 2, D], BF16, "hraw%d" % b) for b in range(2)]
        h_sorted = kept([P, 2, 2, D // 4, 2], BF16, "hre")
        h_codes = [kept([P, ND * 256], U32, "hc%d" % b) for b in range(2)]
        h_scales = [kept([P, ND * 256], U8, "hs%d" % b) for b in range(2)]
        r_codes = [kept([P, J], U32, "rc%d" % k) for k in range(ND)]
        r_scales = [kept([P, J], U8, "rs%d" % k) for k in range(ND)]
        a_codes = [kept([P, T], U32, "ac%d" % g) for g in range(NJ)]
        a_scales = [kept([P, T], U8, "as%d" % g) for g in range(NJ)]
        b_codes = [kept([P, D], U32, "bc%d" % g) for g in range(NJ)]
        b_scales = [kept([P, D], U8, "bs%d" % g) for g in range(NJ)]

        def move(eng, dst, src):
            if eng == "s":
                nc.scalar.copy(out=dst, in_=src)
            else:
                nc.vector.tensor_copy(out=dst, in_=src)

        def quantize(codes, scales, cols, staged):
            nc.vector.quantize_mx(out=codes[:, cols].bitcast(FP8X4), scales=scales[:, cols], in_=staged.rearrange("p c j -> p (c j)"))

        def mx_pass(dst, stationary, moving, first, last):
            nc.tensor.matmul_mx(
                out=dst, lhsT=stationary[0], lhsT_scale=stationary[1], rhs=moving[0], rhs_scale=moving[1], start=first, stop=last
            )

        def fp8(codes, scales, lo, n):
            return codes[:, lo : lo + n].bitcast(FP8X4), scales[:, lo : lo + n]

        def span(half, width):
            return slice(0, width) if half is None else slice(half * width // 2, (half + 1) * width // 2)

        def warm_table():
            x = streamed([P, 512, 4], BF16, "half", HALF_BUFS)
            nc.scalar.activation(out=x[:, 0:1, 0:1], in_=ident[:, 0:1].unsqueeze(2), func=ACT.Sigmoid)

        pc, pr = {}, {}

        def tile_rows(src, q):
            g, t = divmod(q, 4)
            return src[g * 512 : (g + 1) * 512, :].rearrange("(m t) v -> m t v", t=4)[:, t, :]

        def load_part(q, src, a):
            tiles, tag = (pc, "pc") if src is p_chosen else (pr, "pr")
            if q not in tiles:
                tiles[q] = streamed([P, V], BF16, tag, P_BUFS)
            nc.sync.dma_start(out=tiles[q][:, span(a, V)], in_=tile_rows(src, q)[:, span(a, V)])

        def load_p(q, a=None):
            for src in (p_chosen, p_rejected):
                load_part(q, src, a)

        def load_tile(q):
            load_part(q, p_chosen, None)
            for a in range(2):
                load_part(q, p_rejected, a)

        def load_ut(v):
            nc.sync.dma_start(out=ut_codes[v][:].bitcast(I32), in_=ut_words[v].bitcast(I32))

        def load_scales():
            for i in range(4):
                src = ut_scales[:, i:16:4, :].rearrange("g q n -> q g n")
                nc.sync.dma_start(out=ut_sc[i:P:32, :, :].bitcast(I32), in_=src.bitcast(I32))

        def load_r(k, g=None):
            cols = span(g, J)
            x = streamed([P, 4, cols.stop - cols.start], BF16, "rraw", R_BUFS)
            nc.sync.dma_start(out=x[:], in_=r[k * 512 : (k + 1) * 512, cols].rearrange("(p j) c -> p j c", j=4))
            for a in range(NJ):
                if g is None:
                    r_rows[k, a] = x[:, :, span(a, J)]
                elif a == g:
                    r_rows[k, a] = x[:]

        def load_h(b):
            nc.sync.dma_start(out=h_rows[b][:], in_=h[256 * b : 256 * (b + 1), :].rearrange("(i p) k -> p i k", p=P))

        def load_beta():
            nc.sync.dma_start(out=beta_sb[:], in_=beta.rearrange("(g p t) -> p g t", g=NJ, t=4))

        diff, c_turned, c_staged, c_codes, c_scales = {}, {}, {}, {}, {}

        def sub(q, v, n=2):
            diff[q, v] = streamed([P, 2, n * P, 2], BF16, "diff", PIECE_BUFS)
            cols = slice(512 * v, 512 * (v + n))
            nc.vector.tensor_tensor(
                out=diff[q, v][:].rearrange("p u w e -> p w u e"),
                in0=pc[q][:, cols].rearrange("p (w u e) -> p w u e", u=2, e=2),
                in1=pr[q][:, cols].rearrange("p (w u e) -> p w u e", u=2, e=2),
                op=ALU.subtract,
            )

        def turn_c(q, v, b, n=2):
            words = diff[q, v][:].rearrange("p u w e -> p (u w e)").bitcast(F32)
            for i in range(n):
                if i % 2 == 0:
                    c_turned[q, v + i] = bank(b + i // 2, [P, min(n, 2), 2, P])
                for u in range(2):
                    lo = (u * n + i) * P
                    nc.tensor.transpose(c_turned[q, v + i - i % 2][:, i % 2, u, :], words[:, lo : lo + P], ident[:])

        def copy_words(eng, dst, src):
            words = dst.rearrange("p c j -> p (c j)").bitcast(F32)
            move(eng, words.rearrange("p (i r u) -> p i r u", r=P, u=2), src.rearrange("p i u r -> p i r u"))

        def stage_c(q, v, n=2, banks=None, eng="s"):
            if (q, v) not in c_staged:
                c_staged[q, v] = streamed([P, n * P, 4], BF16, "cst", PIECE_BUFS)
            for i in banks or range(0, n, 2):
                copy_words(eng, c_staged[q, v][:, i * P : min(n, i + 2) * P, :], c_turned[q, v + i][:])

        def turn_pass(q, v, b):
            if v % 2 == 0:
                c_turned[q, v] = bank(b, [P, 2, 2, P])
            words = diff[q, v][:].rearrange("p u w e -> p (u w e)").bitcast(F32)
            for u in range(2):
                nc.tensor.transpose(c_turned[q, v - v % 2][:, v % 2, u, :], words[:, u * P : (u + 1) * P], ident[:])

        def stage_pass(q, v):
            c_staged[q, v] = streamed([P, P, 4], BF16, "cst", PIECE_BUFS)
            copy_words("s", c_staged[q, v][:], c_turned[q, v - v % 2][:, v % 2 : v % 2 + 1, :, :])

        def quant_c(q, v, n=2, half=None):
            if q not in c_codes:
                c_codes[q] = streamed([P, NV * P], U32, "cc", C_BUFS, 256)
                c_scales[q] = streamed([P, NV * P], U8, "cs", C_BUFS, 256)
            cols = span(half, n * P)
            quantize(c_codes[q], c_scales[q], slice(v * P + cols.start, v * P + cols.stop), c_staged[q, v][:, cols, :])

        b_acc, b_staged, late_sums = {}, {}, []

        def late_bank(shape):
            late_sums.append(shape)
            return bank((1, 6, 7, 0, 2, 3, 4, 5)[(len(late_sums) - 1) % 8], shape)

        def pass_b(q, v, j, first, last):
            if (q // 2, j) not in b_acc:
                b_acc[q // 2, j] = late_bank([P, 2, W]) if late_sums else bank(2 + j, [P, 2, W])
            lo = W * j
            moving = ut_codes[v][:, 2 * lo : 2 * (lo + W)].bitcast(FP4X4), ut_sc[:, v, lo : lo + W]
            mx_pass(b_acc[q // 2, j][:, q % 2, :], fp8(c_codes[q], c_scales[q], v * P, P), moving, first, last)

        def sweep(q, v, js=range(NB)):
            for j in js:
                pass_b(q, v, j, (q, v) == (0, 0), (q, v) == (1, NV - 1))

        def blocks(q, js, vs=range(NV)):
            for j in js:
                for v in vs:
                    pass_b(q, v, j, v == 0, v == NV - 1)

        def copy_b(pair, j, eng="s"):
            dst = b_pairs[pair // 2, W * j][:, pair % 2, 0:W, :]
            move(eng, dst, b_acc[pair, j][:].rearrange("p e n -> p n e"))

        def weave_b(g, lo, n, eng="v", half=None):
            if not half:
                x = kept([P, n, 4], BF16, "late") if eng == "s" else streamed([P, n, 4], BF16, "stage", STAGE_BUFS)
                for at in range(0, n, W):
                    b_staged[g, lo + at] = x[:, at:n, :]
            dst = b_staged[g, lo][:, span(half, n), :].bitcast(F32)
            src = b_pairs[g, lo][:, :, span(half, n), :].rearrange("p u n e -> p u (n e)").bitcast(F32)
            move(eng, dst, src.rearrange("p u n -> p n u"))

        def quant_b(g, lo, n):
            quantize(b_codes[g], b_scales[g], slice(lo, lo + n), b_staged[g, lo][:, 0:n, :])

        r_staged, h_turned, h_staged = {}, {}, {}

        def weave_r(k, g, eng="v", half=None):
            if k not in r_staged:
                r_staged[k] = streamed([P, J, 4], BF16, "stage", STAGE_BUFS)
            dst = r_staged[k][:, span(g, J), :].rearrange("p (t a b) j -> p a j b t", t=4, b=2)
            src = r_rows[k, g][:, :, span(half, 512)]
            move(eng, dst[:, span(half, 64), :, :, :], src.rearrange("p j (a b t) -> p a j b t", t=4, b=2))

        def quant_r(k, g=None):
            quantize(r_codes[k], r_scales[k], span(g, J), r_staged[k][:, span(g, J), :])

        def sort_h(i):
            dst = h_sorted[:, i, :, :, :].rearrange("p u w e -> p u (w e)").bitcast(F32)
            src = h_rows[0][:, i, :].bitcast(F32)
            move("v", dst.rearrange("p u (a c) -> p a u c", c=4), src.rearrange("p (a c u) -> p a u c", c=4, u=2))

        def turn_h(b, banks):
            for k in range(ND):
                h_turned[k, b] = bank(banks[k], [P, 2, 2, P])
            if b == 0:
                for i in range(2):
                    for k in range(ND):
                        for u in range(2):
                            words = h_sorted[:, i, u, P * k : P * (k + 1), :].rearrange("p w e -> p (w e)").bitcast(F32)
                            nc.tensor.transpose(h_turned[k, b][:, i, u, :], words, ident[:])
            else:
                for k in range(ND):
                    for i in range(2):
                        for u in range(2):
                            words = h_rows[b][:, i, :].bitcast(F32)[:, 256 * k + u : 256 * (k + 1) : 2]
                            nc.tensor.transpose(h_turned[k, b][:, i, u, :], words, ident[:])

        def stage_h(k, b, eng="s"):
            if k != 1:
                h_staged[k, b] = streamed([P, 512 if k == 0 else 256, 4], BF16, "half", HALF_BUFS)
            copy_words(eng, h_staged[k - k % 2, b][:, 256 * (k % 2) : 256 * (k % 2 + 1), :], h_turned[k, b][:])

        def quant_h(k, b):
            quantize(h_codes[b], h_scales[b], slice(256 * k, 512 if k == 0 else 768), h_staged[k, b][:])

        m_acc, sig, a_staged = {}, {}, {}

        def margins(g, b, w):
            m_acc[g, b, w] = late_bank([P, 2, 256])
            for e in range(2):
                for k in range(ND):
                    stationary = fp8(r_codes[k], r_scales[k], g * 512 + (2 * w + e) * P, P)
                    mx_pass(m_acc[g, b, w][:, e, :], stationary, fp8(h_codes[b], h_scales[b], 256 * k, 256), k == 0, k == ND - 1)

        def sigmoid(g, b, w):
            if w == 0:
                sig[g, b] = streamed([P, 2, 256, 2], F32, ("pc", "pr")[g], P_BUFS)
            nc.scalar.activation(out=sig[g, b][:, w, :, :], in_=m_acc[g, b, w][:].rearrange("p e n -> p n e"), func=ACT.Sigmoid)

        def times_beta(g, b):
            a_staged[g, b] = streamed([P, 256, 4], BF16, "half", HALF_BUFS)
            nc.vector.tensor_tensor(
                out=a_staged[g, b][:].rearrange("p n (w e) -> p n w e", w=2),
                in0=sig[g, b][:].rearrange("p w n e -> p n w e"),
                in1=beta_sb[:, g : g + 1, :].to_broadcast([P, 256, 4]).rearrange("p n (w e) -> p n w e", w=2),
                op=ALU.mult,
            )

        def quant_a(g, b):
            quantize(a_codes[g], a_scales[g], span(b, T), a_staged[g, b][:])

        o_acc, stores = {}, []

        def result(i, c0, n=512, tiles=1):
            o_acc[i, c0] = late_bank([P, tiles, n])
            for a in range(tiles):
                for g in range(NJ):
                    stationary = fp8(a_codes[g], a_scales[g], (i + a) * P, P)
                    mx_pass(o_acc[i, c0][:, a, :], stationary, fp8(b_codes[g], b_scales[g], c0, n), g == 0, g == NJ - 1)

        def store(i, c0, eng, n=512, tiles=1):
            free = (("diff", PIECE_BUFS), ("cst", PIECE_BUFS)) if len(stores) < 2 * PIECE_BUFS else (("pc", P_BUFS), ("pr", P_BUFS))
            tag, bufs = free[len(stores) % 2]
            stores.append(tag)
            x = streamed([P, tiles, n], F32, tag, bufs)
            move(eng, x[:], o_acc[i, c0][:])
            nc.sync.dma_start(out=out[i * P : (i + tiles) * P, c0 : c0 + n].rearrange("(a p) c -> p a c", a=tiles), in_=x[:])

        ALL_J, FIRST_V, LAST_V = range(NB), (0, 1), (2, 3)

        def ready(q, v, b, n=2):
            sub(q, v, n)
            turn_c(q, v, b, n)
            stage_c(q, v, n)

        def turn_tile(q):
            turn_c(q, 0, 0, NV)
            stage_c(q, 0, NV)

        def first_blocks(q):
            blocks(q, (0, 1, 2), FIRST_V)
            blocks(q, (0, 1, 2), LAST_V)

        make_identity(nc, ident[:])
        load_p(0, 0)
        load_scales()
        warm_table()
        load_ut(0)
        load_p(1, 0)
        load_ut(1)
        load_p(0, 1)
        load_p(1, 1)
        load_ut(2)
        load_part(2, p_chosen, None)
        load_part(2, p_rejected, 0)
        load_part(2, p_rejected, 1)
        load_ut(3)

        ready(0, 0, 0, 1)
        ready(0, 1, 1, 1)
        quant_c(0, 0, 1)
        sweep(0, 0)
        quant_c(0, 1, 1)
        ready(1, 0, 0, 1)
        ready(1, 1, 1, 1)
        sweep(0, 1)
        quant_c(1, 0, 1)
        sweep(1, 0, (0, 1, 2))
        for v in (2, 3):
            sub(0, v, 1)
        quant_c(1, 1, 1)
        for v in (2, 3):
            sub(1, v, 1)
        for q in range(2):
            for v in (2, 3):
                turn_pass(q, v, q)
            for v in (2, 3):
                stage_pass(q, v)
            if q == 0:
                sweep(1, 0, (3, 4, 5))
            sweep(1, 1, ((0, 1), (2, 3, 4, 5))[q])
        load_tile(3)
        load_r(0)
        load_p(4)
        load_h(0)
        for v in (2, 3):
            quant_c(0, v, 1)
        sweep(0, 2)
        quant_c(1, 2, 1)
        sub(2, 0)
        sub(2, 2)
        quant_c(1, 3, 1)
        sweep(1, 2)
        for v in (0, 2):
            turn_c(2, v, v // 2)
            stage_c(2, v, eng="sv"[v // 2])
        load_p(5)
        load_r(1)
        for j in ALL_J:
            pass_b(0, 3, j, False, False)
            pass_b(1, 3, j, False, True)
        for v in (0, 2):
            quant_c(2, v)
        for j in range(5):
            copy_b(0, j)

        blocks(2, (0, 1, 2))
        for v in (0, 2):
            sub(3, v)
        load_p(6)
        copy_b(0, 5, "v")
        for v in (0, 2):
            turn_c(3, v, v // 2)
        for v in (0, 2):
            stage_c(3, v)
        blocks(2, (3, 4, 5))
        weave_r(0, 0, "v", 0)
        weave_r(0, 1, "s", 0)
        for v in (0, 2):
            quant_c(3, v)
        weave_r(0, 0, "v", 1)

        first_blocks(3)
        blocks(3, (3, 4))
        weave_r(0, 1, "v", 1)
        sub(4, 0, NV)
        load_p(7)
        load_h(1)
        load_r(2)
        load_beta()
        for i in range(2):
            sort_h(i)
        for j in range(4):
            copy_b(1, j)
        turn_c(4, 0, 0, NV)
        stage_c(4, 0, NV, (0,), "v")
        stage_c(4, 0, NV, (2,))
        turn_h(0, (2, 3, 4))
        blocks(3, (5,))
        for a in range(2):
            quant_c(4, 0, NV, a)
            stage_h(a, 0)
        copy_b(1, 4)
        stage_h(2, 0)
        copy_b(1, 5)
        sub(5, 0, NV)

        blocks(4, (3, 0), FIRST_V)
        blocks(4, (3, 0), LAST_V)
        blocks(4, (1,))
        turn_tile(5)
        blocks(4, (2, 4, 5))
        weave_r(1, 1, "s", 0)
        quant_r(0)
        weave_r(1, 0)
        quant_c(5, 0, NV, 0)
        quant_c(5, 0, NV, 1)

        first_blocks(5)
        sub(6, 0, NV)
        copy_b(2, 0)
        turn_tile(6)
        blocks(5, (3, 4, 5))
        weave_b(0, 0, 1024)
        weave_r(1, 1, "v", 1)
        quant_h(2, 0)
        quant_c(6, 0, NV, 0)
        quant_c(6, 0, NV, 1)
        for j in range(1, NB):
            copy_b(2, j)
        sub(7, 0, NV)

        blocks(6, (0, 1), FIRST_V)
        blocks(6, (0, 1), LAST_V)
        blocks(6, (2,))
        turn_tile(7)
        turn_h(1, (6, 7, 0))
        blocks(6, (3,))
        quant_r(1)
        quant_h(0, 0)
        weave_r(2, 0, "v", 0)
        quant_c(7, 0, NV, 0)
        quant_c(7, 0, NV, 1)
        weave_r(2, 0, "v", 1)
        for k in range(ND):
            stage_h(k, 1)
        weave_b(0, 1024, 512, "s", 0)
        weave_r(2, 1, "v", 0)
        quant_r(2, 0)
        weave_r(2, 1, "v", 1)
        quant_h(0, 1)
        quant_r(2, 1)
        quant_h(2, 1)
        quant_b(0, 0, 1024)

        first_blocks(7)
        blocks(7, (3,))
        for j in range(3):
            copy_b(3, j)

        for b in range(2):
            for g in range(NJ):
                for w in range(2):
                    margins(g, b, w)
                    sigmoid(g, b, w)
                if (g, b) == (0, 0):
                    copy_b(3, 3)
                if (g, b) == (1, 0):
                    weave_b(0, 1024, 512, "s", 1)
        weave_b(1, 0, 512)
        times_beta(0, 0)
        quant_b(1, 0, 512)
        times_beta(1, 0)
        quant_a(0, 0)
        quant_a(1, 0)
        weave_b(1, 512, 512)
        times_beta(0, 1)
        quant_b(1, 512, 512)
        times_beta(1, 1)
        for g in range(NJ):
            quant_a(g, 1)

        for i in range(2):
            result(i, 0)
            store(i, 0, "s")
        for j in (4, 5):
            for q in (6, 7):
                blocks(q, (j,))
            copy_b(3, j)
        weave_b(1, 1024, 512)
        quant_b(0, 1024, 512)
        quant_b(1, 1024, 512)
        for i, c0 in ((0, 512), (1, 512), (2, 0), (3, 0), (2, 512)):
            result(i, c0)
            store(i, c0, "s")
        for i, c0, eng in ((3, 512, "v"), (0, 1024, "s"), (1, 1024, "v"), (2, 1024, "s"), (3, 1024, "v")):
            result(i, c0)
            store(i, c0, eng)
